import numpy as np, ml_dtypes
CORES = [24,25,26,27,28,29,30,31]
N = 8
import mx_ref
BF = ml_dtypes.bfloat16
def gentries(a):
    return np.ascontiguousarray(a.reshape(8, 16, -1).transpose(0, 2, 1)).reshape(8, -1)
def gtable(e):
    e = np.asarray(e); return np.ascontiguousarray(e.reshape(8, -1, 16).transpose(0, 2, 1)).reshape(128, -1).astype(np.int32)
def gcols(t, e):
    v = np.concatenate([t.reshape(8, 16, -1, 4), np.zeros((8, 16, 1, 4), BF)], axis=2)
    return np.ascontiguousarray(np.stack([v[g][:, e[g]] for g in range(8)])).reshape(128, -1)
def tile(rs):
    return np.stack(rs, axis=2).reshape(128, -1).astype(BF)
def cut(t, i, w=512):
    return t[:, w * i:w * i + w]
def pick(q, e):
    c = np.concatenate([q[0].reshape(128, -1, 4), np.zeros((128, 1, 4), np.uint8)], axis=1); s = np.concatenate([q[1], np.ones((16, 1), np.uint8)], axis=1)
    return (np.ascontiguousarray(c[:, e].reshape(128, -1)), np.ascontiguousarray(s[:, e]))
def join(*qs):
    return (np.concatenate([q[0] for q in qs], axis=1), np.concatenate([q[1] for q in qs], axis=1))
def put(q, e, v):
    c, s = q[0].reshape(128, -1, 4).copy(), q[1].copy(); c[:, e] = v[0].reshape(128, -1, 4); s[:, e] = v[1]
    return (c.reshape(128, -1), s)
def pk(c, s):
    return (np.ascontiguousarray(c), mx_ref.live(s))
def emit(q):
    return q[0], q[1]
def packed(v, rng):
    q = [mx_ref.quantize(np.ascontiguousarray(v[r])) for r in range(N)]
    return np.stack([a for a, b in q]), np.stack([mx_ref.plane(b, rng) for a, b in q])
def values_of_codes():
    e, c = np.zeros((128, 128, 4), np.float32), np.zeros((128, 2, 4), np.uint8)
    e[np.arange(128), np.arange(128), 0] = 1
    c[:127, :, 0] = np.arange(256).reshape(2, 128).T[:127]
    return mx_ref.matmul(mx_ref.quantize(e.reshape(128, 512).astype(BF)), (c.reshape(128, 8), np.full((16, 2), 127, np.uint8))).T.reshape(-1).astype(np.float64)
CODE_VALUE, SCALE_VALUE = values_of_codes(), 2.0 ** (np.arange(256) - 127.0)
def decode(q):
    return (CODE_VALUE[q[0]].reshape(16, 8, -1, 4) * SCALE_VALUE[q[1]][:, None, :, None] + 0.0).reshape(128, -1).astype(np.float32)
def f(rng, *shape):
    return mx_ref.flush((rng.standard_normal(shape, dtype=np.float32) * np.exp2(rng.integers(-2, 3, shape[:-1] + (1,)))).astype(BF))
def wide(rng, *shape, cols=0):
    v = rng.standard_normal(shape, dtype=np.float32) * np.exp2(rng.integers(-12, 13, shape)).astype(np.float32)
    if cols: v *= np.repeat(np.exp2(rng.integers(-cols, cols + 1, shape[:-2] + (1, shape[-1] // 4))) * (rng.random(shape[:-2] + (1, shape[-1] // 4)) > 0.0625), 4, axis=-1).astype(np.float32)
    return mx_ref.flush(v.astype(BF))
C, K, R = 256, 256, 3
def big(v, k):
    v = v.astype(np.float32) * np.float32(k)
    v[np.abs(v) < np.float32(2.0 ** -16)] = 0
    return v.astype(BF)
def numbers_of(rng):
    return {"x": big(f(rng, N, 128, 4 * C), 1), "u": np.array(f(rng, N, 128, 512)), "v": np.array(f(rng, N, 128, 512))}
def ends(a, b):
    return {"ea": np.stack([gtable(e) for e in a]), "eb": np.stack([gtable(e) for e in b])}
def weights(rng, w):
    c, p = packed(w, rng)
    return {"wc": c, "ws": p}
def still(rng):
    w = np.zeros((N, 128, 4, 128, 4), np.float32)
    i = np.arange(128)
    for b in range(4): w[:, i, b, i, b] = 32
    return weights(rng, w.reshape(N, 128, 2048).astype(BF))
def signs(rng):
    return np.stack([rng.permutation(8) % 2 * 2.0 - 1.0 for r in range(N)])
def setup_inputs(rng):
    d = numbers_of(rng)
    a, b = rng.integers(0, C, (2, N, 8, 2 * K))
    return {**d, **ends(a, b), **weights(rng, f(rng, N, 128, 2048))}
def setup_inputs_ties(rng):
    d = numbers_of(rng)
    x = d["x"].reshape(N, 8, 16, C, 4)
    a, b = np.zeros((2, N, 8, 2 * K), int)
    o = rng.permutation(N)
    for r in range(N):
        k = rng.permutation(C) % 3
        three = x[r][:, :8, :3].copy()
        three[:, :, 2] = 0
        x[r][:, :8] = three[:, :, np.zeros(C, int) if r == o[0] else k]
        e = np.argsort(k, kind="stable")
        at = np.searchsorted(k[e], np.arange(3))
        q = np.stack([rng.permutation(2 * K) % 9 for g in range(8)])
        a[r] = e[at[q // 3] + rng.integers(0, C // 3, q.shape)]
        b[r] = e[at[q % 3] + rng.integers(0, C // 3, q.shape)]
    x[o[1], :, :8] = 0
    u = d["u"].reshape(N, 8, 16, 128, 4)
    u[:, :, 8:, ::16] = 0
    w = np.array(f(rng, N, 128, 2048)).reshape(N, 8, 16, 4, 8, 16, 4)
    w[:, :, 8:, :, :, :8] = 0
    return {"x": x.reshape(N, 128, 4 * C), "u": u.reshape(N, 128, 512), "v": d["v"], **ends(a, b), **weights(rng, w.reshape(N, 128, 2048))}
def setup_inputs_near(rng):
    d = numbers_of(rng)
    x = d["x"].astype(np.float32).reshape(N, 8, 16, C, 4)
    x[:, :, :2] = 0
    x[:, :, 8:10] = 0
    x[:, :, 10:] = rng.integers(4, 8, (N, 8, 6, C, 4)) * rng.choice([-1.0, 1.0], (N, 8, 6, C, 4)) * 2.0 ** -20
    u = d["u"].reshape(N, 128, 128, 4)
    u[:, :, ::16] = 0
    a, b = np.zeros((2, N, 8, 2 * K), int)
    s = np.arange(2 * K) * (C // 2) // (2 * K)
    v = ((np.arange(C // 2)[:, None] >> np.arange(8)) & 1) * np.exp2(np.arange(8) - 23.0)
    sg = signs(rng)
    for r in range(N):
        k = rng.permutation(8) % 4
        up, far = k % 2, k // 2
        for g in range(8):
            e = rng.permutation(C)
            p, z = e[:C // 2], e[C // 2:]
            x[r, g, 0, p, 0] = 1
            x[r, g, 1, p, 0] = 2.0 ** -9
            x[r, g, 8, p] = v[:, :4]
            x[r, g, 9, p] = v[:, 4:]
            if far[g]: x[r, g, 0, p[C // 2 - 1], 0] = 2.0 ** 30
            h = 16 * g
            u[r, h:h + 2, h, 0] = sg[r, g]
            u[r, h + 8:h + 10, h] = sg[r, g]
            m = p[s if up[g] else s[rng.permutation(2 * K)]]
            q = z[rng.integers(0, C // 2, 2 * K)]
            first = rng.random(2 * K) < 0.5
            a[r, g] = np.where(first, m, q)
            b[r, g] = np.where(first, q, m)
    return {"x": x.reshape(N, 128, 4 * C).astype(BF), "u": u.reshape(N, 128, 512), "v": d["v"], **ends(a, b), **still(rng)}
def setup_inputs_huge(rng):
    d = numbers_of(rng)
    far = (rng.permutation(N) < N // 2)[:, None, None, None]
    c = np.stack([rng.permutation(C) % 2 * 2.0 - 1.0 for r in range(N)])
    x = np.where(far, 2.0 ** 30, 2.0 ** -15) * (0.6 + 0.4 * rng.random((N, 128, C, 4))) * c[:, None, :, None]
    u = d["u"].reshape(N, 128, 128, 4)
    s = np.where(far, 2.0 ** 30, 2.0 ** -29) * (1 - 0.25 * rng.random((N, 128, 8, 4))) * signs(rng)[:, None, :, None]
    two = np.isin(np.arange(128)[:, None] - 16 * np.arange(8), (0, 1))[None, :, :, None]
    s = np.where(far | two, s, 0.0)
    u[:, :, ::16] = s.astype(np.float32).astype(BF)
    a, b = np.zeros((2, N, 8, 2 * K), int)
    for r in range(N):
        p = np.flatnonzero(c[r] > 0)[rng.integers(0, C // 2, (8, 2 * K))]
        q = np.flatnonzero(c[r] < 0)[rng.integers(0, C // 2, (8, 2 * K))]
        first = rng.random((8, 2 * K)) < 0.5
        a[r] = np.where(first, p, q)
        b[r] = np.where(first, q, p)
    return {"x": x.astype(np.float32).reshape(N, 128, 4 * C).astype(BF), "u": u.reshape(N, 128, 512), "v": d["v"], **ends(a, b), **still(rng)}
def setup_inputs_knots(rng):
    d = numbers_of(rng)
    x = d["x"].reshape(N, 128, C, 4)
    x[:, :, 0] = 0
    x[:, :, 1] = np.abs(x[:, :, 1].astype(np.float32)).astype(BF)
    u = d["u"].reshape(N, 128, 128, 4)
    u[:, :, ::16] = np.abs(u[:, :, ::16].astype(np.float32)).astype(BF)
    a, b = rng.integers(0, C, (2, N, 8, 2 * K))
    for r in range(N):
        g = rng.permutation(8)
        a[r, g[0]] = 0
        b[r, g[0]] = 1
        b[r, g[1]] = a[r, g[1]]
        for h, lo in ((g[2], 0), (g[3], K)):
            a[r, h] = 0
            b[r, h] = 1
            b[r, h, lo:lo + K] = 0
        a[r, g[4]] = C - 1
        a[r, g[5]] = np.arange(2 * K) % C
        b[r, g[5]] = (np.arange(2 * K) + 1) % C
    return {"x": x.reshape(N, 128, 4 * C), "u": u.reshape(N, 128, 512), "v": d["v"], **ends(a, b), **weights(rng, f(rng, N, 128, 2048))}
def setup_inputs_spread(rng):
    d = setup_inputs(rng)
    d["x"] = big(wide(rng, N, 128, 4 * C, cols=6), 1)
    return d
def check_inputs(d):
    b = []
    for k in ("x", "u", "v"):
        a = np.abs(d[k].astype(np.float32))
        if not (np.isfinite(a).all() and ((a == 0) | (a >= 2.0 ** -30) & (a <= 2.0 ** 30)).all()): b.append("a value of " + k)
    for k in ("ea", "eb"):
        if not ((d[k] >= 0) & (d[k] < C)).all(): b.append("an entry of " + k)
    a = np.abs(np.stack([decode(pk(d["wc"][r], d["ws"][r])) for r in range(N)]))
    if not ((a == 0) | (a >= 2.0 ** -30) & (a <= 2.0 ** 30)).all(): b.append("a number that wc and ws hold")
    return b
def reference(x, u, v, ea, eb, wc, ws):
    qu = [mx_ref.quantize(u[r]) for r in range(N)]
    lay = [pk(wc[r], ws[r]) for r in range(N)]
    a, b = [gentries(ea[r]) for r in range(N)], [gentries(eb[r]) for r in range(N)]
    new = [mx_ref.quantize(x[r]) for r in range(N)]
    held = [q for q in new]
    nums = [np.zeros((128, 0), BF) for r in range(N)]
    s = [np.zeros((8, 0), np.float32) for r in range(N)]
    for t in range(1, R + 1):
        got = decode(join(*new)).astype(BF)
        n = C + (t - 1) * K
        for r in range(N):
            nums[r] = np.concatenate([nums[r], cut(got, r, 4 * C if t == 1 else 4 * K)], axis=1)
            s[r] = np.concatenate([s[r], mx_ref.matmul(qu[r], new[r])[::16]], axis=1)
        for r in range(N):
            z = np.abs(np.take_along_axis(s[r], a[r], axis=1) - np.take_along_axis(s[r], b[r], axis=1))
            e = np.sort(np.argsort(-z, axis=1, kind="stable")[:, :K], axis=1)
            p, q = np.take_along_axis(a[r], e, axis=1), np.take_along_axis(b[r], e, axis=1)
            mid = (gcols(nums[r], p).astype(np.float32) + gcols(nums[r], q).astype(np.float32)) * np.float32(0.5)
            m = mx_ref.quantize(np.ascontiguousarray(mid.astype(BF)))
            w = lay[(r + t) % N]
            new[r] = mx_ref.quantize(tile([mx_ref.matmul(pick(w, np.arange(128 * i, 128 * i + 128)), m) * np.float32(0.03125) for i in range(4)]))
            held[r] = join(held[r], new[r])
            at = np.tile(n + np.arange(K), (8, 1))
            a[r], b[r] = np.stack([p, at], axis=2).reshape(8, -1), np.stack([at, q], axis=2).reshape(8, -1)
    y, el = np.zeros((N, 128, C + R * K), np.float32), np.zeros((N, 8, 4 * K), np.float32)
    oc, osc = np.zeros((N, 128, 4 * (C + R * K)), np.uint8), np.zeros((N, 16, C + R * K), np.uint8)
    for r in range(N):
        y[r] = mx_ref.matmul(mx_ref.quantize(v[r]), held[r])
        el[r] = np.concatenate([a[r], b[r]], axis=1)
        oc[r], osc[r] = emit(held[r])
    return {"y": y, "el": el, "oc": oc, "osc": osc}

@@ -1,0 +1,562 @@
+from concourse.mybir import dt, AluOpType, AxisListType, ActivationFunctionType
+
+N, C, K, R = 8, 256, 256, 3
+X4, U8 = "float8_e4m3fn_x4", "uint8"
+F32, BF, I32, U16 = "float32", "bfloat16", "int32", "uint16"
+NV = 192
+SHARE1 = [0, 0, 0, 0, 0, 0, 176, 128]
+SHARE = [0, 176, 0, 176, 176, 176, 176, 128]
+
+
+def _sb(n, t):
+    return ("sbuf", [128, n], t)
+
+
+SCRATCH = {
+    "xt": _sb(1024, BF), "ut": _sb(512, BF), "vt": _sb(512, BF), "eai": _sb(32, I32), "ebi": _sb(32, I32),
+    "eau": _sb(32, U16), "ebu": _sb(32, U16),
+    "tc": _sb(1024, X4), "tsc": _sb(1024, U8), "uc": _sb(128, X4), "usc": _sb(128, U8),
+    "upc": _sb(128, X4), "ups": _sb(128, U8), "vc": _sb(128, X4), "vsc": _sb(128, U8),
+    "ec": _sb(512, X4), "esc": _sb(512, U8), "mc": _sb(256, X4), "msc": _sb(256, U8),
+    "wo": _sb(512, X4), "wos": _sb(512, U8),
+    "wl1": _sb(512, X4), "wls1": _sb(512, U8), "wl2": _sb(512, X4), "wls2": _sb(512, U8),
+    "wl3": _sb(512, X4), "wls3": _sb(512, U8),
+    "ones": _sb(512, BF), "et": _sb(2048, BF), "mt": _sb(1024, BF), "ft": _sb(1024, BF),
+    "z1": _sb(1024, BF), "z2": _sb(3072, BF), "z3": _sb(3072, BF),
+    "ptab": _sb(256, F32), "pa": _sb(512, F32), "dd": _sb(512, F32), "ss": _sb(512, F32), "sp": _sb(512, F32),
+    "junk": _sb(512, BF), "trs": _sb(512, F32), "sx": _sb(32, F32), "sd": _sb(32, F32),
+    "zp2": _sb(768, F32), "zp3": _sb(768, F32), "zi2": _sb(768, F32), "zi3": _sb(768, F32), "elb": _sb(1024, F32),
+    "ysb": _sb(1024, F32), "g1": _sb(512, F32), "g2": _sb(512, F32), "vm": _sb(512, F32), "phm": _sb(512, F32),
+    "em": _sb(512, F32), "ic": _sb(256, F32), "rr": _sb(512, F32), "ex": _sb(256, F32), "ex2": _sb(256, F32),
+    "c4": _sb(256, F32), "c16": _sb(256, F32), "k4": _sb(256, F32), "k16": _sb(256, F32),
+    "pi": _sb(8, I32), "pj": _sb(8, I32), "pf": _sb(8, F32), "ui": _sb(8, I32), "uo": _sb(8, U16),
+    "ch": _sb(32, F32), "same": _sb(32, F32), "zc": _sb(32, F32), "zc2": _sb(32, F32), "zs": _sb(32, F32),
+    "mk": _sb(64, F32), "d1": _sb(33 * 8, F32), "js": _sb(8, F32), "tmp": _sb(64, F32), "cs": _sb(16, F32),
+    "xx": _sb(64, F32), "tr": _sb(40, F32), "th": _sb(33 * 8, F32), "cnt": _sb(16, F32),
+    "sm": _sb(8, F32), "fl": _sb(130, F32), "keep": _sb(66, F32), "ll": _sb(97, F32), "qq": _sb(97, F32),
+    "zz": _sb(33, F32), "yy": _sb(32, F32), "e1": _sb(33, F32),
+    "prm": _sb(32, U16), "so": _sb(32, U16), "wi": _sb(64, I32), "wa": _sb(64, I32), "wb": _sb(64, I32),
+    "oa": _sb(64 * 3, U16), "ob": _sb(64 * 3, U16), "la": _sb(16 * 3, U16), "lb": _sb(16 * 3, U16),
+    "si": _sb(16, I32), "sa": _sb(16, I32), "sbi": _sb(16, I32), "sf": _sb(16, F32),
+    "vf": _sb(NV + 32, BF), "vf8": _sb(NV + 32, BF), "vo": _sb(NV + 32, BF),
+    "ps": ("psum", [128, 4096], F32),
+}
+POOL = {"v": 56, "s": 36, "t": 20, "g": 14}
+LOADS = ["ldu", "lda", "ldb", "ldx0", "ldx1", "ldw", "ldws", "ldv"]
+SEMAPHORES = ([q + str(i) for q in POOL for i in range(POOL[q])] + LOADS
+              + ["arr1", "arr2", "arr3", "sent", "outy", "outs"])
+BIG = 2.0 ** 30
+A = AluOpType
+ACT = ActivationFunctionType
+
+
+def rank_program(g, core, T, topo):
+    rank = T.rank_of(core)
+    if rank is None:
+        return
+    queue = {"v": g.vector, "s": g.scalar, "t": g.tensor, "g": g, "y": g.sync}
+    ops = []
+
+    def ap(a):
+        if not isinstance(a, tuple):
+            return a
+        if len(a) == 2:
+            return ap(a[0]).indirect(ap(a[1]))
+        return T[a[0]][:, a[1]:a[2]:a[3]] if a[3] != 1 else T[a[0]][:, a[1]:a[2]]
+
+    def V(name, a=0, b=None, step=1):
+        return (name, a, SCRATCH[name][1][1] if b is None else b, step)
+
+    def col(name, a):
+        return V(name, a, a + 1)
+
+    def flat(items):
+        out = []
+        for a in items:
+            if isinstance(a, tuple):
+                out += list(a) if len(a) == 2 else [a]
+        return out
+
+    def add(q, call, reads, writes, sem=None, extra=()):
+        ops.append((q, call, flat(reads), flat(writes), sem, extra))
+
+    def copy(out, in_):
+        if len(out) == 2:
+            add("v", lambda: g.vector.tensor_copy(ap(out), ap(in_)), [in_, out[1]], [out[0]])
+        else:
+            add("v", lambda: g.vector.tensor_copy(ap(out), ap(in_)), [in_], [out])
+
+    def tt(out, a, b, op):
+        add("v", lambda: g.vector.tensor_tensor(ap(out), ap(a), ap(b), op), [a, b], [out])
+
+    def ts(out, a, s1, op0, s2=None, op1=None):
+        if op1 is None:
+            add("v", lambda: g.vector.tensor_scalar(ap(out), ap(a), ap(s1), None, op0), [a, s1], [out])
+        else:
+            add("v", lambda: g.vector.tensor_scalar(ap(out), ap(a), ap(s1), ap(s2), op0, op1), [a, s1, s2], [out])
+
+    def fill(out, c):
+        add("v", lambda: g.vector.memset(ap(out), c), [], [out])
+
+    def scan(out, d0, d1, init, op0, op1):
+        add("v", lambda: g.vector.tensor_tensor_scan(ap(out), ap(d0), ap(d1), ap(init), op0, op1), [d0, d1, init], [out])
+
+    def turn(out, in_):
+        add("v", lambda: g.vector.transpose(ap(out), ap(in_)), [in_], [out])
+
+    def act(out, in_, func, scale=1.0):
+        add("s", lambda: g.scalar.activation(ap(out), ap(in_), func, scale=scale), [in_], [out])
+
+    def lin(out, in_, scale, bias, func):
+        add("s", lambda: g.scalar.activation(ap(out), ap(in_), func, bias=ap(bias), scale=scale), [in_, bias], [out])
+
+    def count(cnt, in_, thr):
+        junk = V("junk", in_[1], in_[2])
+        add("s", lambda: g.scalar.activation(ap(junk), ap(in_), ACT.Sign, bias=ap(thr), scale=-1.0, accum_out=ap(cnt)),
+            [in_, thr], [junk, cnt])
+
+    def quant(codes, scales, a, b, in_):
+        add("v", lambda: g.vector.quantize_mx(T[codes][:, a:b], T[scales][:, a:b], ap(in_)), [in_],
+            [V(codes, a, b), V(scales, a, b)])
+
+    def mm(bank, lc, ls, a, rc, rs, c, d, extra=()):
+        out = V("ps", 512 * bank, 512 * bank + d - c)
+        add("t", lambda: g.tensor.matmul_mx(ap(out), T[lc][:, a:a + 128], T[ls][:, a:a + 128], T[rc][:, c:d], T[rs][:, c:d],
+                                            True, True),
+            [V(lc, a, a + 128), V(ls, a, a + 128), V(rc, c, d), V(rs, c, d)], [out], None, extra)
+
+    def bank(b, n=256):
+        return V("ps", 512 * b, 512 * b + n)
+
+    def iota(out, pattern, base=0, mult=0):
+        if SCRATCH[out[0]][2] == I32:
+            add("g", lambda: g.iota(ap(out), pattern, base, mult), [], [out])
+        else:
+            add("g", lambda: g.iota(ap(out), pattern, base, mult, allow_small_or_imprecise_dtypes=True), [], [out])
+
+    def dma(q, out, in_, reads, writes, sem):
+        add(q, lambda: queue[q].dma_start(out(), in_()), reads, writes, sem)
+
+    outs = {"y": 0, "s": 0}
+
+    def store(q, out, in_, reads):
+        outs[q] += 16
+        dma(q, out, in_, reads, [], "out" + q)
+
+    def store_codes(q, a, b):
+        store(q, lambda: T.oc[:, 4 * a:4 * b], lambda: T.tc[:, a:b].bitcast(dt.uint8), [V("tc", a, b)])
+
+    def store_scales(qs, a, b):
+        for k in range(4):
+            store(qs[k], lambda k=k: T.osc[4 * k:4 * k + 4, a:b], lambda k=k: T.tsc[32 * k:32 * k + 4, a:b], [V("tsc", a, b)])
+
+    def store_y(q, a, b):
+        store(q, lambda: T.y[:, a:b], lambda: T.ysb[:, a:b], [V("ysb", a, b)])
+
+    J, H, B, Q4 = col("pf", 0), col("pf", 1), col("pf", 2), col("pf", 3)
+    THR1, B3, KO, J32 = col("cs", 0), col("cs", 1), col("cs", 2), col("cs", 3)
+
+    dma("y", lambda: T.ut[:], lambda: T.u[:], [], [V("ut")], "ldu")
+    dma("s", lambda: T.xt[:, 0:512], lambda: T.x[:, 0:512], [], [V("xt", 0, 512)], "ldx0")
+    dma("y", lambda: T.xt[:, 512:1024], lambda: T.x[:, 512:1024], [], [V("xt", 512, 1024)], "ldx1")
+    dma("s", lambda: T.ebi[:], lambda: T.eb[:], [], [V("ebi")], "ldb")
+    dma("y", lambda: T.eai[:], lambda: T.ea[:], [], [V("eai")], "lda")
+    dma("y", lambda: T.wo[:].bitcast(dt.uint8), lambda: T.wc[:], [V("xt"), V("ut")], [V("wo")], "ldw")
+    dma("y", lambda: T.wos[:], lambda: T.ws[:], [], [V("wos")], "ldws")
+    dma("y", lambda: T.vt[:], lambda: T.v[:], [], [V("vt")], "ldv")
+
+    iota(col("pi", 0), [[0, 1]], 0, 1)
+    iota(V("ui"), [[16, 8]])
+    iota(V("ch"), [[1, 2], [0, 16]])
+    iota(V("c16"), [[0, 16], [1, 16]])
+    iota(V("ic"), [[1, 256]])
+    iota(V("c4"), [[0, 64], [1, 4]])
+    fill(V("ones"), 1.0)
+    p = col("pi", 0)
+    ts(col("pj", 0), p, 15, A.bitwise_and)
+    ts(col("pj", 1), p, 4, A.arith_shift_right, 1, A.bitwise_and)
+    ts(col("pj", 2), p, 3, A.bitwise_and)
+    ts(col("pj", 3), p, 2, A.arith_shift_right, 3, A.bitwise_and)
+    copy(V("uo"), V("ui"))
+    copy(V("pf", 0, 4), V("pj", 0, 4))
+    fill(col("cs", 5), BIG)
+    fill(V("d1", 0, 66), 1.0)
+    fill(V("d1", 66), 0.0)
+    fill(V("tr"), 0.0)
+    fill(V("keep"), 1.0)
+    fill(V("vf", NV), 0.0)
+    fill(V("vf8", NV), 0.0)
+    ts(col("sm", 7), Q4, -1.0, A.mult)
+    ts(col("cs", 4), J, -1.0, A.mult)
+    ts(J32, J, 32.0, A.mult)
+    ts(V("same"), V("ch"), H, A.is_equal)
+    ts(col("sm", 0), J, 0.0, A.is_equal, 2048.0, A.mult)
+    ts(V("tmp", 0, 16), V("c16", 0, 16), J, A.is_lt, 2047.0, A.mult)
+    ts(V("tmp", 16, 32), V("c16", 0, 16), J, A.is_lt, 1.0, A.add)
+    fill(col("keep", 33), 0.0)
+    ts(V("tmp", 0, 16), V("tmp", 0, 16), 1.0, A.add)
+    add("v", lambda: g.vector.tensor_reduce(ap(col("d1", 32)), ap(V("tmp", 16, 32)), AxisListType.X, A.mult),
+        [V("tmp", 16, 32)], [col("d1", 32)])
+    ts(col("sm", 1), J, 0.0, A.is_gt)
+    scan(V("tmp", 32, 48), V("tmp", 0, 16), V("d1", 66, 82), 2.0 ** -104, A.mult, A.add)
+    ts(col("sm", 2), J, 7.0, A.min, 0.5, A.add)
+    fill(col("js", 5), 2.0 ** -24)
+    ts(THR1, col("tmp", 47), col("sm", 1), A.mult)
+    ts(V("zc2"), V("same"), -1.0, A.add, 4096.0, A.mult)
+    ts(col("d1", 65), J, 1.0 / 16, A.mult, 1.0, A.add)
+    ts(V("zc"), V("zc2"), col("sm", 0), A.add)
+    copy(V("ebu"), V("ebi"))
+    for k in range(4):
+        act(col("js", k), J, ACT.Copy, 2.0 ** (-8 - 4 * k))
+    act(B3, B, ACT.Copy, 3.0)
+    lin(V("g2", 0, 256), V("c16"), 1.0, col("cs", 4), ACT.Abs)
+    lin(V("e1"), V("ic", 0, 33), 1.0, J32, ACT.Identity)
+    lin(V("k16"), V("g2", 0, 256), -BIG, col("cs", 5), ACT.Relu)
+    lin(V("ex"), V("c4"), 1.0, col("sm", 7), ACT.Abs)
+    act(col("js", 4), col("sm", 2), ACT.Copy, 2.0 ** -23)
+
+    small = [
+        lambda: ts(col("vf", NV + 16), H, 8192.0, A.mult, -4096.0, A.add),
+        lambda: ts(col("fl", 64), J, -16.0, A.mult, -0.5, A.add),
+        lambda: ts(V("tmp", 0, 32), V("c16", 0, 32), J, A.is_gt),
+        lambda: ts(col("sm", 3), J, 8.0, A.mult, 8.5, A.add),
+        lambda: tt(V("tmp", 32, 64), V("tmp", 0, 32), V("same"), A.mult),
+        lambda: ts(col("cs", 6), J, 16.0, A.mult, 16.5 - 8192.0 - 65536.0, A.add),
+        lambda: ts(KO, col("sm", 3), J, A.mult, -1672.0, A.add),
+        lambda: tt(V("mk", 0, 32), V("same"), V("tmp", 32, 64), A.subtract),
+        lambda: ts(V("mk", 32, 64), V("tmp", 32, 64), 65536.0, A.mult, col("cs", 6), A.add),
+        lambda: ts(col("cs", 7), KO, -1.0, A.mult, 256.0, A.add),
+        lambda: fill(V("ll", 0, 31), 8192.0),
+    ]
+
+    def late_constants():
+        lin(V("k4"), V("ex"), -BIG, col("cs", 5), ACT.Relu)
+        act(col("fl", 97), col("fl", 64), ACT.Copy)
+        act(col("vf8", NV + 16), col("vf", NV + 16), ACT.Copy)
+        act(col("vf", NV), col("zc", 0), ACT.Copy)
+        act(col("vf8", NV), col("zc2", 0), ACT.Copy)
+
+    iota(V("em"), [[256, 32], [8192, 16]], -65536)
+    for b in range(4):
+        o = V("et", 512 * b, 512 * b + 512)
+        add("g", lambda o=o, b=b: g.affine_select(ap(o), T.ones[:], [[-1, 512]], A.is_equal, 0.0, b, 4), [V("ones")], [o])
+
+    def send(t):
+        dst = T.cores[(rank - t) % N]
+        rid, pid = topo.addr(dst)[:2]
+        m = topo.mask(core, dst)
+        arr = T.sem["arr%d" % t]
+        add("g", lambda: g.remote_dma(T["wl%d" % t][:].bitcast(dt.uint8), T.wo[:].bitcast(dt.uint8), arr, T.sem.sent, pid, rid, m),
+            [V("wo")], [], "remote")
+        add("g", lambda: g.remote_dma(T["wls%d" % t][:], T.wos[:], arr, T.sem.sent, pid, rid, m), [V("wos")], [], "remote")
+        return 2 * len(topo.engines(core, dst))
+
+    sent = send(1)
+    iota(V("phm"), [[12, 16], [1, 2], [192, 16]])
+    iota(V("zi2", 1, 768, 3), [[1, 256]], C)
+    sent += send(2)
+    iota(V("zi3", 1, 768, 3), [[1, 256]], C + K)
+    iota(V("elb", 1, 512, 2), [[1, 256]], C + 2 * K)
+    iota(V("elb", 512, 1024, 2), [[1, 256]], C + 2 * K)
+    sent += send(3)
+
+    act(V("g1", 0, 256), (V("ic"), V("ebu", 0, 16)), ACT.Copy, 2.0 ** -8)
+    quant("uc", "usc", 0, 128, V("ut"))
+    add("v", lambda: g.vector.tensor_copy(T.upc[:].bitcast(dt.uint32), T.uc[:].bitcast(dt.uint32).indirect(T.uo[:])),
+        [V("uc"), V("uo")], [V("upc")])
+    add("s", lambda: g.scalar.activation(T.ups[:], T.usc[:].indirect(T.uo[:]), ACT.Copy), [V("usc"), V("uo")], [V("ups")])
+    act(V("g1", 256, 512), (V("ic"), V("ebu", 16, 32)), ACT.Copy, 2.0 ** -8)
+    quant("tc", "tsc", 0, 128, V("xt", 0, 512))
+    quant("tc", "tsc", 128, 256, V("xt", 512, 1024))
+    copy(V("eau"), V("eai"))
+    mm(0, "upc", "ups", 0, "tc", "tsc", 0, 256)
+    copy(V("prm"), V("e1", 0, 32))
+    copy(V("ptab"), bank(0))
+    store_codes("y", 0, 256)
+    store_scales("yyyy", 0, 256)
+    for h in range(2):
+        act(V("pa", 256 * h, 256 * h + 256), (V("ptab"), V("eau", 16 * h, 16 * h + 16)), ACT.Copy)
+    tt(V("g2", 0, 256), (V("ic"), V("eau", 0, 16)), V("g1", 0, 256), A.add)
+    for h in range(2):
+        tt(V("dd", 256 * h, 256 * h + 256), (V("ptab"), V("ebu", 16 * h, 16 * h + 16)), V("pa", 256 * h, 256 * h + 256), A.subtract)
+    act(V("ss", 0, 256), V("dd", 0, 256), ACT.Abs)
+    count(col("cnt", 8), V("ss", 0, 256), THR1)
+    act(V("ss", 256, 512), V("dd", 256, 512), ACT.Abs)
+    tt(V("g2", 256, 512), (V("ic"), V("eau", 16, 32)), V("g1", 256, 512), A.add)
+
+    DB = [1, 2, 3, 5]
+    for t in range(1, R + 1):
+        n = C + (t - 1) * K
+        zw = V("z%d" % t)
+        zn = "z3" if t == 2 else "z2"
+        oa, ob = 64 * (t - 1), 64 * (t - 1)
+        lo = 16 * (t - 1)
+
+        def th(k, c):
+            return col("th", 33 * (k - 1) + c)
+
+        LO2 = th(2, 31)
+
+        def shared(k):
+            return (SHARE if t > 1 else SHARE1)[k - 1]
+
+        def slot(k):
+            if k == 7:
+                ts(col("sm", 5), th(7, 32), col("d1", 263), A.add, LO2, A.add)
+                ts(col("sm", 6), th(7, 31), LO2, A.add)
+            if shared(k + 1):
+                nv = shared(k + 1)
+                f, thr = ("vf8", col("sm", 5)) if k == 7 else ("vf", th(k, 32))
+                ts(V(f, NV - nv, NV), V("ss", 512 - nv, 512), thr, A.is_lt, -2.0, A.mult)
+                if k == 6:
+                    ts(col("sm", 4), th(6, 32), LO2, A.subtract)
+                scan(V("vo", 0, nv + 32), V("ones", 0, nv + 32), V(f, NV - nv), float(nv), A.mult, A.add)
+            if k == 1 and t == 1:
+                turn(V("trs"), V("ss"))
+            if k == 2:
+                ts(V("d1", 98, 264, 33), V("js", 0, 6), LO2, A.mult)
+                ts(V("sp", 0, 512 - shared(8)), V("ss", 0, 512 - shared(8)), LO2, A.subtract)
+            if k == 3 and t == 1:
+                quant("ec", "esc", 0, 256, V("et", 0, 1024))
+                quant("ec", "esc", 256, 512, V("et", 1024, 2048))
+                quant("vc", "vsc", 0, 128, V("vt"))
+                for b in range(4):
+                    mm(DB[b], "ec", "esc", 128 * b, "tc", "tsc", 0, 256)
+                mm(6, "vc", "vsc", 0, "tc", "tsc", 0, 256)
+            if k == 4 and t == 1:
+                late_constants()
+                tt(V("vm", 0, 256), (V("g2"), V("prm", 0, 16)), V("em", 0, 256), A.add)
+            if k == 5 and t == 1:
+                tt(V("vm", 256, 512), (V("g2"), V("prm", 16, 32)), V("em", 256, 512), A.add)
+
+        gaps = list(small) if t == 1 else []
+
+        def gap():
+            if gaps:
+                gaps.pop(0)()
+
+        ts(V("zs"), V("zc2"), col("cnt", 8), A.subtract)
+        for k in range(1, 9):
+            thr = THR1 if k == 1 else th(k - 1, 32)
+            cnt = col("cnt", k - 1)
+            nv = shared(k)
+            count(cnt, V("ss", 256, 512) if k == 1 else V("sp" if k == 8 else "ss", 0, 512 - nv), thr)
+            if k > 1:
+                slot(k - 1)
+            elif t > 1:
+                turn(V("trs", 0, 256), V("ss", 0, 256))
+                turn(V("trs", 256, 512), V("ss", 256, 512))
+            val = col("sm", 4) if k == 7 else col("sm", 5) if k == 8 else thr
+            ts(V("xx", 0, 32), V("vo", nv, nv + 32) if nv else V("zs" if k == 1 else "zc"), cnt, A.is_ge, val, A.mult)
+            gap()
+            turn(V("tr", 0, 32), V("xx", 0, 32))
+            gap()
+            if k == 1:
+                gaps.extend([lambda: copy(V("sx", 0, 16), V("trs", 0, 512, 32)), lambda: copy(V("sx", 16, 32), V("trs", 16, 512, 32)),
+                             lambda: turn(V("sd"), V("sx"))])
+            if k < 8:
+                scan(V("th", 33 * (k - 1), 33 * k), V("tr", 0, 33), V("d1", 33 * (k - 1), 33 * k), 0.0, A.max,
+                     A.mult if k < 3 else A.add)
+            else:
+                scan(V("th", 231, 263), V("tr", 0, 32), V("d1", 231, 263), col("sm", 6), A.max, A.add)
+        TT = th(8, 31)
+
+        if t > 1:
+            zo = V("z%d" % (t - 1))
+            for h in range(2):
+                act(V("zp%d" % t, 384 * h + 1, 384 * h + 384, 3), bank(4 * h, 128), ACT.Copy)
+            for c in range(2):
+                act(V(zw[0], 1536 * c + 2, 1536 * c + 1536, 3), (zo, V("ob", ob - 64 + 32 * c, ob - 32 + 32 * c)), ACT.Copy)
+        for b in range(4):
+            act(V("z1", b, 1024, 4) if t == 1 else V(zw[0], 3 * b + 1, 3072, 12), bank(DB[b]), ACT.Copy, 0.5)
+        if t > 1:
+            iw = V("ic") if t == 2 else V("zi2")
+            act(V("zi%d" % t, 0, 768, 3), (iw, V("la", lo - 16, lo)), ACT.Copy)
+            act(V("zi%d" % t, 2, 768, 3), (iw, V("lb", lo - 16, lo)), ACT.Copy)
+        act(V("ysb", n - 256, n), bank(6), ACT.Copy)
+        store_y("y", n - 256, n)
+
+        ts(V("fl", 65, 97), V("sd"), TT, A.is_ge, -0.5, A.add)
+        ts(V("fl", 98, 130), V("sd"), TT, A.is_gt, -0.5, A.add)
+        scan(V("ll", 31, 97), V("keep"), V("fl", 64, 130), 8192.0, A.mult, A.add)
+        ts(V("xx", 0, 32), V("mk", 0, 32), col("ll", 96), A.mult)
+        ts(V("xx", 32, 64), V("mk", 32, 64), col("ll", 63), A.add, 0.0, A.max)
+        turn(V("fl", 0, 64), V("xx"))
+        scan(V("qq"), V("fl", 0, 97), V("ll"), col("cs", 7), A.add, A.min)
+        tt(V("zz"), V("qq", 64, 97), V("e1"), A.mult)
+        tt(V("yy"), V("zz", 1, 33), V("zz", 0, 32), A.subtract)
+        ts(V("so"), V("yy"), col("qq", 31), A.subtract, 256.0, A.add)
+        copy((V("rr"), V("so")), V("vm" if t == 1 else "phm"))
+        scan(V("ex"), V("k4"), V("rr", 256, 512), 0.0, A.add, A.min)
+        exv, ex2v = V("ex", 3, 256, 4), V("ex2", 15, 256, 16)
+        if t == 1:
+            ts(V("wi"), exv, 256.0, A.mult)
+            ts(V("wa"), V("wi"), 8, A.arith_shift_right, 255, A.bitwise_and)
+            ts(V("wb"), V("wi"), 255, A.bitwise_and)
+            ts(V("oa", 0, 64), V("wa"), 4.0, A.mult, B, A.add)
+            ts(V("ob", 0, 64), V("wb"), 4.0, A.mult, B, A.add)
+        else:
+            ts(V("oa", oa, oa + 64), exv, B3, A.add)
+            ts(V("ob", ob, ob + 64), exv, B3, A.add, 1.0, A.add)
+
+        for c in range(4):
+            act(V(zn, 768 * c, 768 * c + 768, 3), (zw, V("oa", oa + 16 * c, oa + 16 * c + 16)), ACT.Copy)
+        scan(V("ex2"), V("k16"), V("rr", 256, 512), 0.0, A.add, A.min)
+        if t == 1:
+            ts(V("si"), ex2v, 256.0, A.mult)
+        else:
+            ts(V("sf"), ex2v, 0.25, A.mult, 0.4, A.add)
+
+        def lists_a():
+            if t == 1:
+                ts(V("sa"), V("si"), 8, A.arith_shift_right, 255, A.bitwise_and)
+                ts(V("sbi"), V("si"), 255, A.bitwise_and)
+            else:
+                copy(V("sa"), V("sf"))
+
+        def lists_b():
+            copy(V("la", lo, lo + 16), V("sa"))
+            if t == 1:
+                copy(V("lb", lo, lo + 16), V("sbi"))
+            else:
+                ts(V("lb", lo, lo + 16), V("sa"), 1.0, A.add)
+
+        def mid(c):
+            tt(V("mt", 256 * c, 256 * c + 256), (zw, V("ob", ob + 16 * c, ob + 16 * c + 16)), V(zn, 768 * c, 768 * c + 768, 3), A.add)
+
+        def layer(h):
+            quant("mc", "msc", 128 * h, 128 * h + 128, V("mt", 512 * h, 512 * h + 512))
+            for b in range(4):
+                src = T.cores[(rank + t) % N]
+                extra = (("arr%d" % t, 2 * len(topo.engines(src, core))),) if h == 0 and b == 0 else ()
+                mm(4 * h + b, "wl%d" % t, "wls%d" % t, 128 * b, "mc", "msc", 128 * h, 128 * h + 128, extra)
+
+        def scale(h, b, q):
+            out = V("ft", 512 * h + b, 512 * h + 512, 4)
+            if q == "s":
+                act(out, bank(4 * h + b, 128), ACT.Copy, 0.03125)
+            else:
+                ts(out, bank(4 * h + b, 128), 0.03125, A.mult)
+
+        def end(h, e, q):
+            a = V("lb" if e else "la", lo + 8 * h, lo + 8 * h + 8)
+            if t < R:
+                w, o = V("ptab") if t == 1 else V("zp%d" % t), V("zp%d" % (t + 1), 384 * h + 2 * e, 384 * h + 384, 3)
+            else:
+                w, o = V("zi3"), V("elb", 513 * e + 256 * h, 512 * e + 256 * h + 256, 2)
+            if q == "s":
+                act(o, (w, a), ACT.Copy)
+            else:
+                copy(o, (w, a))
+
+        def fresh(h):
+            a = n + 128 * h
+            quant("tc", "tsc", a, a + 128, V("ft", 512 * h, 512 * h + 512))
+            mm(4 * h, "upc" if t < R else "vc", "ups" if t < R else "vsc", 0, "tc", "tsc", a, a + 128)
+
+        def diffs(h):
+            o = "zp%d" % (t + 1)
+            tt(V("dd", 256 * h, 256 * h + 256, 2), V(o, 384 * h, 384 * h + 384, 3), bank(4 * h, 128), A.subtract)
+            tt(V("dd", 256 * h + 1, 256 * h + 256, 2), V(o, 384 * h + 2, 384 * h + 384, 3), bank(4 * h, 128), A.subtract)
+
+        mid(0)
+        lists_a()
+        mid(1)
+        layer(0)
+        lists_b()
+        mid(2)
+        for b in range(4):
+            scale(0, b, "s")
+        end(0, 0, "s")
+        end(0, 1, "s")
+        mid(3)
+        if t < R:
+            fresh(0)
+            layer(1)
+            diffs(0)
+            end(1, 0, "s")
+            scale(1, 0, "v")
+            scale(1, 1, "v")
+            scale(1, 2, "v")
+            scale(1, 3, "s")
+            act(V("ss", 0, 256), V("dd", 0, 256), ACT.Abs)
+            count(col("cnt", 8), V("ss", 0, 256), THR1)
+            fresh(1)
+            end(1, 1, "v")
+            diffs(1)
+            act(V("ss", 256, 512, 2), V("dd", 256, 512, 2), ACT.Abs)
+            act(V("ss", 257, 512, 2), V("dd", 257, 512, 2), ACT.Abs)
+            for b in range(4):
+                mm(DB[b], "ec", "esc", 128 * b, "tc", "tsc", n, n + 256)
+            mm(6, "vc", "vsc", 0, "tc", "tsc", n, n + 256)
+            store_codes("y", n, n + 256)
+            store_scales("yyyy", n, n + 256)
+        else:
+            layer(1)
+            fresh(0)
+            store_codes("y", n, n + 128)
+            scale(1, 0, "v")
+            scale(1, 1, "s")
+            scale(1, 2, "v")
+            scale(1, 3, "s")
+            end(1, 0, "s")
+            end(1, 1, "s")
+            store("s", lambda: T.el[:, :], lambda: T.elb[0:128:16, :], [V("elb")])
+            fresh(1)
+            copy(V("ysb", n, n + 128), bank(0, 128))
+            store_y("y", n, n + 128)
+            store_codes("y", n + 128, n + 256)
+            store_scales("yyss", n, n + 256)
+            copy(V("ysb", n + 128, n + 256), bank(4, 128))
+            store_y("y", n + 128, n + 256)
+
+    emit(T, queue, ops)
+    g.wait_ge(T.sem.sent, sent)
+    g.sync.wait_ge(T.sem.outy, outs["y"])
+    g.scalar.wait_ge(T.sem.outs, outs["s"])
+
+
+def emit(T, queue, ops):
+    def bits(a):
+        if a[0] == "ps":
+            return 1 << (a[1] // 512)
+        m = 0
+        for c in range(a[1], a[2], a[3]):
+            m |= 1 << c
+        return m
+
+    seen, known, done, waits, needed = {}, {}, [], [], set()
+    for i, (q, call, reads, writes, sem, extra) in enumerate(ops):
+        deps = set()
+        touch = [(a[0], bits(a), False) for a in reads] + [(a[0], bits(a), True) for a in writes]
+        for name, m, w in touch:
+            for j, m2, w2 in seen.get(name, []):
+                if m & m2 and (w or w2 or (name == "ps" and ops[j][0] != q)):
+                    deps.add(j)
+        mine = []
+        for j in sorted(deps, reverse=True):
+            if not known.get(q, 0) >> j & 1:
+                mine.append(j)
+                needed.add(j)
+                known[q] = known.get(q, 0) | done[j]
+        waits.append(mine)
+        done.append(known.get(q, 0) | 1 << i)
+        for name, m, w in touch:
+            seen.setdefault(name, []).append((i, m, w))
+    used, token = {}, {}
+    for i, (q, call, reads, writes, sem, extra) in enumerate(ops):
+        for j in waits[i]:
+            queue[q].wait_ge(T.sem[token[j][0]], token[j][1])
+        for name, val in extra:
+            queue[q].wait_ge(T.sem[name], val)
+        ins = call()
+        if sem == "remote":
+            continue
+        if sem is not None:
+            ins.then_inc(T.sem[sem], 16)
+            token[i] = (sem, 16)
+        elif i in needed:
+            k = used.get(q, 0)
+            used[q] = k + 1
+            token[i] = (q + str(k % POOL[q]), k // POOL[q] + 1)
+            ins.then_inc(T.sem[token[i][0]], 1)

@@ -3,9 +3,7 @@ from concourse.mybir import dt, AluOpType, AxisListType, ActivationFunctionType
 N, C, K, R = 8, 256, 256, 3
 X4, U8 = "float8_e4m3fn_x4", "uint8"
 F32, BF, I32, U16 = "float32", "bfloat16", "int32", "uint16"
-NV = 192
-SHARE1 = [0, 0, 0, 0, 0, 0, 176, 128]
-SHARE = [0, 176, 0, 176, 176, 176, 176, 128]
+NV = 256
 
 
 def _sb(n, t):
@@ -30,15 +28,17 @@ SCRATCH = {
     "em": _sb(512, F32), "ic": _sb(256, F32), "rr": _sb(512, F32), "ex": _sb(256, F32), "ex2": _sb(256, F32),
     "c4": _sb(256, F32), "c16": _sb(256, F32), "k4": _sb(256, F32), "k16": _sb(256, F32),
     "pi": _sb(8, I32), "pj": _sb(8, I32), "pf": _sb(8, F32), "ui": _sb(8, I32), "uo": _sb(8, U16),
-    "ch": _sb(32, F32), "same": _sb(32, F32), "zc": _sb(32, F32), "zc2": _sb(32, F32), "zs": _sb(32, F32),
-    "mk": _sb(64, F32), "d1": _sb(33 * 8, F32), "js": _sb(8, F32), "tmp": _sb(64, F32), "cs": _sb(16, F32),
-    "xx": _sb(64, F32), "tr": _sb(40, F32), "th": _sb(33 * 8, F32), "cnt": _sb(16, F32),
+    "ch": _sb(32, F32), "same": _sb(32, F32),
+    "mk": _sb(64, F32), "js": _sb(8, F32), "tmp": _sb(64, F32), "cs": _sb(16, F32),
+    "xx": _sb(64, F32), "tr": _sb(32, BF), "th": _sb(32 * 9, F32), "cnt": _sb(16, F32),
     "sm": _sb(8, F32), "fl": _sb(130, F32), "keep": _sb(66, F32), "ll": _sb(97, F32), "qq": _sb(97, F32),
     "zz": _sb(33, F32), "yy": _sb(32, F32), "e1": _sb(33, F32),
     "prm": _sb(32, U16), "so": _sb(32, U16), "wi": _sb(64, I32), "wa": _sb(64, I32), "wb": _sb(64, I32),
     "oa": _sb(64 * 3, U16), "ob": _sb(64 * 3, U16), "la": _sb(16 * 3, U16), "lb": _sb(16 * 3, U16),
     "si": _sb(16, I32), "sa": _sb(16, I32), "sbi": _sb(16, I32), "sf": _sb(16, F32),
-    "vf": _sb(NV + 32, BF), "vf8": _sb(NV + 32, BF), "vo": _sb(NV + 32, BF),
+    "vf": _sb(NV + 34, BF), "vo": _sb(NV + 34, BF), "dz": _sb(NV + 34, BF), "dz2": _sb(NV + 34, BF), "vf1": _sb(33, F32),
+    "oth": _sb(32, F32), "rows": _sb(64, F32), "t1": _sb(32, F32), "t2": _sb(32, F32), "l2t": _sb(32, F32),
+    "gg": _sb(193, F32), "gl": _sb(193, F32), "row": _sb(32, F32), "row2": _sb(32, F32),
     "ps": ("psum", [128, 4096], F32),
 }
 POOL = {"v": 56, "s": 36, "t": 20, "g": 14}
@@ -46,6 +46,7 @@ LOADS = ["ldu", "lda", "ldb", "ldx0", "ldx1", "ldw", "ldws", "ldv"]
 SEMAPHORES = ([q + str(i) for q in POOL for i in range(POOL[q])] + LOADS
               + ["arr1", "arr2", "arr3", "sent", "outy", "outs"])
 BIG = 2.0 ** 30
+HUGE = 2.0 ** 84
 A = AluOpType
 ACT = ActivationFunctionType
 
@@ -103,6 +104,9 @@ def rank_program(g, core, T, topo):
 
     def turn(out, in_):
         add("v", lambda: g.vector.transpose(ap(out), ap(in_)), [in_], [out])
+
+    def product(out, in_):
+        add("v", lambda: g.vector.tensor_reduce(ap(out), ap(in_), AxisListType.X, A.mult), [in_], [out])
 
     def act(out, in_, func, scale=1.0):
         add("s", lambda: g.scalar.activation(ap(out), ap(in_), func, scale=scale), [in_], [out])
@@ -171,7 +175,7 @@ def rank_program(g, core, T, topo):
     iota(V("c16"), [[0, 16], [1, 16]])
     iota(V("ic"), [[1, 256]])
     iota(V("c4"), [[0, 64], [1, 4]])
-    fill(V("ones"), 1.0)
+    fill(V("ones"), 0.5)
     p = col("pi", 0)
     ts(col("pj", 0), p, 15, A.bitwise_and)
     ts(col("pj", 1), p, 4, A.arith_shift_right, 1, A.bitwise_and)
@@ -180,31 +184,26 @@ def rank_program(g, core, T, topo):
     copy(V("uo"), V("ui"))
     copy(V("pf", 0, 4), V("pj", 0, 4))
     fill(col("cs", 5), BIG)
-    fill(V("d1", 0, 66), 1.0)
-    fill(V("d1", 66), 0.0)
-    fill(V("tr"), 0.0)
-    fill(V("keep"), 1.0)
+    fill(V("dz"), 1.0)
+    fill(V("dz2"), 1.0)
     fill(V("vf", NV), 0.0)
-    fill(V("vf8", NV), 0.0)
-    ts(col("sm", 7), Q4, -1.0, A.mult)
-    ts(col("cs", 4), J, -1.0, A.mult)
-    ts(J32, J, 32.0, A.mult)
-    ts(V("same"), V("ch"), H, A.is_equal)
-    ts(col("sm", 0), J, 0.0, A.is_equal, 2048.0, A.mult)
+    fill(V("vf1"), 0.0)
+    fill(V("xx", 0, 16), 0.0)
     ts(V("tmp", 0, 16), V("c16", 0, 16), J, A.is_lt, 2047.0, A.mult)
     ts(V("tmp", 16, 32), V("c16", 0, 16), J, A.is_lt, 1.0, A.add)
-    fill(col("keep", 33), 0.0)
+    ts(V("same"), V("ch"), H, A.is_equal)
+    ts(col("sm", 7), Q4, -1.0, A.mult)
     ts(V("tmp", 0, 16), V("tmp", 0, 16), 1.0, A.add)
-    add("v", lambda: g.vector.tensor_reduce(ap(col("d1", 32)), ap(V("tmp", 16, 32)), AxisListType.X, A.mult),
-        [V("tmp", 16, 32)], [col("d1", 32)])
+    product(col("cs", 8), V("tmp", 16, 32))
     ts(col("sm", 1), J, 0.0, A.is_gt)
-    scan(V("tmp", 32, 48), V("tmp", 0, 16), V("d1", 66, 82), 2.0 ** -104, A.mult, A.add)
-    ts(col("sm", 2), J, 7.0, A.min, 0.5, A.add)
-    fill(col("js", 5), 2.0 ** -24)
+    ts(col("cs", 4), J, -1.0, A.mult)
+    scan(V("tmp", 32, 48), V("tmp", 0, 16), V("xx", 0, 16), 2.0 ** -104, A.mult, A.add)
+    ts(J32, J, 32.0, A.mult)
+    ts(V("oth"), V("same"), -1.0, A.mult, 1.0, A.add)
+    ts(V("xx", 32, 64), V("same"), col("cs", 8), A.mult)
     ts(THR1, col("tmp", 47), col("sm", 1), A.mult)
-    ts(V("zc2"), V("same"), -1.0, A.add, 4096.0, A.mult)
-    ts(col("d1", 65), J, 1.0 / 16, A.mult, 1.0, A.add)
-    ts(V("zc"), V("zc2"), col("sm", 0), A.add)
+    ts(col("sm", 2), J, 7.0, A.min, 0.5, A.add)
+    ts(col("vf1", 17), H, 2048.0 * HUGE, A.mult, -1024.0 * HUGE, A.add)
     copy(V("ebu"), V("ebi"))
     for k in range(4):
         act(col("js", k), J, ACT.Copy, 2.0 ** (-8 - 4 * k))
@@ -214,27 +213,66 @@ def rank_program(g, core, T, topo):
     lin(V("k16"), V("g2", 0, 256), -BIG, col("cs", 5), ACT.Relu)
     lin(V("ex"), V("c4"), 1.0, col("sm", 7), ACT.Abs)
     act(col("js", 4), col("sm", 2), ACT.Copy, 2.0 ** -23)
+    act(col("gg", 192), col("sm", 2), ACT.Copy, 2.0 ** -23)
+    act(col("vf", NV + 18), col("vf1", 17), ACT.Copy)
+
+    def early0():
+        ts(V("xx", 0, 32), V("same"), THR1, A.mult)
+        ts(V("tmp", 48, 64), V("c16", 0, 16), J, A.is_lt, -0.5, A.mult)
+        fill(col("dz", NV + 1), 0.5)
+        fill(col("dz2", 0), 0.5)
+        ts(col("vf1", 1), H, -1024.0 * HUGE, A.mult)
+        turn(V("rows"), V("xx"))
+        ts(V("tmp", 48, 64), V("tmp", 48, 64), 1.0, A.add)
+
+    def early1():
+        fill(col("dz", NV + 2), -HUGE)
+        fill(col("dz2", NV + 2), -HUGE)
+        ts(V("xx", 0, 32), V("oth"), 64.0 * HUGE, A.mult)
+        ts(V("t1"), V("rows", 0, 32), col("cs", 8), A.mult)
+        ts(col("sm", 0), J, 0.0, A.is_equal, 512.0 * HUGE, A.mult)
+        fill(col("vf", NV + 1), -0.25)
+        fill(col("vf", NV), 0.0)
+        product(col("cs", 9), V("tmp", 48, 64))
+        ts(V("tmp", 0, 32), V("oth"), 65536.0, A.mult)
+        ts(col("cs", 10), J, 1.0 / 16, A.mult, 1.0, A.add)
+
+    def early():
+        ts(col("vf", NV + 2), col("vf1", 1), col("sm", 0), A.add)
+        tt(V("t1"), V("t1"), V("xx", 0, 32), A.add)
+        ts(V("l2t"), V("rows", 32, 64), col("cs", 9), A.mult)
+        ts(V("rows", 0, 32), V("oth"), 2.0 ** 25, A.mult, J, A.subtract)
+        ts(V("tmp", 32, 64), V("c16", 0, 32), 7.0, A.min, J, A.add)
+        tt(V("l2t"), V("l2t"), V("tmp", 0, 32), A.add)
+        ts(col("cs", 11), col("js", 4), -1.0, A.mult, 2.0 ** -23, A.add)
+        tt(V("tmp", 32, 64), V("tmp", 32, 64), V("rows", 0, 32), A.add)
+        tt(V("rows", 0, 32), V("rows", 0, 32), V("c16", 0, 32), A.add)
+        ts(V("t2"), V("l2t"), col("cs", 10), A.mult)
+
+    def early2():
+        for k in range(5):
+            ts(V("gg", 32 * k, 32 * k + 32), V("rows", 0, 32), 2.0 ** (-4 - 4 * k), A.mult, col("js", k), A.add)
+        ts(V("gg", 160, 192), V("tmp", 32, 64), 2.0 ** -23, A.mult, col("cs", 11), A.add)
 
     small = [
-        lambda: ts(col("vf", NV + 16), H, 8192.0, A.mult, -4096.0, A.add),
-        lambda: ts(col("fl", 64), J, -16.0, A.mult, -0.5, A.add),
-        lambda: ts(V("tmp", 0, 32), V("c16", 0, 32), J, A.is_gt),
-        lambda: ts(col("sm", 3), J, 8.0, A.mult, 8.5, A.add),
-        lambda: tt(V("tmp", 32, 64), V("tmp", 0, 32), V("same"), A.mult),
-        lambda: ts(col("cs", 6), J, 16.0, A.mult, 16.5 - 8192.0 - 65536.0, A.add),
-        lambda: ts(KO, col("sm", 3), J, A.mult, -1672.0, A.add),
-        lambda: tt(V("mk", 0, 32), V("same"), V("tmp", 32, 64), A.subtract),
-        lambda: ts(V("mk", 32, 64), V("tmp", 32, 64), 65536.0, A.mult, col("cs", 6), A.add),
-        lambda: ts(col("cs", 7), KO, -1.0, A.mult, 256.0, A.add),
-        lambda: fill(V("ll", 0, 31), 8192.0),
+        lambda: (ts(col("fl", 64), J, -16.0, A.mult, -0.5, A.add),
+                 ts(V("tmp", 0, 32), V("c16", 0, 32), J, A.is_gt),
+                 ts(col("sm", 3), J, 8.0, A.mult, 8.5, A.add)),
+        lambda: (tt(V("tmp", 32, 64), V("tmp", 0, 32), V("same"), A.mult),
+                 ts(col("cs", 6), J, 16.0, A.mult, 16.5 - 8192.0 - 65536.0, A.add),
+                 ts(KO, col("sm", 3), J, A.mult, -1672.0, A.add)),
+        lambda: (tt(V("mk", 0, 32), V("same"), V("tmp", 32, 64), A.subtract),
+                 ts(V("mk", 32, 64), V("tmp", 32, 64), 65536.0, A.mult, col("cs", 6), A.add),
+                 ts(col("cs", 7), KO, -1.0, A.mult, 256.0, A.add)),
+        lambda: (fill(V("ll", 0, 31), 8192.0), fill(V("keep", 0, 33), 1.0), fill(V("keep", 34, 66), 1.0), fill(col("keep", 33), 0.0)),
     ]
 
     def late_constants():
         lin(V("k4"), V("ex"), -BIG, col("cs", 5), ACT.Relu)
         act(col("fl", 97), col("fl", 64), ACT.Copy)
-        act(col("vf8", NV + 16), col("vf", NV + 16), ACT.Copy)
-        act(col("vf", NV), col("zc", 0), ACT.Copy)
-        act(col("vf8", NV), col("zc2", 0), ACT.Copy)
+
+    def third(c):
+        act(V("z3", 1536 * c + 2, 1536 * c + 1536, 3), V("ones"), ACT.Copy)
 
     iota(V("em"), [[256, 32], [8192, 16]], -65536)
     for b in range(4):
@@ -271,104 +309,135 @@ def rank_program(g, core, T, topo):
     copy(V("eau"), V("eai"))
     mm(0, "upc", "ups", 0, "tc", "tsc", 0, 256)
     copy(V("prm"), V("e1", 0, 32))
+    early0()
     copy(V("ptab"), bank(0))
     store_codes("y", 0, 256)
     store_scales("yyyy", 0, 256)
     for h in range(2):
         act(V("pa", 256 * h, 256 * h + 256), (V("ptab"), V("eau", 16 * h, 16 * h + 16)), ACT.Copy)
     tt(V("g2", 0, 256), (V("ic"), V("eau", 0, 16)), V("g1", 0, 256), A.add)
+    early1()
     for h in range(2):
         tt(V("dd", 256 * h, 256 * h + 256), (V("ptab"), V("ebu", 16 * h, 16 * h + 16)), V("pa", 256 * h, 256 * h + 256), A.subtract)
     act(V("ss", 0, 256), V("dd", 0, 256), ACT.Abs)
     count(col("cnt", 8), V("ss", 0, 256), THR1)
     act(V("ss", 256, 512), V("dd", 256, 512), ACT.Abs)
-    tt(V("g2", 256, 512), (V("ic"), V("eau", 16, 32)), V("g1", 256, 512), A.add)
+    early()
 
     DB = [1, 2, 3, 5]
     for t in range(1, R + 1):
         n = C + (t - 1) * K
-        zw = V("z%d" % t)
-        zn = "z3" if t == 2 else "z2"
         oa, ob = 64 * (t - 1), 64 * (t - 1)
         lo = 16 * (t - 1)
 
-        def th(k, c):
-            return col("th", 33 * (k - 1) + c)
+        def th(k):
+            return col("th", 32 * k - 1)
 
-        LO2 = th(2, 31)
+        LO2 = col("th", 287)
 
-        def shared(k):
-            return (SHARE if t > 1 else SHARE1)[k - 1]
+        def unpack_first():
+            quant("vc", "vsc", 0, 128, V("vt"))
+            for b in range(4):
+                mm(DB[b], "ec", "esc", 128 * b, "tc", "tsc", 0, 256)
+            mm(6, "vc", "vsc", 0, "tc", "tsc", 0, 256)
 
-        def slot(k):
-            if k == 7:
-                ts(col("sm", 5), th(7, 32), col("d1", 263), A.add, LO2, A.add)
-                ts(col("sm", 6), th(7, 31), LO2, A.add)
-            if shared(k + 1):
-                nv = shared(k + 1)
-                f, thr = ("vf8", col("sm", 5)) if k == 7 else ("vf", th(k, 32))
-                ts(V(f, NV - nv, NV), V("ss", 512 - nv, 512), thr, A.is_lt, -2.0, A.mult)
-                if k == 6:
-                    ts(col("sm", 4), th(6, 32), LO2, A.subtract)
-                scan(V("vo", 0, nv + 32), V("ones", 0, nv + 32), V(f, NV - nv), float(nv), A.mult, A.add)
-            if k == 1 and t == 1:
-                turn(V("trs"), V("ss"))
-            if k == 2:
-                ts(V("d1", 98, 264, 33), V("js", 0, 6), LO2, A.mult)
-                ts(V("sp", 0, 512 - shared(8)), V("ss", 0, 512 - shared(8)), LO2, A.subtract)
-            if k == 3 and t == 1:
-                quant("ec", "esc", 0, 256, V("et", 0, 1024))
-                quant("ec", "esc", 256, 512, V("et", 1024, 2048))
-                quant("vc", "vsc", 0, 128, V("vt"))
-                for b in range(4):
-                    mm(DB[b], "ec", "esc", 128 * b, "tc", "tsc", 0, 256)
-                mm(6, "vc", "vsc", 0, "tc", "tsc", 0, 256)
-            if k == 4 and t == 1:
+        spread = [lambda: (copy(V("sx", 0, 16), V("trs", 0, 512, 32)), copy(V("sx", 16, 32), V("trs", 16, 512, 32))),
+                  lambda: turn(V("sd"), V("sx"))]
+        if t == 1:
+            work = ([early2]
+                    + [lambda c=c: tt(V("g2", c, c + 128), (V("ic"), V("eau", c // 16, c // 16 + 8)), V("g1", c, c + 128), A.add)
+                       for c in (256, 384)]
+                    + [lambda a=a, b=b: turn(V("trs", a, b), V("ss", a, b)) for a, b in ((0, 160), (160, 352), (352, 512))]
+                    + small
+                    + [lambda c=c: quant("ec", "esc", 128 * c, 128 * c + 128, V("et", 512 * c, 512 * c + 512)) for c in range(4)]
+                    + [unpack_first]
+                    + [lambda c=c: tt(V("vm", 128 * c, 128 * c + 128), (V("g2"), V("prm", 8 * c, 8 * c + 8)),
+                                      V("em", 128 * c, 128 * c + 128), A.add) for c in range(4)] + spread)
+            gaps = {1: work[0:2]}
+            for k in range(2, 9):
+                gaps[k] = work[3 * k - 4:3 * k - 1]
+        else:
+            def both(b, e, h):
+                a = 1536 * h + 3 * b
+                tt(V("z3", a + e, 1536 * h + 1536, 12), V("z%d" % t, a + 2 * e, 1536 * h + 1536, 12),
+                   V("ps", 512 * DB[b] + 128 * h, 512 * DB[b] + 128 * h + 128), A.add)
+
+            w = [lambda b=b, e=e, h=h: both(b, e, h) for e in range(2) for h in range(2) for b in range(4)]
+            gaps = {2: list(spread), 3: w[0:3], 4: w[3:6], 5: w[6:9], 6: w[9:12], 7: w[12:15], 8: w[15:16]}
+
+        def old(e, c):
+            o = "ob" if e else "oa"
+            act(V("z%d" % t, 768 * c + 2 * e, 768 * c + 768, 3), (V("z%d" % (t - 1)), V(o, oa - 64 + 16 * c, oa - 48 + 16 * c)), ACT.Copy)
+
+        def idle(k):
+            if t == 1 and k == 5:
                 late_constants()
-                tt(V("vm", 0, 256), (V("g2"), V("prm", 0, 16)), V("em", 0, 256), A.add)
-            if k == 5 and t == 1:
-                tt(V("vm", 256, 512), (V("g2"), V("prm", 16, 32)), V("em", 256, 512), A.add)
+            if t == 1 and k in (6, 7):
+                third(k - 6)
+            if t == 3 and k < 3:
+                old(0, 2 * k - 2)
+                old(0, 2 * k - 1)
+            if t > 1 and 3 <= k <= 6:
+                old(1, k - 3)
+            if k == 3:
+                act(col("sm", 5), LO2, ACT.Copy, -1.0)
+            if k == (4 if t == 1 else 7):
+                lin(V("sp"), V("ss"), 1.0, col("sm", 5), ACT.Identity)
 
-        gaps = list(small) if t == 1 else []
+        def gap(k):
+            if gaps.get(k):
+                gaps[k].pop(0)()
 
-        def gap():
-            if gaps:
-                gaps.pop(0)()
-
-        ts(V("zs"), V("zc2"), col("cnt", 8), A.subtract)
+        ts(col("vf1", 0), col("cnt", 8), 0.5, A.mult, -0.25, A.add)
         for k in range(1, 9):
-            thr = THR1 if k == 1 else th(k - 1, 32)
+            thr = THR1 if k == 1 else th(k - 1)
             cnt = col("cnt", k - 1)
-            nv = shared(k)
-            count(cnt, V("ss", 256, 512) if k == 1 else V("sp" if k == 8 else "ss", 0, 512 - nv), thr)
-            if k > 1:
-                slot(k - 1)
-            elif t > 1:
-                turn(V("trs", 0, 256), V("ss", 0, 256))
-                turn(V("trs", 256, 512), V("ss", 256, 512))
-            val = col("sm", 4) if k == 7 else col("sm", 5) if k == 8 else thr
-            ts(V("xx", 0, 32), V("vo", nv, nv + 32) if nv else V("zs" if k == 1 else "zc"), cnt, A.is_ge, val, A.mult)
-            gap()
-            turn(V("tr", 0, 32), V("xx", 0, 32))
-            gap()
+            src = "sp" if k == 8 else "ss"
+            row = V("t1") if k == 1 else V("row")
             if k == 1:
-                gaps.extend([lambda: copy(V("sx", 0, 16), V("trs", 0, 512, 32)), lambda: copy(V("sx", 16, 32), V("trs", 16, 512, 32)),
-                             lambda: turn(V("sd"), V("sx"))])
-            if k < 8:
-                scan(V("th", 33 * (k - 1), 33 * k), V("tr", 0, 33), V("d1", 33 * (k - 1), 33 * k), 0.0, A.max,
-                     A.mult if k < 3 else A.add)
+                count(cnt, V("ss", 256, 512), thr)
+                idle(k)
+                if t > 1:
+                    turn(V("trs", 0, 256), V("ss", 0, 256))
+                    turn(V("trs", 256, 512), V("ss", 256, 512))
+                scan(V("vo", NV + 1), V("dz", NV + 1), V("vf1"), cnt, A.mult, A.add)
             else:
-                scan(V("th", 231, 263), V("tr", 0, 32), V("d1", 231, 263), col("sm", 6), A.max, A.add)
-        TT = th(8, 31)
+                count(cnt, V(src, 0, 512 - NV), thr)
+                idle(k)
+                ts(V("vf", 0, NV), V(src, 512 - NV, 512), thr, A.is_lt, -0.5, A.add)
+                if k == 2:
+                    ts(row, V("t2"), thr, A.mult)
+                    ts(V("row2"), V("l2t"), thr, A.mult)
+                elif k == 3:
+                    ts(V("gl"), V("gg"), LO2, A.mult)
+                elif k == 7:
+                    ts(col("sm", 4), thr, LO2, A.subtract)
+                elif k == 8:
+                    ts(row, V("gl", 160, 192), thr, A.add, LO2, A.add)
+                    ts(col("sm", 6), thr, col("gl", 192), A.subtract, LO2, A.add)
+                else:
+                    ts(row, V("gl", 32 * k - 96, 32 * k - 64), thr, A.add)
+                scan(V("vo", 0, NV + 34), V("dz2"), V("vf"), cnt, A.mult, A.add)
+                if k == 3 or k == 7:
+                    ts(row, V("gl", 32 * k - 96, 32 * k - 64), thr if k == 3 else col("sm", 4), A.add)
+            gap(k)
+            turn(V("tr"), V("vo", NV + 2))
+            gap(k)
+            scan(V("th", 32 * k - 32, 32 * k), V("tr"), row, col("sm", 6) if k == 8 else 0.0, A.max, A.min)
+            if k == 2:
+                scan(V("th", 256, 288), V("tr"), V("row2"), 0.0, A.max, A.min)
+            if k == 7:
+                copy(col("vf", NV + 2), col("vf1", 1))
+            if k == 8 and t < R:
+                ts(col("vf", NV + 2), col("vf1", 1), col("sm", 0), A.add)
+            gap(k)
+        TT = th(8)
 
         if t > 1:
-            zo = V("z%d" % (t - 1))
             for h in range(2):
                 act(V("zp%d" % t, 384 * h + 1, 384 * h + 384, 3), bank(4 * h, 128), ACT.Copy)
-            for c in range(2):
-                act(V(zw[0], 1536 * c + 2, 1536 * c + 1536, 3), (zo, V("ob", ob - 64 + 32 * c, ob - 32 + 32 * c)), ACT.Copy)
-        for b in range(4):
-            act(V("z1", b, 1024, 4) if t == 1 else V(zw[0], 3 * b + 1, 3072, 12), bank(DB[b]), ACT.Copy, 0.5)
+        for b in range(4 if t < R else 0):
+            act(V("z1", b, 1024, 4) if t == 1 else V("z2", 3 * b + 1, 3072, 12), bank(DB[b]), ACT.Copy)
         if t > 1:
             iw = V("ic") if t == 2 else V("zi2")
             act(V("zi%d" % t, 0, 768, 3), (iw, V("la", lo - 16, lo)), ACT.Copy)
@@ -395,17 +464,11 @@ def rank_program(g, core, T, topo):
             ts(V("wb"), V("wi"), 255, A.bitwise_and)
             ts(V("oa", 0, 64), V("wa"), 4.0, A.mult, B, A.add)
             ts(V("ob", 0, 64), V("wb"), 4.0, A.mult, B, A.add)
+            for c in range(4):
+                act(V("z2", 768 * c, 768 * c + 768, 3), (V("z1"), V("oa", 16 * c, 16 * c + 16)), ACT.Copy)
         else:
             ts(V("oa", oa, oa + 64), exv, B3, A.add)
-            ts(V("ob", ob, ob + 64), exv, B3, A.add, 1.0, A.add)
-
-        for c in range(4):
-            act(V(zn, 768 * c, 768 * c + 768, 3), (zw, V("oa", oa + 16 * c, oa + 16 * c + 16)), ACT.Copy)
         scan(V("ex2"), V("k16"), V("rr", 256, 512), 0.0, A.add, A.min)
-        if t == 1:
-            ts(V("si"), ex2v, 256.0, A.mult)
-        else:
-            ts(V("sf"), ex2v, 0.25, A.mult, 0.4, A.add)
 
         def lists_a():
             if t == 1:
@@ -422,7 +485,14 @@ def rank_program(g, core, T, topo):
                 ts(V("lb", lo, lo + 16), V("sa"), 1.0, A.add)
 
         def mid(c):
-            tt(V("mt", 256 * c, 256 * c + 256), (zw, V("ob", ob + 16 * c, ob + 16 * c + 16)), V(zn, 768 * c, 768 * c + 768, 3), A.add)
+            tt(V("mt", 256 * c, 256 * c + 256), (V("z1"), V("ob", 16 * c, 16 * c + 16)), V("z2", 768 * c, 768 * c + 768, 3), A.add)
+
+        def pick(c, q):
+            o, i = V("mt", 256 * c, 256 * c + 256), (V("z3"), V("oa", oa + 16 * c, oa + 16 * c + 16))
+            if q == "s":
+                act(o, i, ACT.Copy)
+            else:
+                copy(o, i)
 
         def layer(h):
             quant("mc", "msc", 128 * h, 128 * h + 128, V("mt", 512 * h, 512 * h + 512))
@@ -459,31 +529,49 @@ def rank_program(g, core, T, topo):
             tt(V("dd", 256 * h, 256 * h + 256, 2), V(o, 384 * h, 384 * h + 384, 3), bank(4 * h, 128), A.subtract)
             tt(V("dd", 256 * h + 1, 256 * h + 256, 2), V(o, 384 * h + 2, 384 * h + 384, 3), bank(4 * h, 128), A.subtract)
 
-        mid(0)
-        lists_a()
-        mid(1)
-        layer(0)
-        lists_b()
-        mid(2)
-        for b in range(4):
-            scale(0, b, "s")
-        end(0, 0, "s")
-        end(0, 1, "s")
-        mid(3)
-        if t < R:
-            fresh(0)
+        if t == 1:
+            ts(V("si"), ex2v, 256.0, A.mult)
+            lists_a()
+            mid(0)
+            mid(1)
+            lists_b()
+            layer(0)
+            mid(2)
+            for b in range(4):
+                scale(0, b, "s")
+            end(0, 0, "s")
+            end(0, 1, "s")
+            mid(3)
             layer(1)
-            diffs(0)
+        else:
+            pick(0, "s")
+            pick(1, "v")
+            pick(2, "s")
+            ts(V("sf"), ex2v, 0.25, A.mult, 0.4, A.add)
+            layer(0)
+            pick(3, "v")
+            lists_a()
+            layer(1)
+            lists_b()
+            for b in range(4):
+                scale(0, b, "s")
+            end(0, 0, "s")
+            end(0, 1, "v")
+        fresh(0)
+        if t < R:
             end(1, 0, "s")
             scale(1, 0, "v")
-            scale(1, 1, "v")
+            scale(1, 1, "s")
             scale(1, 2, "v")
             scale(1, 3, "s")
+            diffs(0)
+            fresh(1)
             act(V("ss", 0, 256), V("dd", 0, 256), ACT.Abs)
             count(col("cnt", 8), V("ss", 0, 256), THR1)
-            fresh(1)
             end(1, 1, "v")
             diffs(1)
+            if t == 2:
+                ts(V("ob", ob, ob + 64), exv, B3, A.add, 1.0, A.add)
             act(V("ss", 256, 512, 2), V("dd", 256, 512, 2), ACT.Abs)
             act(V("ss", 257, 512, 2), V("dd", 257, 512, 2), ACT.Abs)
             for b in range(4):
@@ -492,8 +580,6 @@ def rank_program(g, core, T, topo):
             store_codes("y", n, n + 256)
             store_scales("yyyy", n, n + 256)
         else:
-            layer(1)
-            fresh(0)
             store_codes("y", n, n + 128)
             scale(1, 0, "v")
             scale(1, 1, "s")

@@ -4,6 +4,7 @@ N, C, K, R = 8, 256, 256, 3
 X4, U8 = "float8_e4m3fn_x4", "uint8"
 F32, BF, I32, U16 = "float32", "bfloat16", "int32", "uint16"
 NV = 256
+NF = NV + 36
 
 
 def _sb(n, t):
@@ -19,36 +20,38 @@ SCRATCH = {
     "wo": _sb(512, X4), "wos": _sb(512, U8),
     "wl1": _sb(512, X4), "wls1": _sb(512, U8), "wl2": _sb(512, X4), "wls2": _sb(512, U8),
     "wl3": _sb(512, X4), "wls3": _sb(512, U8),
-    "ones": _sb(512, BF), "et": _sb(2048, BF), "mt": _sb(1024, BF), "ft": _sb(1024, BF),
-    "z1": _sb(1024, BF), "z2": _sb(3072, BF), "z3": _sb(3072, BF),
+    "ones": _sb(516, BF), "et": _sb(516, BF), "mt": _sb(1024, BF), "ft": _sb(1024, BF),
+    "z1": _sb(1024, BF), "ea2": _sb(2048, BF), "eb2": _sb(2048, BF), "a3": _sb(1024, BF), "b3": _sb(1024, BF),
+    "mid": _sb(2048, BF),
     "ptab": _sb(256, F32), "pa": _sb(512, F32), "dd": _sb(512, F32), "ss": _sb(512, F32), "sp": _sb(512, F32),
-    "junk": _sb(512, BF), "trs": _sb(512, F32), "sx": _sb(32, F32), "sd": _sb(32, F32),
-    "zp2": _sb(768, F32), "zp3": _sb(768, F32), "zi2": _sb(768, F32), "zi3": _sb(768, F32), "elb": _sb(1024, F32),
-    "ysb": _sb(1024, F32), "g1": _sb(512, F32), "g2": _sb(512, F32), "vm": _sb(512, F32), "phm": _sb(512, F32),
-    "em": _sb(512, F32), "ic": _sb(256, F32), "rr": _sb(512, F32), "ex": _sb(256, F32), "ex2": _sb(256, F32),
-    "c4": _sb(256, F32), "c16": _sb(256, F32), "k4": _sb(256, F32), "k16": _sb(256, F32),
+    "junk": _sb(512, BF), "sd": _sb(32 * R, F32),
+    "pa2": _sb(512, F32), "pb2": _sb(512, F32), "pa3": _sb(256, F32), "pb3": _sb(256, F32),
+    "ia2": _sb(512, F32), "ib2": _sb(512, F32), "ia3": _sb(512, F32), "ib3": _sb(512, F32), "elb": _sb(1024, F32),
+    "ysb": _sb(1024, F32), "xl": _sb(64, F32), "x0": _sb(512, F32), "xr": _sb(512, F32), "phm": _sb(512, BF),
+    "ic": _sb(256, F32), "r1": _sb(1024, F32), "r2": _sb(1024, BF), "ex1": _sb(256, F32), "ex2": _sb(256, BF),
+    "c16": _sb(256, BF), "k1": _sb(256, F32), "k1a": _sb(256, BF), "k1b": _sb(256, F32), "k2": _sb(256, BF),
     "pi": _sb(8, I32), "pj": _sb(8, I32), "pf": _sb(8, F32), "ui": _sb(8, I32), "uo": _sb(8, U16),
-    "ch": _sb(32, F32), "same": _sb(32, F32),
-    "mk": _sb(64, F32), "js": _sb(8, F32), "tmp": _sb(64, F32), "cs": _sb(16, F32),
-    "xx": _sb(64, F32), "tr": _sb(32, BF), "th": _sb(32 * 9, F32), "cnt": _sb(16, F32),
-    "sm": _sb(8, F32), "fl": _sb(130, F32), "keep": _sb(66, F32), "ll": _sb(97, F32), "qq": _sb(97, F32),
-    "zz": _sb(33, F32), "yy": _sb(32, F32), "e1": _sb(33, F32),
-    "prm": _sb(32, U16), "so": _sb(32, U16), "wi": _sb(64, I32), "wa": _sb(64, I32), "wb": _sb(64, I32),
-    "oa": _sb(64 * 3, U16), "ob": _sb(64 * 3, U16), "la": _sb(16 * 3, U16), "lb": _sb(16 * 3, U16),
-    "si": _sb(16, I32), "sa": _sb(16, I32), "sbi": _sb(16, I32), "sf": _sb(16, F32),
-    "vf": _sb(NV + 34, BF), "vo": _sb(NV + 34, BF), "dz": _sb(NV + 34, BF), "dz2": _sb(NV + 34, BF), "vf1": _sb(33, F32),
-    "oth": _sb(32, F32), "rows": _sb(64, F32), "t1": _sb(32, F32), "t2": _sb(32, F32), "l2t": _sb(32, F32),
-    "gg": _sb(193, F32), "gl": _sb(193, F32), "row": _sb(32, F32), "row2": _sb(32, F32),
+    "c32": _sb(32, F32), "cm": _sb(32, F32), "oth": _sb(32, F32), "tmp": _sb(128, F32), "cs": _sb(32, F32),
+    "xx": _sb(64, F32), "rows": _sb(64, F32), "tr": _sb(32, BF), "th": _sb(32 * 9, F32), "cnt": _sb(16, F32),
+    "sm": _sb(8, F32), "t1": _sb(32, F32), "t2": _sb(32, F32), "l2t": _sb(32, F32), "aa": _sb(32, F32),
+    "gg": _sb(193, F32), "gl": _sb(193, F32), "row": _sb(32 * 9, F32),
+    "vf1": _sb(292, BF), "vf": _sb(NF, BF), "vf8": _sb(NF, BF), "vo": _sb(max(NF, 292), BF), "dz": _sb(NF, BF),
+    "dz1": _sb(292, BF),
+    "fgt": _sb(64, F32), "mgt": _sb(64, F32), "mge": _sb(64, F32), "oge": _sb(64, F32),
+    "h0": _sb(256, F32), "h1": _sb(256, F32), "qq": _sb(160, F32), "j0": _sb(96, F32), "yy": _sb(96, F32),
+    "so": _sb(32, U16), "wi": _sb(16, I32), "wb": _sb(16, I32), "la": _sb(16, U16), "lb": _sb(16, U16),
+    "l2": _sb(16, U16), "l3": _sb(16, U16),
     "ps": ("psum", [128, 4096], F32),
 }
-POOL = {"v": 56, "s": 36, "t": 20, "g": 14}
-LOADS = ["ldu", "lda", "ldb", "ldx0", "ldx1", "ldw", "ldws", "ldv"]
+POOL = {"v": 56, "s": 40, "t": 20, "g": 10}
+LOADS = ["ldu", "lda", "ldb", "ldx0", "ldx1", "ldw", "ldws", "ldv", "row0", "row1", "rows", "sd1", "sd2", "sd3"]
 SEMAPHORES = ([q + str(i) for q in POOL for i in range(POOL[q])] + LOADS
               + ["arr1", "arr2", "arr3", "sent", "outy", "outs"])
-BIG = 2.0 ** 30
 HUGE = 2.0 ** 84
+UP, DOWN = 2.0 ** 60, 2.0 ** -60
 A = AluOpType
 ACT = ActivationFunctionType
+CY, WAKE, GATHER, SCATTER = 1.04, 150.0, 1.56, 3.8
 
 
 def rank_program(g, core, T, topo):
@@ -78,73 +81,91 @@ def rank_program(g, core, T, topo):
                 out += list(a) if len(a) == 2 else [a]
         return out
 
-    def add(q, call, reads, writes, sem=None, extra=()):
-        ops.append((q, call, flat(reads), flat(writes), sem, extra))
+    def size(a):
+        return 16 * size(a[1]) if len(a) == 2 else len(range(a[1], a[2], a[3]))
+
+    def vcost(*sides):
+        n = size(sides[0])
+        if len(sides[0]) == 2:
+            return 50 + n * GATHER * CY
+        return max(64, n * (0.5 if all(SCRATCH[a[0]][2] in (BF, U16) for a in sides) else 1)) * CY
+
+    def add(q, call, reads, writes, cost, sem=None, extra=(), late=None):
+        ops.append((q, call, flat(reads), flat(writes), sem, extra, cost, cost if late is None else late))
 
     def copy(out, in_):
         if len(out) == 2:
-            add("v", lambda: g.vector.tensor_copy(ap(out), ap(in_)), [in_, out[1]], [out[0]])
+            add("v", lambda: g.vector.tensor_copy(ap(out), ap(in_)), [in_, out[1]], [out[0]], 50 + size(in_) * SCATTER * CY)
         else:
-            add("v", lambda: g.vector.tensor_copy(ap(out), ap(in_)), [in_], [out])
+            add("v", lambda: g.vector.tensor_copy(ap(out), ap(in_)), [in_], [out], vcost(in_, out))
 
     def tt(out, a, b, op):
-        add("v", lambda: g.vector.tensor_tensor(ap(out), ap(a), ap(b), op), [a, b], [out])
+        k = 1 if "ps" in (a[0], b[0]) else 2
+        add("v", lambda: g.vector.tensor_tensor(ap(out), ap(a), ap(b), op), [a, b], [out],
+            (50 if len(a) == 2 else 0) + max(64, k * size(a)) * CY)
 
     def ts(out, a, s1, op0, s2=None, op1=None):
         if op1 is None:
-            add("v", lambda: g.vector.tensor_scalar(ap(out), ap(a), ap(s1), None, op0), [a, s1], [out])
+            add("v", lambda: g.vector.tensor_scalar(ap(out), ap(a), ap(s1), None, op0), [a, s1], [out], vcost(a, out))
         else:
-            add("v", lambda: g.vector.tensor_scalar(ap(out), ap(a), ap(s1), ap(s2), op0, op1), [a, s1, s2], [out])
+            add("v", lambda: g.vector.tensor_scalar(ap(out), ap(a), ap(s1), ap(s2), op0, op1), [a, s1, s2], [out], vcost(a, out))
 
     def fill(out, c):
-        add("v", lambda: g.vector.memset(ap(out), c), [], [out])
+        add("v", lambda: g.vector.memset(ap(out), c), [], [out], vcost(out))
 
     def scan(out, d0, d1, init, op0, op1):
-        add("v", lambda: g.vector.tensor_tensor_scan(ap(out), ap(d0), ap(d1), ap(init), op0, op1), [d0, d1, init], [out])
+        add("v", lambda: g.vector.tensor_tensor_scan(ap(out), ap(d0), ap(d1), ap(init), op0, op1), [d0, d1, init], [out],
+            vcost(d0, d1, out))
 
     def turn(out, in_):
-        add("v", lambda: g.vector.transpose(ap(out), ap(in_)), [in_], [out])
+        add("v", lambda: g.vector.transpose(ap(out), ap(in_)), [in_], [out], vcost(in_, out))
 
     def product(out, in_):
-        add("v", lambda: g.vector.tensor_reduce(ap(out), ap(in_), AxisListType.X, A.mult), [in_], [out])
+        add("v", lambda: g.vector.tensor_reduce(ap(out), ap(in_), AxisListType.X, A.mult), [in_], [out], vcost(in_))
 
-    def act(out, in_, func, scale=1.0):
-        add("s", lambda: g.scalar.activation(ap(out), ap(in_), func, scale=scale), [in_], [out])
+    def act(out, in_, func=ACT.Copy, scale=1.0):
+        add("s", lambda: g.scalar.activation(ap(out), ap(in_), func, scale=ap(scale)), [in_, scale], [out],
+            65 + size(in_) * CY * (GATHER if len(in_) == 2 else 1))
 
-    def lin(out, in_, scale, bias, func):
-        add("s", lambda: g.scalar.activation(ap(out), ap(in_), func, bias=ap(bias), scale=scale), [in_, bias], [out])
+    def lin(out, in_, scale, bias):
+        add("s", lambda: g.scalar.activation(ap(out), ap(in_), ACT.Identity, bias=ap(bias), scale=ap(scale)), [in_, bias, scale], [out],
+            65 + size(in_) * CY)
+
+    def move(q, out, in_):
+        if q == "s":
+            act(out, in_)
+        else:
+            copy(out, in_)
 
     def count(cnt, in_, thr):
         junk = V("junk", in_[1], in_[2])
         add("s", lambda: g.scalar.activation(ap(junk), ap(in_), ACT.Sign, bias=ap(thr), scale=-1.0, accum_out=ap(cnt)),
-            [in_, thr], [junk, cnt])
+            [in_, thr], [junk, cnt], 85 + size(in_) * CY)
 
     def quant(codes, scales, a, b, in_):
         add("v", lambda: g.vector.quantize_mx(T[codes][:, a:b], T[scales][:, a:b], ap(in_)), [in_],
-            [V(codes, a, b), V(scales, a, b)])
+            [V(codes, a, b), V(scales, a, b)], (12 + 0.22 * size(in_)) * CY / 0.83)
 
     def mm(bank, lc, ls, a, rc, rs, c, d, extra=()):
         out = V("ps", 512 * bank, 512 * bank + d - c)
         add("t", lambda: g.tensor.matmul_mx(ap(out), T[lc][:, a:a + 128], T[ls][:, a:a + 128], T[rc][:, c:d], T[rs][:, c:d],
                                             True, True),
-            [V(lc, a, a + 128), V(ls, a, a + 128), V(rc, c, d), V(rs, c, d)], [out], None, extra)
+            [V(lc, a, a + 128), V(ls, a, a + 128), V(rc, c, d), V(rs, c, d)], [out], (d - c + 16) * 0.9, None, extra)
 
-    def bank(b, n=256):
-        return V("ps", 512 * b, 512 * b + n)
+    def bank(b, a=0, n=256):
+        return V("ps", 512 * b + a, 512 * b + a + n)
 
     def iota(out, pattern, base=0, mult=0):
         if SCRATCH[out[0]][2] == I32:
-            add("g", lambda: g.iota(ap(out), pattern, base, mult), [], [out])
+            add("g", lambda: g.iota(ap(out), pattern, base, mult), [], [out], 130 + 2 * CY * size(out))
         else:
-            add("g", lambda: g.iota(ap(out), pattern, base, mult, allow_small_or_imprecise_dtypes=True), [], [out])
+            add("g", lambda: g.iota(ap(out), pattern, base, mult, allow_small_or_imprecise_dtypes=True), [], [out],
+                130 + 2 * CY * size(out))
 
-    def dma(q, out, in_, reads, writes, sem):
-        add(q, lambda: queue[q].dma_start(out(), in_()), reads, writes, sem)
-
-    outs = {"y": 0, "s": 0}
+    def dma(q, out, in_, reads, writes, sem, late=2400):
+        add(q, lambda: queue[q].dma_start(out(), in_()), reads, writes, 60, sem, (), late)
 
     def store(q, out, in_, reads):
-        outs[q] += 16
         dma(q, out, in_, reads, [], "out" + q)
 
     def store_codes(q, a, b):
@@ -157,452 +178,347 @@ def rank_program(g, core, T, topo):
     def store_y(q, a, b):
         store(q, lambda: T.y[:, a:b], lambda: T.ysb[:, a:b], [V("ysb", a, b)])
 
-    J, H, B, Q4 = col("pf", 0), col("pf", 1), col("pf", 2), col("pf", 3)
-    THR1, B3, KO, J32 = col("cs", 0), col("cs", 1), col("cs", 2), col("cs", 3)
+    J, RR, H = col("pf", 0), col("pf", 1), col("cs", 0)
+    THR1, NTH, P2, P2N = col("cs", 1), col("cs", 2), col("cs", 3), col("cs", 4)
 
     dma("y", lambda: T.ut[:], lambda: T.u[:], [], [V("ut")], "ldu")
     dma("s", lambda: T.xt[:, 0:512], lambda: T.x[:, 0:512], [], [V("xt", 0, 512)], "ldx0")
     dma("y", lambda: T.xt[:, 512:1024], lambda: T.x[:, 512:1024], [], [V("xt", 512, 1024)], "ldx1")
     dma("s", lambda: T.ebi[:], lambda: T.eb[:], [], [V("ebi")], "ldb")
     dma("y", lambda: T.eai[:], lambda: T.ea[:], [], [V("eai")], "lda")
-    dma("y", lambda: T.wo[:].bitcast(dt.uint8), lambda: T.wc[:], [V("xt"), V("ut")], [V("wo")], "ldw")
-    dma("y", lambda: T.wos[:], lambda: T.ws[:], [], [V("wos")], "ldws")
-    dma("y", lambda: T.vt[:], lambda: T.v[:], [], [V("vt")], "ldv")
+    dma("y", lambda: T.wo[:].bitcast(dt.uint8), lambda: T.wc[:], [V("xt"), V("ut")], [V("wo")], "ldw", 3000)
+    dma("y", lambda: T.wos[:], lambda: T.ws[:], [V("xt")], [V("wos")], "ldws")
+    dma("y", lambda: T.vt[:], lambda: T.v[:], [V("xt")], [V("vt")], "ldv")
 
     iota(col("pi", 0), [[0, 1]], 0, 1)
     iota(V("ui"), [[16, 8]])
-    iota(V("ch"), [[1, 2], [0, 16]])
-    iota(V("c16"), [[0, 16], [1, 16]])
-    iota(V("ic"), [[1, 256]])
-    iota(V("c4"), [[0, 64], [1, 4]])
-    fill(V("ones"), 0.5)
-    p = col("pi", 0)
-    ts(col("pj", 0), p, 15, A.bitwise_and)
-    ts(col("pj", 1), p, 4, A.arith_shift_right, 1, A.bitwise_and)
-    ts(col("pj", 2), p, 3, A.bitwise_and)
-    ts(col("pj", 3), p, 2, A.arith_shift_right, 3, A.bitwise_and)
+    iota(V("c32"), [[1, 32]])
+    iota(V("cm"), [[0, 2], [1, 16]])
+    c16 = V("cm", 0, 16)
+    ts(col("pj", 0), col("pi", 0), 15, A.bitwise_and)
+    ts(col("pj", 1), col("pi", 0), 31, A.bitwise_and)
     copy(V("uo"), V("ui"))
-    copy(V("pf", 0, 4), V("pj", 0, 4))
-    fill(col("cs", 5), BIG)
-    fill(V("dz"), 1.0)
-    fill(V("dz2"), 1.0)
-    fill(V("vf", NV), 0.0)
-    fill(V("vf1"), 0.0)
-    fill(V("xx", 0, 16), 0.0)
-    ts(V("tmp", 0, 16), V("c16", 0, 16), J, A.is_lt, 2047.0, A.mult)
-    ts(V("tmp", 16, 32), V("c16", 0, 16), J, A.is_lt, 1.0, A.add)
-    ts(V("same"), V("ch"), H, A.is_equal)
-    ts(col("sm", 7), Q4, -1.0, A.mult)
-    ts(V("tmp", 0, 16), V("tmp", 0, 16), 1.0, A.add)
-    product(col("cs", 8), V("tmp", 16, 32))
+    copy(V("pf", 0, 2), V("pj", 0, 2))
+    ts(H, RR, 16.0, A.is_ge)
+    ts(V("oth"), V("c32"), 16.0, A.is_ge, H, A.not_equal)
+    ts(V("tmp", 0, 16), c16, J, A.is_lt, 2048.0, A.mult)
+    ts(V("tmp", 16, 32), V("tmp", 0, 16), 1.0, A.max)
+    fill(V("tmp", 32, 48), 0.0)
+    scan(V("tmp", 48, 64), V("tmp", 16, 32), V("tmp", 32, 48), 2.0 ** -104, A.mult, A.add)
     ts(col("sm", 1), J, 0.0, A.is_gt)
-    ts(col("cs", 4), J, -1.0, A.mult)
-    scan(V("tmp", 32, 48), V("tmp", 0, 16), V("xx", 0, 16), 2.0 ** -104, A.mult, A.add)
-    ts(J32, J, 32.0, A.mult)
-    ts(V("oth"), V("same"), -1.0, A.mult, 1.0, A.add)
-    ts(V("xx", 32, 64), V("same"), col("cs", 8), A.mult)
-    ts(THR1, col("tmp", 47), col("sm", 1), A.mult)
-    ts(col("sm", 2), J, 7.0, A.min, 0.5, A.add)
-    ts(col("vf1", 17), H, 2048.0 * HUGE, A.mult, -1024.0 * HUGE, A.add)
-    copy(V("ebu"), V("ebi"))
+    ts(THR1, col("tmp", 63), col("sm", 1), A.mult)
+    act(NTH, THR1, ACT.Copy, -1.0)
+    ts(V("tmp", 64, 80), c16, J, A.is_lt, 1.0, A.add)
+    product(P2, V("tmp", 64, 80))
+    ts(V("tmp", 80, 96), c16, J, A.is_ge, 1.0, A.add)
+    product(P2N, V("tmp", 80, 96))
+    ts(V("xx", 0, 32), V("oth"), 2.0 ** 90, A.mult, THR1, A.max)
+    ts(V("xx", 32, 64), V("oth"), 2.0 ** 32, A.mult, P2, A.max)
+    turn(V("rows"), V("xx"))
+    act(V("t1"), V("rows", 0, 32), ACT.Copy, P2)
+    ts(V("l2t"), V("rows", 32, 64), P2N, A.mult, 2.0 ** -16, A.mult)
+    ts(col("cs", 5), J, 1.0 / 16, A.mult, 1.0, A.add)
+    act(V("t2"), V("l2t"), ACT.Copy, col("cs", 5))
+    ts(V("tmp", 96, 128), V("oth"), 2.0 ** 25, A.mult)
+    tt(V("aa"), V("tmp", 96, 128), V("cm"), A.add)
     for k in range(4):
-        act(col("js", k), J, ACT.Copy, 2.0 ** (-8 - 4 * k))
-    act(B3, B, ACT.Copy, 3.0)
-    lin(V("g2", 0, 256), V("c16"), 1.0, col("cs", 4), ACT.Abs)
-    lin(V("e1"), V("ic", 0, 33), 1.0, J32, ACT.Identity)
-    lin(V("k16"), V("g2", 0, 256), -BIG, col("cs", 5), ACT.Relu)
-    lin(V("ex"), V("c4"), 1.0, col("sm", 7), ACT.Abs)
-    act(col("js", 4), col("sm", 2), ACT.Copy, 2.0 ** -23)
-    act(col("gg", 192), col("sm", 2), ACT.Copy, 2.0 ** -23)
-    act(col("vf", NV + 18), col("vf1", 17), ACT.Copy)
+        act(col("cs", 8 + k), J, ACT.Copy, -15 * 2.0 ** (-8 - 4 * k))
+    ts(col("cs", 12), J, -7 * 2.0 ** -23, A.mult, 2.0 ** -24, A.add)
+    ts(col("cs", 13), J, -2.0 ** -23, A.mult, 2.0 ** -24, A.add)
+    ts(col("gg", 192), J, 2.0 ** -23, A.mult, 2.0 ** -24, A.add)
+    for k in range(6):
+        lin(V("gg", 32 * k, 32 * k + 32), V("aa"), 2.0 ** (-4 - 4 * k if k < 5 else -23), col("cs", 8 + k))
+    act(col("cs", 14), H, ACT.Copy, -1024.0 * HUGE)
+    ts(col("cs", 15), H, 2048.0 * HUGE, A.mult, -1024.0 * HUGE, A.add)
+    ts(col("cs", 16), J, 0.0, A.is_equal, 512.0 * HUGE, A.mult)
+    for name, n in (("dz1", 256), ("dz", NV)) if NV != 256 else (("dz", NV),):
+        fill(V(name, 0, 2), 1.0)
+        fill(col(name, 2), 0.5)
+        fill(V(name, 3, n + 4), 1.0)
+        fill(col(name, n + 4), -HUGE)
+        fill(V(name, n + 5, n + 36), 1.0)
+    for name, n in (("vf1", 256), ("vf", NV), ("vf8", NV)):
+        fill(V(name, 0, 2) if name != "vf1" else col(name, 1), 0.0)
+        fill(col(name, n + 2), -128.0 if name == "vf1" else 0.0)
+        fill(col(name, n + 3), -0.25)
+        fill(V(name, n + 5, n + 36), 0.0)
+        act(col(name, n + 20), col("cs", 15))
+        if name == "vf":
+            lin(col(name, n + 4), col("cs", 14), 1.0, col("cs", 16))
+        else:
+            act(col(name, n + 4), col("cs", 14))
+    fill(V("fgt", 32, 64), 0.0)
+    fill(V("mgt"), 1.0)
+    ts(col("mgt", 32), H, -1.0, A.mult, 1.0, A.add)
+    ts(col("mgt", 32), col("mgt", 32), DOWN, A.max)
+    ts(col("mgt", 48), H, UP, A.mult, 1.0, A.max)
+    fill(V("mge", 0, 32), 1.0)
+    ts(col("cs", 17), RR, 1.0, A.add)
+    ts(V("mge", 32, 64), V("c32"), col("cs", 17), A.is_equal, UP, A.mult)
+    ts(V("mge", 32, 64), V("mge", 32, 64), 1.0, A.max)
+    fill(col("mge", 32), DOWN)
+    copy(col("mge", 48), H)
+    fill(V("h0", 64, 256), 0.0)
+    fill(V("h0", 64, 160, 3), 1.0)
+    ts(V("h1", 0, 32), V("c32"), RR, A.is_ge, 8192.0, A.mult)
+    ts(V("h1", 0, 32), V("h1", 0, 32), -256.0, A.add)
+    fill(V("h1", 32, 256), 8192.0)
+    fill(col("h1", 63), 0.0)
+    fill(V("j0", 0, 96, 3), 0.0)
+    fill(V("j0", 1, 96, 3), -1.0)
+    ts(col("cs", 18), J, -32.0, A.mult, -257.0, A.add)
+    lin(V("j0", 2, 96, 3), V("c32"), -1.0, col("cs", 18))
+    iota(V("c16"), [[0, 16], [1, 16]])
+    ts(col("cs", 19), J, 1.0, A.add)
+    ts(V("k1a"), V("c16"), J, A.not_equal)
+    for c in range(2):
+        a, b = 128 * c, 128 * c + 128
+        ts(V("k1b", a, b), V("c16", a, b), col("cs", 19), A.is_equal, 2.0 ** 48, A.mult)
+    for c in range(4):
+        a, b = 64 * c, 64 * c + 64
+        tt(V("k1", a, b), V("k1a", a, b), V("k1b", a, b), A.max)
+    ts(V("k2"), V("c16"), J, A.is_equal, 1024.0, A.mult)
+    ts(col("cs", 20), J, 15.0, A.is_equal, 2.0 ** -48, A.max)
+    act(col("cs", 21), col("cs", 20), ACT.Copy, 512.0)
 
-    def early0():
-        ts(V("xx", 0, 32), V("same"), THR1, A.mult)
-        ts(V("tmp", 48, 64), V("c16", 0, 16), J, A.is_lt, -0.5, A.mult)
-        fill(col("dz", NV + 1), 0.5)
-        fill(col("dz2", 0), 0.5)
-        ts(col("vf1", 1), H, -1024.0 * HUGE, A.mult)
-        turn(V("rows"), V("xx"))
-        ts(V("tmp", 48, 64), V("tmp", 48, 64), 1.0, A.add)
+    fill(V("ones", 0, 258), 0.5)
+    fill(V("ones", 258, 516), 0.5)
+    add("g", lambda: g.affine_select(T.et[:], T.ones[:], [[-1, 516]], A.is_equal, 0.0, 3, 4), [V("ones")], [V("et")],
+        170 + 2 * CY * 516)
 
-    def early1():
-        fill(col("dz", NV + 2), -HUGE)
-        fill(col("dz2", NV + 2), -HUGE)
-        ts(V("xx", 0, 32), V("oth"), 64.0 * HUGE, A.mult)
-        ts(V("t1"), V("rows", 0, 32), col("cs", 8), A.mult)
-        ts(col("sm", 0), J, 0.0, A.is_equal, 512.0 * HUGE, A.mult)
-        fill(col("vf", NV + 1), -0.25)
-        fill(col("vf", NV), 0.0)
-        product(col("cs", 9), V("tmp", 48, 64))
-        ts(V("tmp", 0, 32), V("oth"), 65536.0, A.mult)
-        ts(col("cs", 10), J, 1.0 / 16, A.mult, 1.0, A.add)
-
-    def early():
-        ts(col("vf", NV + 2), col("vf1", 1), col("sm", 0), A.add)
-        tt(V("t1"), V("t1"), V("xx", 0, 32), A.add)
-        ts(V("l2t"), V("rows", 32, 64), col("cs", 9), A.mult)
-        ts(V("rows", 0, 32), V("oth"), 2.0 ** 25, A.mult, J, A.subtract)
-        ts(V("tmp", 32, 64), V("c16", 0, 32), 7.0, A.min, J, A.add)
-        tt(V("l2t"), V("l2t"), V("tmp", 0, 32), A.add)
-        ts(col("cs", 11), col("js", 4), -1.0, A.mult, 2.0 ** -23, A.add)
-        tt(V("tmp", 32, 64), V("tmp", 32, 64), V("rows", 0, 32), A.add)
-        tt(V("rows", 0, 32), V("rows", 0, 32), V("c16", 0, 32), A.add)
-        ts(V("t2"), V("l2t"), col("cs", 10), A.mult)
-
-    def early2():
-        for k in range(5):
-            ts(V("gg", 32 * k, 32 * k + 32), V("rows", 0, 32), 2.0 ** (-4 - 4 * k), A.mult, col("js", k), A.add)
-        ts(V("gg", 160, 192), V("tmp", 32, 64), 2.0 ** -23, A.mult, col("cs", 11), A.add)
-
-    small = [
-        lambda: (ts(col("fl", 64), J, -16.0, A.mult, -0.5, A.add),
-                 ts(V("tmp", 0, 32), V("c16", 0, 32), J, A.is_gt),
-                 ts(col("sm", 3), J, 8.0, A.mult, 8.5, A.add)),
-        lambda: (tt(V("tmp", 32, 64), V("tmp", 0, 32), V("same"), A.mult),
-                 ts(col("cs", 6), J, 16.0, A.mult, 16.5 - 8192.0 - 65536.0, A.add),
-                 ts(KO, col("sm", 3), J, A.mult, -1672.0, A.add)),
-        lambda: (tt(V("mk", 0, 32), V("same"), V("tmp", 32, 64), A.subtract),
-                 ts(V("mk", 32, 64), V("tmp", 32, 64), 65536.0, A.mult, col("cs", 6), A.add),
-                 ts(col("cs", 7), KO, -1.0, A.mult, 256.0, A.add)),
-        lambda: (fill(V("ll", 0, 31), 8192.0), fill(V("keep", 0, 33), 1.0), fill(V("keep", 34, 66), 1.0), fill(col("keep", 33), 0.0)),
-    ]
-
-    def late_constants():
-        lin(V("k4"), V("ex"), -BIG, col("cs", 5), ACT.Relu)
-        act(col("fl", 97), col("fl", 64), ACT.Copy)
-
-    def third(c):
-        act(V("z3", 1536 * c + 2, 1536 * c + 1536, 3), V("ones"), ACT.Copy)
-
-    iota(V("em"), [[256, 32], [8192, 16]], -65536)
-    for b in range(4):
-        o = V("et", 512 * b, 512 * b + 512)
-        add("g", lambda o=o, b=b: g.affine_select(ap(o), T.ones[:], [[-1, 512]], A.is_equal, 0.0, b, 4), [V("ones")], [o])
-
-    def send(t):
+    sent = 0
+    for t in range(1, R + 1):
         dst = T.cores[(rank - t) % N]
         rid, pid = topo.addr(dst)[:2]
         m = topo.mask(core, dst)
-        arr = T.sem["arr%d" % t]
-        add("g", lambda: g.remote_dma(T["wl%d" % t][:].bitcast(dt.uint8), T.wo[:].bitcast(dt.uint8), arr, T.sem.sent, pid, rid, m),
-            [V("wo")], [], "remote")
-        add("g", lambda: g.remote_dma(T["wls%d" % t][:], T.wos[:], arr, T.sem.sent, pid, rid, m), [V("wos")], [], "remote")
-        return 2 * len(topo.engines(core, dst))
+        for o, i, cast in (("wl%d" % t, "wo", True), ("wls%d" % t, "wos", False)):
+            def send(o=o, i=i, cast=cast, t=t, pid=pid, rid=rid, m=m):
+                a, b = (T[o][:].bitcast(dt.uint8), T[i][:].bitcast(dt.uint8)) if cast else (T[o][:], T[i][:])
+                return g.remote_dma(a, b, T.sem["arr%d" % t], T.sem.sent, pid, rid, m)
+            add("g", send, [V(i)], [V(o)], 1000, "remote", (), 7000)
+        sent += 2 * len(topo.engines(core, dst))
 
-    sent = send(1)
-    iota(V("phm"), [[12, 16], [1, 2], [192, 16]])
-    iota(V("zi2", 1, 768, 3), [[1, 256]], C)
-    sent += send(2)
-    iota(V("zi3", 1, 768, 3), [[1, 256]], C + K)
+    iota(V("ic"), [[1, 256]])
+    iota(V("phm"), [[1, 32], [32, 16]], -256)
+    iota(V("ia2", 1, 512, 2), [[1, 256]], C)
+    iota(V("ib2", 0, 512, 2), [[1, 256]], C)
+    iota(V("ia3", 1, 512, 2), [[1, 256]], C + K)
+    iota(V("ib3", 0, 512, 2), [[1, 256]], C + K)
     iota(V("elb", 1, 512, 2), [[1, 256]], C + 2 * K)
     iota(V("elb", 512, 1024, 2), [[1, 256]], C + 2 * K)
-    sent += send(3)
 
-    act(V("g1", 0, 256), (V("ic"), V("ebu", 0, 16)), ACT.Copy, 2.0 ** -8)
     quant("uc", "usc", 0, 128, V("ut"))
     add("v", lambda: g.vector.tensor_copy(T.upc[:].bitcast(dt.uint32), T.uc[:].bitcast(dt.uint32).indirect(T.uo[:])),
-        [V("uc"), V("uo")], [V("upc")])
-    add("s", lambda: g.scalar.activation(T.ups[:], T.usc[:].indirect(T.uo[:]), ACT.Copy), [V("usc"), V("uo")], [V("ups")])
-    act(V("g1", 256, 512), (V("ic"), V("ebu", 16, 32)), ACT.Copy, 2.0 ** -8)
-    quant("tc", "tsc", 0, 128, V("xt", 0, 512))
-    quant("tc", "tsc", 128, 256, V("xt", 512, 1024))
+        [V("uc"), V("uo")], [V("upc")], 50 + 128 * GATHER * CY)
+    add("s", lambda: g.scalar.activation(T.ups[:], T.usc[:].indirect(T.uo[:]), ACT.Copy), [V("usc"), V("uo")], [V("ups")],
+        65 + 128 * GATHER * CY)
+    for h in range(2):
+        quant("tc", "tsc", 128 * h, 128 * h + 128, V("xt", 512 * h, 512 * h + 512))
+        mm(4 * h, "upc", "ups", 0, "tc", "tsc", 128 * h, 128 * h + 128)
+        move("sv"[h], V("ptab", 128 * h, 128 * h + 128), bank(4 * h, 0, 128))
     copy(V("eau"), V("eai"))
-    mm(0, "upc", "ups", 0, "tc", "tsc", 0, 256)
-    copy(V("prm"), V("e1", 0, 32))
-    early0()
-    copy(V("ptab"), bank(0))
+    copy(V("ebu"), V("ebi"))
+    for c in range(4):
+        move("sssv"[c], V("pa", 128 * c, 128 * c + 128), (V("ptab"), V("eau", 8 * c, 8 * c + 8)))
+    for c in range(4):
+        tt(V("dd", 128 * c, 128 * c + 128), (V("ptab"), V("ebu", 8 * c, 8 * c + 8)), V("pa", 128 * c, 128 * c + 128), A.subtract)
     store_codes("y", 0, 256)
     store_scales("yyyy", 0, 256)
-    for h in range(2):
-        act(V("pa", 256 * h, 256 * h + 256), (V("ptab"), V("eau", 16 * h, 16 * h + 16)), ACT.Copy)
-    tt(V("g2", 0, 256), (V("ic"), V("eau", 0, 16)), V("g1", 0, 256), A.add)
-    early1()
-    for h in range(2):
-        tt(V("dd", 256 * h, 256 * h + 256), (V("ptab"), V("ebu", 16 * h, 16 * h + 16)), V("pa", 256 * h, 256 * h + 256), A.subtract)
-    act(V("ss", 0, 256), V("dd", 0, 256), ACT.Abs)
-    count(col("cnt", 8), V("ss", 0, 256), THR1)
-    act(V("ss", 256, 512), V("dd", 256, 512), ACT.Abs)
-    early()
+
+    ts(V("xl", 32, 64), V("ebi"), 2.0 ** -9, A.mult, 1.0, A.add)
+    for s in range(2):
+        tt(V("xl", 16 * s, 16 * s + 16), V("eai", s, 32, 2), V("xl", 32 + s, 64, 2), A.add)
+        dma("y", lambda s=s: T.x0[0:128:16, 256 * s:256 * s + 256], lambda s=s: T.xl[:, 16 * s:16 * s + 16],
+            [V("xl", 16 * s, 16 * s + 16)], [V("x0", 256 * s, 256 * s + 256)], "row%d" % s)
+    for j in range(16):
+        dma("y", lambda j=j: T.xr[j:128:16, :], lambda: T.x0[0:128:16, :], [V("x0")], [V("xr", j, 512, 16)], "rows")
 
     DB = [1, 2, 3, 5]
+    for b in range(4):
+        quant("ec", "esc", 128 * b, 128 * b + 128, V("et", 3 - b, 515 - b))
+    quant("vc", "vsc", 0, 128, V("vt"))
+
+    def unpack(n):
+        for b in range(4):
+            mm(DB[b], "ec", "esc", 128 * b, "tc", "tsc", n, n + 256)
+        mm(6, "vc", "vsc", 0, "tc", "tsc", n, n + 256)
+
+    unpack(0)
+
     for t in range(1, R + 1):
         n = C + (t - 1) * K
-        oa, ob = 64 * (t - 1), 64 * (t - 1)
-        lo = 16 * (t - 1)
+        sd = V("sd", 32 * t - 32, 32 * t)
+        li = "l%d" % t
 
         def th(k):
             return col("th", 32 * k - 1)
 
         LO2 = col("th", 287)
 
-        def unpack_first():
-            quant("vc", "vsc", 0, 128, V("vt"))
-            for b in range(4):
-                mm(DB[b], "ec", "esc", 128 * b, "tc", "tsc", 0, 256)
-            mm(6, "vc", "vsc", 0, "tc", "tsc", 0, 256)
+        act(V("ss", 0, 256), V("dd", 0, 256), ACT.Abs)
+        count(col("cnt", 8), V("ss", 0, 256), THR1)
+        copy(col("vf1", 0), col("cnt", 8))
+        count(col("cnt", 0), V("dd", 256, 512), THR1)
+        ts(V("vf1", 2, 258), V("dd", 256, 512), NTH, A.is_gt, -0.5, A.add)
+        act(V("ss", 256, 512), V("dd", 256, 512), ACT.Abs)
+        dma("y", lambda t=t: T.sd[:, 32 * t - 32:32 * t], lambda: T.ss[0:128:16, :], [V("ss")], [sd], "sd%d" % t)
 
-        spread = [lambda: (copy(V("sx", 0, 16), V("trs", 0, 512, 32)), copy(V("sx", 16, 32), V("trs", 16, 512, 32))),
-                  lambda: turn(V("sd"), V("sx"))]
-        if t == 1:
-            work = ([early2]
-                    + [lambda c=c: tt(V("g2", c, c + 128), (V("ic"), V("eau", c // 16, c // 16 + 8)), V("g1", c, c + 128), A.add)
-                       for c in (256, 384)]
-                    + [lambda a=a, b=b: turn(V("trs", a, b), V("ss", a, b)) for a, b in ((0, 160), (160, 352), (352, 512))]
-                    + small
-                    + [lambda c=c: quant("ec", "esc", 128 * c, 128 * c + 128, V("et", 512 * c, 512 * c + 512)) for c in range(4)]
-                    + [unpack_first]
-                    + [lambda c=c: tt(V("vm", 128 * c, 128 * c + 128), (V("g2"), V("prm", 8 * c, 8 * c + 8)),
-                                      V("em", 128 * c, 128 * c + 128), A.add) for c in range(4)] + spread)
-            gaps = {1: work[0:2]}
-            for k in range(2, 9):
-                gaps[k] = work[3 * k - 4:3 * k - 1]
-        else:
-            def both(b, e, h):
-                a = 1536 * h + 3 * b
-                tt(V("z3", a + e, 1536 * h + 1536, 12), V("z%d" % t, a + 2 * e, 1536 * h + 1536, 12),
-                   V("ps", 512 * DB[b] + 128 * h, 512 * DB[b] + 128 * h + 128), A.add)
-
-            w = [lambda b=b, e=e, h=h: both(b, e, h) for e in range(2) for h in range(2) for b in range(4)]
-            gaps = {2: list(spread), 3: w[0:3], 4: w[3:6], 5: w[6:9], 6: w[9:12], 7: w[12:15], 8: w[15:16]}
-
-        def old(e, c):
-            o = "ob" if e else "oa"
-            act(V("z%d" % t, 768 * c + 2 * e, 768 * c + 768, 3), (V("z%d" % (t - 1)), V(o, oa - 64 + 16 * c, oa - 48 + 16 * c)), ACT.Copy)
-
-        def idle(k):
-            if t == 1 and k == 5:
-                late_constants()
-            if t == 1 and k in (6, 7):
-                third(k - 6)
-            if t == 3 and k < 3:
-                old(0, 2 * k - 2)
-                old(0, 2 * k - 1)
-            if t > 1 and 3 <= k <= 6:
-                old(1, k - 3)
-            if k == 3:
-                act(col("sm", 5), LO2, ACT.Copy, -1.0)
-            if k == (4 if t == 1 else 7):
-                lin(V("sp"), V("ss"), 1.0, col("sm", 5), ACT.Identity)
-
-        def gap(k):
-            if gaps.get(k):
-                gaps[k].pop(0)()
-
-        ts(col("vf1", 0), col("cnt", 8), 0.5, A.mult, -0.25, A.add)
         for k in range(1, 9):
             thr = THR1 if k == 1 else th(k - 1)
             cnt = col("cnt", k - 1)
             src = "sp" if k == 8 else "ss"
-            row = V("t1") if k == 1 else V("row")
+            row = V("t1") if k == 1 else V("row", 32 * k - 32, 32 * k)
             if k == 1:
-                count(cnt, V("ss", 256, 512), thr)
-                idle(k)
-                if t > 1:
-                    turn(V("trs", 0, 256), V("ss", 0, 256))
-                    turn(V("trs", 256, 512), V("ss", 256, 512))
-                scan(V("vo", NV + 1), V("dz", NV + 1), V("vf1"), cnt, A.mult, A.add)
+                scan(V("vo", 0, 292), V("dz" if NV == 256 else "dz1"), V("vf1"), cnt, A.mult, A.add)
+                turn(V("tr"), V("vo", 260, 292))
             else:
+                vf = "vf8" if k == 8 else "vf"
                 count(cnt, V(src, 0, 512 - NV), thr)
-                idle(k)
-                ts(V("vf", 0, NV), V(src, 512 - NV, 512), thr, A.is_lt, -0.5, A.add)
+                ts(V(vf, 2, NV + 2), V(src, 512 - NV, 512), thr, A.is_lt, -0.5, A.add)
                 if k == 2:
                     ts(row, V("t2"), thr, A.mult)
-                    ts(V("row2"), V("l2t"), thr, A.mult)
+                    ts(V("row", 0, 32), V("l2t"), thr, A.mult)
                 elif k == 3:
-                    ts(V("gl"), V("gg"), LO2, A.mult)
+                    act(col("sm", 5), LO2, ACT.Copy, -1.0)
+                    ts(V("gl", 0, 32), V("gg", 0, 32), LO2, A.mult)
+                    ts(row, V("gl", 0, 32), thr, A.add)
+                    act(V("gl", 32, 193), V("gg", 32, 193), ACT.Copy, LO2)
+                    lin(V("sp", 0, 256), V("ss", 0, 256), 1.0, col("sm", 5))
+                    lin(V("sp", 256, 512), V("ss", 256, 512), 1.0, col("sm", 5))
                 elif k == 7:
                     ts(col("sm", 4), thr, LO2, A.subtract)
+                    ts(row, V("gl", 128, 160), col("sm", 4), A.add)
                 elif k == 8:
                     ts(row, V("gl", 160, 192), thr, A.add, LO2, A.add)
                     ts(col("sm", 6), thr, col("gl", 192), A.subtract, LO2, A.add)
                 else:
                     ts(row, V("gl", 32 * k - 96, 32 * k - 64), thr, A.add)
-                scan(V("vo", 0, NV + 34), V("dz2"), V("vf"), cnt, A.mult, A.add)
-                if k == 3 or k == 7:
-                    ts(row, V("gl", 32 * k - 96, 32 * k - 64), thr if k == 3 else col("sm", 4), A.add)
-            gap(k)
-            turn(V("tr"), V("vo", NV + 2))
-            gap(k)
+                scan(V("vo", 0, NF), V("dz"), V(vf), cnt, A.mult, A.add)
+                turn(V("tr"), V("vo", NV + 4, NF))
             scan(V("th", 32 * k - 32, 32 * k), V("tr"), row, col("sm", 6) if k == 8 else 0.0, A.max, A.min)
             if k == 2:
-                scan(V("th", 256, 288), V("tr"), V("row2"), 0.0, A.max, A.min)
-            if k == 7:
-                copy(col("vf", NV + 2), col("vf1", 1))
-            if k == 8 and t < R:
-                ts(col("vf", NV + 2), col("vf1", 1), col("sm", 0), A.add)
-            gap(k)
+                scan(V("th", 256, 288), V("tr"), V("row", 0, 32), 0.0, A.max, A.min)
         TT = th(8)
 
-        if t > 1:
-            for h in range(2):
-                act(V("zp%d" % t, 384 * h + 1, 384 * h + 384, 3), bank(4 * h, 128), ACT.Copy)
-        for b in range(4 if t < R else 0):
-            act(V("z1", b, 1024, 4) if t == 1 else V("z2", 3 * b + 1, 3072, 12), bank(DB[b]), ACT.Copy)
-        if t > 1:
-            iw = V("ic") if t == 2 else V("zi2")
-            act(V("zi%d" % t, 0, 768, 3), (iw, V("la", lo - 16, lo)), ACT.Copy)
-            act(V("zi%d" % t, 2, 768, 3), (iw, V("lb", lo - 16, lo)), ACT.Copy)
-        act(V("ysb", n - 256, n), bank(6), ACT.Copy)
+        if t == 1:
+            for b in range(4):
+                act(V("z1", 256 * b, 256 * b + 256), bank(DB[b]))
+        else:
+            for e in range(2):
+                for b in range(4):
+                    if t == 2:
+                        old = V("eb2" if e else "ea2", 512 * b + e, 512 * b + 512, 2)
+                        if e:
+                            act(old, (V("z1", 256 * b, 256 * b + 256), V("lb")))
+                    else:
+                        old = V("b3" if e else "a3", 256 * b, 256 * b + 256)
+                        act(old, (V("eb2" if e else "ea2", 512 * b, 512 * b + 512), V("l2")))
+                    for h in range(2):
+                        st = old[3]
+                        tt(V("mid", 512 * b + 256 * h + e, 512 * b + 256 * h + 256, 2),
+                           V(old[0], old[1] + 128 * st * h, old[1] + 128 * st * h + 127 * st + 1, st), bank(DB[b], 128 * h, 128), A.add)
+            if t == 2:
+                for h in range(2):
+                    act(V("pa2", 256 * h + 1, 256 * h + 256, 2), bank(4 * h, 0, 128))
+                    act(V("pb2", 256 * h, 256 * h + 256, 2), bank(4 * h, 0, 128))
+                for b in range(4):
+                    act(V("ea2", 512 * b + 1, 512 * b + 512, 2), bank(DB[b]))
+                    act(V("eb2", 512 * b, 512 * b + 512, 2), bank(DB[b]))
+                act(V("ia2", 0, 512, 2), (V("ic"), V("la")))
+                act(V("ib2", 1, 512, 2), (V("ic"), V("lb")))
+            else:
+                act(V("ia3", 0, 512, 2), (V("ia2"), V("l2")))
+                act(V("ib3", 1, 512, 2), (V("ib2"), V("l2")))
+        act(V("ysb", n - 256, n), bank(6))
         store_y("y", n - 256, n)
 
-        ts(V("fl", 65, 97), V("sd"), TT, A.is_ge, -0.5, A.add)
-        ts(V("fl", 98, 130), V("sd"), TT, A.is_gt, -0.5, A.add)
-        scan(V("ll", 31, 97), V("keep"), V("fl", 64, 130), 8192.0, A.mult, A.add)
-        ts(V("xx", 0, 32), V("mk", 0, 32), col("ll", 96), A.mult)
-        ts(V("xx", 32, 64), V("mk", 32, 64), col("ll", 63), A.add, 0.0, A.max)
-        turn(V("fl", 0, 64), V("xx"))
-        scan(V("qq"), V("fl", 0, 97), V("ll"), col("cs", 7), A.add, A.min)
-        tt(V("zz"), V("qq", 64, 97), V("e1"), A.mult)
-        tt(V("yy"), V("zz", 1, 33), V("zz", 0, 32), A.subtract)
-        ts(V("so"), V("yy"), col("qq", 31), A.subtract, 256.0, A.add)
-        copy((V("rr"), V("so")), V("vm" if t == 1 else "phm"))
-        scan(V("ex"), V("k4"), V("rr", 256, 512), 0.0, A.add, A.min)
-        exv, ex2v = V("ex", 3, 256, 4), V("ex2", 15, 256, 16)
+        ts(V("fgt", 0, 32), sd, TT, A.is_gt)
+        ts(V("h0", 65, 160, 3), sd, TT, A.is_ge, -1.0, A.add)
+        scan(V("h1", 65, 256, 3), V("mgt"), V("fgt"), 0.0, A.mult, A.add)
+        scan(V("oge"), V("mge"), V("h0", 65, 256, 3), 32.0, A.mult, A.add)
+        turn(V("h0", 0, 32), V("h1", 161, 256, 3))
+        turn(V("h0", 32, 64), V("oge", 32, 64))
+        scan(V("qq"), V("h0", 0, 160), V("h1", 0, 160), -256.0, A.add, A.min)
+        scan(V("yy"), V("j0"), V("qq", 64, 160), 0.0, A.mult, A.add)
+        ts(V("so"), V("yy", 2, 96, 3), col("qq", 31), A.subtract, -1.0, A.add)
         if t == 1:
-            ts(V("wi"), exv, 256.0, A.mult)
-            ts(V("wa"), V("wi"), 8, A.arith_shift_right, 255, A.bitwise_and)
-            ts(V("wb"), V("wi"), 255, A.bitwise_and)
-            ts(V("oa", 0, 64), V("wa"), 4.0, A.mult, B, A.add)
-            ts(V("ob", 0, 64), V("wb"), 4.0, A.mult, B, A.add)
-            for c in range(4):
-                act(V("z2", 768 * c, 768 * c + 768, 3), (V("z1"), V("oa", 16 * c, 16 * c + 16)), ACT.Copy)
+            copy((V("r1"), V("so")), V("xr"))
+            scan(V("ex1"), V("k1"), V("r1", 0, 256), 0.0, A.mult, A.add)
+            ts(V("la"), V("ex1", 15, 256, 16), col("cs", 20), A.mult, -1.0, A.add)
+            ts(V("wi"), V("ex1", 15, 256, 16), col("cs", 21), A.mult)
+            ts(V("wb"), V("wi"), 511, A.bitwise_and)
+            copy(V("lb"), V("wb"))
         else:
-            ts(V("oa", oa, oa + 64), exv, B3, A.add)
-        scan(V("ex2"), V("k16"), V("rr", 256, 512), 0.0, A.add, A.min)
+            copy((V("r2"), V("so")), V("phm"))
+            scan(V("ex2"), V("k2"), V("r2", 0, 256), 0.0, A.add, A.min)
+            ts(V(li), V("ex2", 15, 256, 16), 256.0, A.add)
 
-        def lists_a():
-            if t == 1:
-                ts(V("sa"), V("si"), 8, A.arith_shift_right, 255, A.bitwise_and)
-                ts(V("sbi"), V("si"), 255, A.bitwise_and)
-            else:
-                copy(V("sa"), V("sf"))
-
-        def lists_b():
-            copy(V("la", lo, lo + 16), V("sa"))
-            if t == 1:
-                copy(V("lb", lo, lo + 16), V("sbi"))
-            else:
-                ts(V("lb", lo, lo + 16), V("sa"), 1.0, A.add)
-
-        def mid(c):
-            tt(V("mt", 256 * c, 256 * c + 256), (V("z1"), V("ob", 16 * c, 16 * c + 16)), V("z2", 768 * c, 768 * c + 768, 3), A.add)
-
-        def pick(c, q):
-            o, i = V("mt", 256 * c, 256 * c + 256), (V("z3"), V("oa", oa + 16 * c, oa + 16 * c + 16))
-            if q == "s":
-                act(o, i, ACT.Copy)
-            else:
-                copy(o, i)
-
-        def layer(h):
+        for h in range(2):
+            for b in range(4):
+                o = V("mt", 512 * h + b, 512 * h + 512, 4)
+                if t == 1:
+                    w = V("z1", 256 * b, 256 * b + 256)
+                    a = V("ea2", 512 * b + 256 * h, 512 * b + 256 * h + 256, 2)
+                    act(a, (w, V("la", 8 * h, 8 * h + 8)))
+                    tt(o, (w, V("lb", 8 * h, 8 * h + 8)), a, A.add)
+                else:
+                    move(PICK[h][b], o, (V("mid", 512 * b, 512 * b + 512), V(li, 8 * h, 8 * h + 8)))
             quant("mc", "msc", 128 * h, 128 * h + 128, V("mt", 512 * h, 512 * h + 512))
+        ends = {}
+        for h in range(2):
+            for e in range(2):
+                if t == 1:
+                    w, a = V("ptab"), V("lb" if e else "la", 8 * h, 8 * h + 8)
+                    o = V("pb2" if e else "pa2", 256 * h + e, 256 * h + 256, 2)
+                elif t == 2:
+                    w, a = V("pb2" if e else "pa2"), V(li, 8 * h, 8 * h + 8)
+                    o = V("pb3" if e else "pa3", 128 * h, 128 * h + 128)
+                else:
+                    w, a = V("ib3" if e else "ia3"), V(li, 8 * h, 8 * h + 8)
+                    o = V("elb", 513 * e + 256 * h, 512 * e + 256 * h + 256, 2)
+                move(ENDS[t - 1][2 * h + e], o, (w, a))
+                ends[h, e] = o
+        for h in range(2):
             for b in range(4):
                 src = T.cores[(rank + t) % N]
                 extra = (("arr%d" % t, 2 * len(topo.engines(src, core))),) if h == 0 and b == 0 else ()
                 mm(4 * h + b, "wl%d" % t, "wls%d" % t, 128 * b, "mc", "msc", 128 * h, 128 * h + 128, extra)
-
-        def scale(h, b, q):
-            out = V("ft", 512 * h + b, 512 * h + 512, 4)
-            if q == "s":
-                act(out, bank(4 * h + b, 128), ACT.Copy, 0.03125)
-            else:
-                ts(out, bank(4 * h + b, 128), 0.03125, A.mult)
-
-        def end(h, e, q):
-            a = V("lb" if e else "la", lo + 8 * h, lo + 8 * h + 8)
-            if t < R:
-                w, o = V("ptab") if t == 1 else V("zp%d" % t), V("zp%d" % (t + 1), 384 * h + 2 * e, 384 * h + 384, 3)
-            else:
-                w, o = V("zi3"), V("elb", 513 * e + 256 * h, 512 * e + 256 * h + 256, 2)
-            if q == "s":
-                act(o, (w, a), ACT.Copy)
-            else:
-                copy(o, (w, a))
-
-        def fresh(h):
+            for b in range(4):
+                out = V("ft", 512 * h + b, 512 * h + 512, 4)
+                if SCALE[t - 1][h][b] == "s":
+                    act(out, bank(4 * h + b, 0, 128), ACT.Copy, 0.03125)
+                else:
+                    ts(out, bank(4 * h + b, 0, 128), 0.03125, A.mult)
             a = n + 128 * h
             quant("tc", "tsc", a, a + 128, V("ft", 512 * h, 512 * h + 512))
             mm(4 * h, "upc" if t < R else "vc", "ups" if t < R else "vsc", 0, "tc", "tsc", a, a + 128)
-
-        def diffs(h):
-            o = "zp%d" % (t + 1)
-            tt(V("dd", 256 * h, 256 * h + 256, 2), V(o, 384 * h, 384 * h + 384, 3), bank(4 * h, 128), A.subtract)
-            tt(V("dd", 256 * h + 1, 256 * h + 256, 2), V(o, 384 * h + 2, 384 * h + 384, 3), bank(4 * h, 128), A.subtract)
-
-        if t == 1:
-            ts(V("si"), ex2v, 256.0, A.mult)
-            lists_a()
-            mid(0)
-            mid(1)
-            lists_b()
-            layer(0)
-            mid(2)
-            for b in range(4):
-                scale(0, b, "s")
-            end(0, 0, "s")
-            end(0, 1, "s")
-            mid(3)
-            layer(1)
-        else:
-            pick(0, "s")
-            pick(1, "v")
-            pick(2, "s")
-            ts(V("sf"), ex2v, 0.25, A.mult, 0.4, A.add)
-            layer(0)
-            pick(3, "v")
-            lists_a()
-            layer(1)
-            lists_b()
-            for b in range(4):
-                scale(0, b, "s")
-            end(0, 0, "s")
-            end(0, 1, "v")
-        fresh(0)
+            if t < R:
+                for e in range(2):
+                    tt(V("dd", 256 * h + e, 256 * h + 256, 2), ends[h, e], bank(4 * h, 0, 128), A.subtract)
+            else:
+                copy(V("ysb", a, a + 128), bank(4 * h, 0, 128))
+                store_y("y", a, a + 128)
+                store_codes("y", a, a + 128)
         if t < R:
-            end(1, 0, "s")
-            scale(1, 0, "v")
-            scale(1, 1, "s")
-            scale(1, 2, "v")
-            scale(1, 3, "s")
-            diffs(0)
-            fresh(1)
-            act(V("ss", 0, 256), V("dd", 0, 256), ACT.Abs)
-            count(col("cnt", 8), V("ss", 0, 256), THR1)
-            end(1, 1, "v")
-            diffs(1)
-            if t == 2:
-                ts(V("ob", ob, ob + 64), exv, B3, A.add, 1.0, A.add)
-            act(V("ss", 256, 512, 2), V("dd", 256, 512, 2), ACT.Abs)
-            act(V("ss", 257, 512, 2), V("dd", 257, 512, 2), ACT.Abs)
-            for b in range(4):
-                mm(DB[b], "ec", "esc", 128 * b, "tc", "tsc", n, n + 256)
-            mm(6, "vc", "vsc", 0, "tc", "tsc", n, n + 256)
+            unpack(n)
             store_codes("y", n, n + 256)
             store_scales("yyyy", n, n + 256)
         else:
-            store_codes("y", n, n + 128)
-            scale(1, 0, "v")
-            scale(1, 1, "s")
-            scale(1, 2, "v")
-            scale(1, 3, "s")
-            end(1, 0, "s")
-            end(1, 1, "s")
-            store("s", lambda: T.el[:, :], lambda: T.elb[0:128:16, :], [V("elb")])
-            fresh(1)
-            copy(V("ysb", n, n + 128), bank(0, 128))
-            store_y("y", n, n + 128)
-            store_codes("y", n + 128, n + 256)
             store_scales("yyss", n, n + 256)
-            copy(V("ysb", n + 128, n + 256), bank(4, 128))
-            store_y("y", n + 128, n + 256)
+            store("s", lambda: T.el[:, :], lambda: T.elb[0:128:16, :], [V("elb")])
 
-    emit(T, queue, ops)
+    outs = emit(T, queue, ops)
     g.wait_ge(T.sem.sent, sent)
-    g.sync.wait_ge(T.sem.outy, outs["y"])
-    g.scalar.wait_ge(T.sem.outs, outs["s"])
+    g.sync.wait_ge(T.sem.outy, outs["outy"])
+    g.scalar.wait_ge(T.sem.outs, outs["outs"])
 
 
-def emit(T, queue, ops):
+PICK = ["vvss", "vvss"]
+ENDS = ["svsv", "svsv", "ssss"]
+SCALE = [["ssss", "ssvv"], ["ssvv", "ssvv"], ["ssvv", "ssvv"]]
+
+
+def depends(ops):
     def bits(a):
         if a[0] == "ps":
             return 1 << (a[1] // 512)
@@ -611,38 +527,115 @@ def emit(T, queue, ops):
             m |= 1 << c
         return m
 
-    seen, known, done, waits, needed = {}, {}, [], [], set()
-    for i, (q, call, reads, writes, sem, extra) in enumerate(ops):
-        deps = set()
-        touch = [(a[0], bits(a), False) for a in reads] + [(a[0], bits(a), True) for a in writes]
+    seen, deps = {}, []
+    for i, op in enumerate(ops):
+        d = set()
+        touch = [(a[0], bits(a), False) for a in op[2]] + [(a[0], bits(a), True) for a in op[3]]
         for name, m, w in touch:
             for j, m2, w2 in seen.get(name, []):
-                if m & m2 and (w or w2 or (name == "ps" and ops[j][0] != q)):
-                    deps.add(j)
+                if m & m2 and (w or w2 or (name == "ps" and ops[j][0] != op[0])):
+                    d.add(j)
+        deps.append(d)
+        for name, m, w in touch:
+            seen.setdefault(name, []).append((i, m, w))
+    return deps
+
+
+def arrange(ops, deps):
+    n = len(ops)
+    after = [[] for _ in range(n)]
+    for i in range(n):
+        for j in deps[i]:
+            after[j].append(i)
+    tail = [0.0] * n
+    for i in range(n - 1, -1, -1):
+        tail[i] = ops[i][7] + max([WAKE + tail[k] for k in after[i]] + [0.0])
+    best = None
+    for turn in range(6):
+        start, busy = [0.0] * n, {}
+        for i in sorted(range(n), key=lambda i: (-tail[i], i)):
+            t = max([start[j] + ops[j][7] + WAKE for j in deps[i]] + [0.0])
+            line = busy.setdefault(ops[i][0], [])
+            k = 0
+            for k in range(len(line) + 1):
+                if k == len(line) or t + ops[i][6] <= line[k][0] + 1e-6:
+                    break
+                t = max(t, line[k][1])
+            line.insert(k, (t, t + ops[i][6]))
+            start[i] = t
+        end = max(start[i] + ops[i][7] for i in range(n))
+        order = sorted(range(n), key=lambda i: (start[i], i))
+        if best is None or end < best[0] - 1e-6:
+            best = (end, order)
+        late, busy = [0.0] * n, {}
+        for i in sorted(range(n), key=lambda i: (-(start[i] + ops[i][7]), -i)):
+            t = max([late[k] + WAKE for k in after[i]] + [0.0]) + ops[i][7] - ops[i][6]
+            line = busy.setdefault(ops[i][0], [])
+            k = 0
+            for k in range(len(line) + 1):
+                if k == len(line) or t + ops[i][6] <= line[k][0] + 1e-6:
+                    break
+                t = max(t, line[k][1])
+            line.insert(k, (t, t + ops[i][6]))
+            late[i] = t + ops[i][6]
+        tail = late
+    return best[1]
+
+
+PLAN = []
+
+
+def emit(T, queue, ops):
+    deps = depends(ops)
+    if not PLAN:
+        PLAN.append(arrange(ops, deps))
+    order = PLAN[0]
+    at = {i: p for p, i in enumerate(order)}
+    total = {}
+    for op in ops:
+        if op[4] not in (None, "remote"):
+            total[op[4]] = total.get(op[4], 0) + 16
+    group = {}
+    for i, op in enumerate(ops):
+        if op[4] is not None:
+            group[op[4]] = group.get(op[4], 0) | 1 << i
+    known, done, waits, needed = {}, {}, {}, set()
+    for i in order:
+        q = ops[i][0]
         mine = []
-        for j in sorted(deps, reverse=True):
+        for j in sorted(deps[i], key=lambda j: -at[j]):
+            if ops[j][4] == "remote":
+                continue
             if not known.get(q, 0) >> j & 1:
                 mine.append(j)
                 needed.add(j)
-                known[q] = known.get(q, 0) | done[j]
-        waits.append(mine)
-        done.append(known.get(q, 0) | 1 << i)
-        for name, m, w in touch:
-            seen.setdefault(name, []).append((i, m, w))
-    used, token = {}, {}
-    for i, (q, call, reads, writes, sem, extra) in enumerate(ops):
-        for j in waits[i]:
+                known[q] = known.get(q, 0) | done[j] | group.get(ops[j][4], 0)
+        waits[i] = (mine, known.get(q, 0))
+        done[i] = known.get(q, 0) | 1 << i
+    token, last, used = {}, {}, {}
+    for i in order:
+        q, call, sem, extra = ops[i][0], ops[i][1], ops[i][4], ops[i][5]
+        for j in waits[i][0]:
             queue[q].wait_ge(T.sem[token[j][0]], token[j][1])
         for name, val in extra:
             queue[q].wait_ge(T.sem[name], val)
+        if sem is None and i in needed:
+            k = used.get(q, 0)
+            free = [c % POOL[q] for c in range(k, k + POOL[q])
+                    if (q, c % POOL[q]) not in last or waits[i][1] >> last[q, c % POOL[q]] & 1]
+            c = free[0] if free else k % POOL[q]
+            j = last.get((q, c))
+            if not free:
+                queue[q].wait_ge(T.sem[token[j][0]], token[j][1])
+            token[i] = (q + str(c), 1 if j is None else token[j][1] + 1)
+            last[q, c] = i
+            used[q] = c + 1
         ins = call()
         if sem == "remote":
             continue
         if sem is not None:
             ins.then_inc(T.sem[sem], 16)
-            token[i] = (sem, 16)
+            token[i] = (sem, total[sem])
         elif i in needed:
-            k = used.get(q, 0)
-            used[q] = k + 1
-            token[i] = (q + str(k % POOL[q]), k // POOL[q] + 1)
             ins.then_inc(T.sem[token[i][0]], 1)
+    return total

@@ -4,7 +4,10 @@ N, C, K, R = 8, 256, 256, 3
 X4, U8 = "float8_e4m3fn_x4", "uint8"
 F32, BF, I32, U16 = "float32", "bfloat16", "int32", "uint16"
 NV = 256
-NF = NV + 36
+NV2 = 288
+TAIL = 34
+W2 = 1398096
+W = {3: 82242, 4: 4838, 5: 285, 6: 17, 7: 1, 8: 0}
 
 
 def _sb(n, t):
@@ -24,21 +27,23 @@ SCRATCH = {
     "z1": _sb(1024, BF), "ea2": _sb(2048, BF), "eb2": _sb(2048, BF), "a3": _sb(1024, BF), "b3": _sb(1024, BF),
     "mid": _sb(2048, BF),
     "ptab": _sb(256, F32), "pa": _sb(512, F32), "dd": _sb(512, F32), "ss": _sb(512, F32), "sp": _sb(512, F32),
-    "junk": _sb(512, BF), "sd": _sb(32 * R, F32),
+    "junk": _sb(1024, BF), "sd": _sb(32 * R, F32),
     "pa2": _sb(512, F32), "pb2": _sb(512, F32), "pa3": _sb(256, F32), "pb3": _sb(256, F32),
     "ia2": _sb(512, F32), "ib2": _sb(512, F32), "ia3": _sb(512, F32), "ib3": _sb(512, F32), "elb": _sb(1024, F32),
-    "ysb": _sb(1024, F32), "xl": _sb(64, F32), "x0": _sb(512, F32), "xr": _sb(512, F32), "phm": _sb(512, BF),
-    "ic": _sb(256, F32), "r1": _sb(1024, F32), "r2": _sb(1024, BF), "ex1": _sb(256, F32), "ex2": _sb(256, BF),
-    "c16": _sb(256, BF), "k1": _sb(256, F32), "k1a": _sb(256, BF), "k1b": _sb(256, F32), "k2": _sb(256, BF),
-    "pi": _sb(8, I32), "pj": _sb(8, I32), "pf": _sb(8, F32), "ui": _sb(8, I32), "uo": _sb(8, U16),
-    "c32": _sb(32, F32), "cm": _sb(32, F32), "oth": _sb(32, F32), "tmp": _sb(128, F32), "cs": _sb(32, F32),
-    "xx": _sb(64, F32), "rows": _sb(64, F32), "tr": _sb(32, BF), "th": _sb(32 * 9, F32), "cnt": _sb(16, F32),
-    "sm": _sb(8, F32), "t1": _sb(32, F32), "t2": _sb(32, F32), "l2t": _sb(32, F32), "aa": _sb(32, F32),
-    "gg": _sb(193, F32), "gl": _sb(193, F32), "row": _sb(32 * 9, F32),
-    "vf1": _sb(292, BF), "vf": _sb(NF, BF), "vf8": _sb(NF, BF), "vo": _sb(max(NF, 292), BF), "dz": _sb(NF, BF),
-    "dz1": _sb(292, BF),
-    "fgt": _sb(64, F32), "mgt": _sb(64, F32), "mge": _sb(64, F32), "oge": _sb(64, F32),
-    "h0": _sb(256, F32), "h1": _sb(256, F32), "qq": _sb(160, F32), "j0": _sb(96, F32), "yy": _sb(96, F32),
+    "ysb": _sb(1024, F32), "xl": _sb(64, F32), "x0": _sb(512, F32), "xr": _sb(512, F32), "phm": _sb(256, BF),
+    "ic": _sb(256, F32), "r1": _sb(1024, F32), "r2": _sb(2560, BF), "ex1": _sb(256, F32), "ex2": _sb(256, BF),
+    "c16": _sb(128, BF), "k1": _sb(128, F32), "k2": _sb(128, BF),
+    "pw": _sb(544, F32), "pn": _sb(800, BF), "r3": _sb(2560, BF), "k3": _sb(258, BF), "fx": _sb(514, BF),
+    "pi": _sb(8, I32), "pj": _sb(8, I32), "pf": _sb(8, F32), "ui": _sb(16, I32), "uo": _sb(16, U16),
+    "c32": _sb(32, F32), "cm": _sb(32, F32), "oth": _sb(32, F32), "tmp": _sb(256, F32), "cs": _sb(32, F32),
+    "xx": _sb(64, F32), "rows": _sb(64, F32), "tr": _sb(64, BF), "th": _sb(64 * 10, F32), "cnt": _sb(16, F32),
+    "sm": _sb(8, F32), "t1": _sb(128, F32), "ef": _sb(96, F32), "e65": _sb(65, F32), "f65": _sb(65, F32),
+    "g65": _sb(65, F32), "fab": _sb(64, F32), "aa": _sb(33, F32),
+    "gg": _sb(33 * 5, F32), "gl": _sb(33, F32), "row": _sb(65 * 8, F32),
+    "v1": _sb(258 + TAIL, BF), "va": _sb(2 + NV2 + TAIL, BF), "vb": _sb(514 + TAIL, BF), "dz": _sb(514 + TAIL, BF),
+    "oa": _sb(2 + NV2 + TAIL, BF), "ob": _sb(514 + TAIL, BF),
+    "fgt": _sb(64, F32), "mgt": _sb(64, F32), "mge": _sb(64, BF), "oge": _sb(64, BF),
+    "h0": _sb(256, BF), "h1": _sb(256, BF), "qq": _sb(160, BF), "j0": _sb(96, F32), "yy": _sb(96, F32),
     "so": _sb(32, U16), "wi": _sb(16, I32), "wb": _sb(16, I32), "la": _sb(16, U16), "lb": _sb(16, U16),
     "l2": _sb(16, U16), "l3": _sb(16, U16),
     "ps": ("psum", [128, 4096], F32),
@@ -49,9 +54,10 @@ SEMAPHORES = ([q + str(i) for q in POOL for i in range(POOL[q])] + LOADS
               + ["arr1", "arr2", "arr3", "sent", "outy", "outs"])
 HUGE = 2.0 ** 84
 UP, DOWN = 2.0 ** 60, 2.0 ** -60
+STEP = 2.0 ** -23
 A = AluOpType
 ACT = ActivationFunctionType
-CY, WAKE, GATHER, SCATTER = 1.04, 150.0, 1.56, 3.8
+CY, WAKE, GATHER, SCATTER, SFIX, MM = 1.1, 200.0, 1.8, 3.8, 100, 1.2
 
 
 def rank_program(g, core, T, topo):
@@ -73,6 +79,9 @@ def rank_program(g, core, T, topo):
 
     def col(name, a):
         return V(name, a, a + 1)
+
+    def last(name, n):
+        return V(name, SCRATCH[name][1][1] - n)
 
     def flat(items):
         out = []
@@ -102,7 +111,7 @@ def rank_program(g, core, T, topo):
     def tt(out, a, b, op):
         k = 1 if "ps" in (a[0], b[0]) else 2
         add("v", lambda: g.vector.tensor_tensor(ap(out), ap(a), ap(b), op), [a, b], [out],
-            (50 if len(a) == 2 else 0) + max(64, k * size(a)) * CY)
+            50 + size(a) * GATHER * CY if len(a) == 2 else max(64, k * size(a)) * CY)
 
     def ts(out, a, s1, op0, s2=None, op1=None):
         if op1 is None:
@@ -120,16 +129,13 @@ def rank_program(g, core, T, topo):
     def turn(out, in_):
         add("v", lambda: g.vector.transpose(ap(out), ap(in_)), [in_], [out], vcost(in_, out))
 
-    def product(out, in_):
-        add("v", lambda: g.vector.tensor_reduce(ap(out), ap(in_), AxisListType.X, A.mult), [in_], [out], vcost(in_))
-
     def act(out, in_, func=ACT.Copy, scale=1.0):
         add("s", lambda: g.scalar.activation(ap(out), ap(in_), func, scale=ap(scale)), [in_, scale], [out],
-            65 + size(in_) * CY * (GATHER if len(in_) == 2 else 1))
+            65 + size(in_) * CY * GATHER if len(in_) == 2 else SFIX + size(in_) * CY)
 
     def lin(out, in_, scale, bias):
         add("s", lambda: g.scalar.activation(ap(out), ap(in_), ACT.Identity, bias=ap(bias), scale=ap(scale)), [in_, bias, scale], [out],
-            65 + size(in_) * CY)
+            SFIX + size(in_) * CY)
 
     def move(q, out, in_):
         if q == "s":
@@ -137,10 +143,10 @@ def rank_program(g, core, T, topo):
         else:
             copy(out, in_)
 
-    def count(cnt, in_, thr):
-        junk = V("junk", in_[1], in_[2])
+    def count(cnt, in_, thr, side=0):
+        junk = V("junk", 512 * side + in_[1], 512 * side + in_[2])
         add("s", lambda: g.scalar.activation(ap(junk), ap(in_), ACT.Sign, bias=ap(thr), scale=-1.0, accum_out=ap(cnt)),
-            [in_, thr], [junk, cnt], 85 + size(in_) * CY)
+            [in_, thr], [junk, cnt], SFIX + 20 + size(in_) * CY)
 
     def quant(codes, scales, a, b, in_):
         add("v", lambda: g.vector.quantize_mx(T[codes][:, a:b], T[scales][:, a:b], ap(in_)), [in_],
@@ -150,7 +156,7 @@ def rank_program(g, core, T, topo):
         out = V("ps", 512 * bank, 512 * bank + d - c)
         add("t", lambda: g.tensor.matmul_mx(ap(out), T[lc][:, a:a + 128], T[ls][:, a:a + 128], T[rc][:, c:d], T[rs][:, c:d],
                                             True, True),
-            [V(lc, a, a + 128), V(ls, a, a + 128), V(rc, c, d), V(rs, c, d)], [out], (d - c + 16) * 0.9, None, extra)
+            [V(lc, a, a + 128), V(ls, a, a + 128), V(rc, c, d), V(rs, c, d)], [out], (d - c + 16) * MM, None, extra)
 
     def bank(b, a=0, n=256):
         return V("ps", 512 * b + a, 512 * b + a + n)
@@ -163,6 +169,7 @@ def rank_program(g, core, T, topo):
                 130 + 2 * CY * size(out))
 
     def dma(q, out, in_, reads, writes, sem, late=2400):
+        late = late + (1500 if sem[:2] in ("ro", "sd") else 0)
         add(q, lambda: queue[q].dma_start(out(), in_()), reads, writes, 60, sem, (), late)
 
     def store(q, out, in_, reads):
@@ -179,7 +186,7 @@ def rank_program(g, core, T, topo):
         store(q, lambda: T.y[:, a:b], lambda: T.ysb[:, a:b], [V("ysb", a, b)])
 
     J, RR, H = col("pf", 0), col("pf", 1), col("cs", 0)
-    THR1, NTH, P2, P2N = col("cs", 1), col("cs", 2), col("cs", 3), col("cs", 4)
+    PA, PB, NA, NB = col("tmp", 47), col("cs", 2), col("cs", 3), col("cs", 4)
 
     dma("y", lambda: T.ut[:], lambda: T.u[:], [], [V("ut")], "ldu")
     dma("s", lambda: T.xt[:, 0:512], lambda: T.x[:, 0:512], [], [V("xt", 0, 512)], "ldx0")
@@ -191,62 +198,67 @@ def rank_program(g, core, T, topo):
     dma("y", lambda: T.vt[:], lambda: T.v[:], [V("xt")], [V("vt")], "ldv")
 
     iota(col("pi", 0), [[0, 1]], 0, 1)
-    iota(V("ui"), [[16, 8]])
+    iota(V("ui", 0, 8), [[16, 8]])
     iota(V("c32"), [[1, 32]])
     iota(V("cm"), [[0, 2], [1, 16]])
+    iota(V("ui", 8, 12), [[16, 2], [0, 2]], 1)
+    iota(V("tmp", 128, 164), [[0, 6], [1, 6]])
     c16 = V("cm", 0, 16)
     ts(col("pj", 0), col("pi", 0), 15, A.bitwise_and)
     ts(col("pj", 1), col("pi", 0), 31, A.bitwise_and)
-    copy(V("uo"), V("ui"))
+    copy(V("uo", 0, 8), V("ui", 0, 8))
     copy(V("pf", 0, 2), V("pj", 0, 2))
     ts(H, RR, 16.0, A.is_ge)
     ts(V("oth"), V("c32"), 16.0, A.is_ge, H, A.not_equal)
-    ts(V("tmp", 0, 16), c16, J, A.is_lt, 2048.0, A.mult)
+    ts(V("tmp", 0, 16), c16, J, A.is_lt, 32.0, A.mult)
     ts(V("tmp", 16, 32), V("tmp", 0, 16), 1.0, A.max)
-    fill(V("tmp", 32, 48), 0.0)
-    scan(V("tmp", 48, 64), V("tmp", 16, 32), V("tmp", 32, 48), 2.0 ** -104, A.mult, A.add)
-    ts(col("sm", 1), J, 0.0, A.is_gt)
-    ts(THR1, col("tmp", 63), col("sm", 1), A.mult)
-    act(NTH, THR1, ACT.Copy, -1.0)
-    ts(V("tmp", 64, 80), c16, J, A.is_lt, 1.0, A.add)
-    product(P2, V("tmp", 64, 80))
-    ts(V("tmp", 80, 96), c16, J, A.is_ge, 1.0, A.add)
-    product(P2N, V("tmp", 80, 96))
-    ts(V("xx", 0, 32), V("oth"), 2.0 ** 90, A.mult, THR1, A.max)
-    ts(V("xx", 32, 64), V("oth"), 2.0 ** 32, A.mult, P2, A.max)
+    scan(V("tmp", 32, 48), V("tmp", 16, 32), V("tmp", 16, 32), 2.0 ** -88, A.mult, A.min)
+    act(PB, PA, ACT.Copy, 2.0 ** 80)
+    act(NA, PA, ACT.Copy, -1.0)
+    act(NB, PA, ACT.Copy, -2.0 ** 80)
+    ts(V("xx", 0, 32), V("oth"), 2.0 ** 90, A.mult, PA, A.max)
+    ts(V("xx", 32, 64), V("oth"), 2.0 ** 90, A.mult, PB, A.max)
     turn(V("rows"), V("xx"))
-    act(V("t1"), V("rows", 0, 32), ACT.Copy, P2)
-    ts(V("l2t"), V("rows", 32, 64), P2N, A.mult, 2.0 ** -16, A.mult)
-    ts(col("cs", 5), J, 1.0 / 16, A.mult, 1.0, A.add)
-    act(V("t2"), V("l2t"), ACT.Copy, col("cs", 5))
-    ts(V("tmp", 96, 128), V("oth"), 2.0 ** 25, A.mult)
-    tt(V("aa"), V("tmp", 96, 128), V("cm"), A.add)
-    for k in range(4):
-        act(col("cs", 8 + k), J, ACT.Copy, -15 * 2.0 ** (-8 - 4 * k))
-    ts(col("cs", 12), J, -7 * 2.0 ** -23, A.mult, 2.0 ** -24, A.add)
-    ts(col("cs", 13), J, -2.0 ** -23, A.mult, 2.0 ** -24, A.add)
-    ts(col("gg", 192), J, 2.0 ** -23, A.mult, 2.0 ** -24, A.add)
-    for k in range(6):
-        lin(V("gg", 32 * k, 32 * k + 32), V("aa"), 2.0 ** (-4 - 4 * k if k < 5 else -23), col("cs", 8 + k))
-    act(col("cs", 14), H, ACT.Copy, -1024.0 * HUGE)
-    ts(col("cs", 15), H, 2048.0 * HUGE, A.mult, -1024.0 * HUGE, A.add)
-    ts(col("cs", 16), J, 0.0, A.is_equal, 512.0 * HUGE, A.mult)
-    for name, n in (("dz1", 256), ("dz", NV)) if NV != 256 else (("dz", NV),):
-        fill(V(name, 0, 2), 1.0)
-        fill(col(name, 2), 0.5)
-        fill(V(name, 3, n + 4), 1.0)
-        fill(col(name, n + 4), -HUGE)
-        fill(V(name, n + 5, n + 36), 1.0)
-    for name, n in (("vf1", 256), ("vf", NV), ("vf8", NV)):
-        fill(V(name, 0, 2) if name != "vf1" else col(name, 1), 0.0)
-        fill(col(name, n + 2), -128.0 if name == "vf1" else 0.0)
-        fill(col(name, n + 3), -0.25)
-        fill(V(name, n + 5, n + 36), 0.0)
-        act(col(name, n + 20), col("cs", 15))
-        if name == "vf":
-            lin(col(name, n + 4), col("cs", 14), 1.0, col("cs", 16))
-        else:
-            act(col(name, n + 4), col("cs", 14))
+    fill(V("tmp", 64, 100), 1.0)
+    fill(V("tmp", 70, 100, 6), 2.0)
+    scan(V("ef", 0, 36), V("tmp", 64, 100), V("tmp", 64, 100), 1.0, A.mult, A.max)
+    ts(V("tmp", 164, 200), V("tmp", 128, 164), W2 * STEP, A.mult, 1.0, A.add)
+    tt(V("ef", 48, 84), V("ef", 0, 36), V("tmp", 164, 200), A.mult)
+    ts(V("uo", 8, 12), V("ui", 8, 12), J, A.add)
+    act(V("xl", 0, 64), (V("ef", 0, 36), V("uo", 8, 12)))
+    act(V("f65", 0, 64), (V("ef", 48, 84), V("uo", 8, 12)))
+    fill(col("e65", 64), 1.0)
+    fill(col("f65", 64), 1.0)
+    turn(V("fab"), V("f65", 0, 64))
+    act(V("t1", 0, 64), V("rows"), ACT.Copy, col("fab", 0))
+    act(V("t1", 64, 128), V("rows"), ACT.Copy, col("fab", 32))
+    ts(V("tmp", 200, 232), V("oth"), 2.0 ** 25, A.mult)
+    tt(V("e65", 0, 32), V("xl", 0, 32), V("tmp", 200, 232), A.max)
+    tt(V("e65", 32, 64), V("xl", 32, 64), V("tmp", 200, 232), A.max)
+    ts(col("cs", 5), J, W[3] * STEP, A.mult, W[3] * STEP, A.add)
+    act(V("row", 0, 65), V("e65"), ACT.Copy, col("cs", 5))
+    tt(V("g65"), V("row", 0, 65), V("f65"), A.add)
+    tt(V("aa", 0, 32), V("tmp", 200, 232), V("cm"), A.add)
+    fill(col("aa", 32), -1.0)
+    for k in range(3, 8):
+        ts(col("cs", 5 + k), J, (W[k + 1] - W[k]) * STEP, A.mult, (W[k + 1] + {5: -0.5, 7: 0.5}.get(k, 0.0)) * STEP, A.add)
+        lin(V("gg", 33 * k - 99, 33 * k - 66), V("aa"), W[k] * STEP, col("cs", 5 + k))
+    act(col("cs", 14), H, ACT.Copy, -4096.0 * HUGE)
+    ts(col("cs", 15), H, 8192.0 * HUGE, A.mult, -4096.0 * HUGE, A.add)
+    fill(V("dz", 0, 516), 1.0)
+    fill(col("dz", 516), -HUGE)
+    fill(V("dz", 517, 548), 1.0)
+    fill(col("vb", 514), -float(NV2))
+    fill(col("vb", 515), -0.5)
+    fill(V("vb", 517, 548), 0.0)
+    act(col("vb", 516), col("cs", 14))
+    act(col("vb", 532), col("cs", 15))
+    fill(col("vb", 1), NV2 - 768.0)
+    act(last("va", TAIL - 1), last("vb", TAIL - 1))
+    act(last("v1", TAIL - 1), last("vb", TAIL - 1))
+    fill(col("va", 2 + NV2), -float(NV))
+    fill(col("va", 1), float(NV - NV2))
+    fill(col("v1", 258), -512.0)
     fill(V("fgt", 32, 64), 0.0)
     fill(V("mgt"), 1.0)
     ts(col("mgt", 32), H, -1.0, A.mult, 1.0, A.add)
@@ -268,22 +280,41 @@ def rank_program(g, core, T, topo):
     fill(V("j0", 1, 96, 3), -1.0)
     ts(col("cs", 18), J, -32.0, A.mult, -257.0, A.add)
     lin(V("j0", 2, 96, 3), V("c32"), -1.0, col("cs", 18))
-    iota(V("c16"), [[0, 16], [1, 16]])
+    IN6, FG6, MG, J6, Y6 = 0, 96, 224, 352, 448
+    P0, P1, ME, OE, Q6 = 0, 192, 384, 512, 640
+    SG = col("cs", 22)
+    ts(col("pj", 2), col("pi", 0), 1, A.bitwise_and)
+    ts(SG, col("pj", 2), 2.0, A.mult, -1.0, A.add)
+    iota(V("pw", IN6, IN6 + 96), [[0, 96]], -1)
+    iota(V("pw", FG6 + 96, FG6 + 128), [[0, 32]])
+    iota(V("pw", MG, MG + 96), [[0, 96]], -1)
+    ts(V("pw", MG + 96, MG + 128), V("c32"), col("cs", 17), A.not_equal)
+    act(col("pw", MG + 96), col("mgt", 32), ACT.Copy, SG)
+    act(col("pw", MG + 112), H, ACT.Copy, UP)
+    iota(V("pn", ME, ME + 96), [[0, 96]], -1)
+    act(V("pn", ME + 97, ME + 128), V("mge", 33, 64))
+    act(col("pn", ME + 96), SG, ACT.Copy, DOWN)
+    iota(V("pn", P0 + 160, P0 + 192), [[0, 32]])
+    iota(V("pn", P1, P1 + 63), [[0, 63]], 8192)
+    iota(col("pn", P1 + 63), [[0, 1]])
+    iota(V("pw", J6, J6 + 96), [[0, 16], [0, 3], [1, 2]])
+    iota(V("pw", J6 + 3, J6 + 96, 6), [[0, 16]], -3)
+    fill(V("pw", J6 + 4, J6 + 96, 6), 0.5)
+    ts(col("cs", 23), J, 32.0, A.mult, 172.0, A.add)
+    lin(V("pw", J6 + 2, J6 + 96, 6), c16, 2.0, col("cs", 23))
+    iota(V("c16"), [[0, 8], [1, 16]])
     ts(col("cs", 19), J, 1.0, A.add)
-    ts(V("k1a"), V("c16"), J, A.not_equal)
+    ts(V("fx", 0, 128), V("c16"), J, A.not_equal)
+    ts(V("ex1", 0, 128), V("c16"), col("cs", 19), A.is_equal, 2.0 ** 48, A.mult)
     for c in range(2):
-        a, b = 128 * c, 128 * c + 128
-        ts(V("k1b", a, b), V("c16", a, b), col("cs", 19), A.is_equal, 2.0 ** 48, A.mult)
-    for c in range(4):
         a, b = 64 * c, 64 * c + 64
-        tt(V("k1", a, b), V("k1a", a, b), V("k1b", a, b), A.max)
+        tt(V("k1", a, b), V("fx", a, b), V("ex1", a, b), A.max)
     ts(V("k2"), V("c16"), J, A.is_equal, 1024.0, A.mult)
     ts(col("cs", 20), J, 15.0, A.is_equal, 2.0 ** -48, A.max)
     act(col("cs", 21), col("cs", 20), ACT.Copy, 512.0)
 
-    fill(V("ones", 0, 258), 0.5)
-    fill(V("ones", 258, 516), 0.5)
-    add("g", lambda: g.affine_select(T.et[:], T.ones[:], [[-1, 516]], A.is_equal, 0.0, 3, 4), [V("ones")], [V("et")],
+    iota(V("ones"), [[0, 516]])
+    add("g", lambda: g.affine_select(T.et[:], T.ones[:], [[-1, 516]], A.not_equal, 0.5, 3, 4), [V("ones")], [V("et")],
         170 + 2 * CY * 516)
 
     sent = 0
@@ -295,11 +326,14 @@ def rank_program(g, core, T, topo):
             def send(o=o, i=i, cast=cast, t=t, pid=pid, rid=rid, m=m):
                 a, b = (T[o][:].bitcast(dt.uint8), T[i][:].bitcast(dt.uint8)) if cast else (T[o][:], T[i][:])
                 return g.remote_dma(a, b, T.sem["arr%d" % t], T.sem.sent, pid, rid, m)
-            add("g", send, [V(i)], [V(o)], 1000, "remote", (), 7000)
+            add("g", send, [V(i)], [V(o)], 1600, "remote", (), 9000)
         sent += 2 * len(topo.engines(core, dst))
 
     iota(V("ic"), [[1, 256]])
-    iota(V("phm"), [[1, 32], [32, 16]], -256)
+    iota(V("phm"), [[2, 16], [32, 16]], -255)
+    iota(V("k3"), [[0, 129], [-3, 2]], 2)
+    iota(V("r2", 0, 512), [[0, 512]], -1000)
+    iota(V("r3", 0, 512), [[0, 512]], -1000)
     iota(V("ia2", 1, 512, 2), [[1, 256]], C)
     iota(V("ib2", 0, 512, 2), [[1, 256]], C)
     iota(V("ia3", 1, 512, 2), [[1, 256]], C + K)
@@ -308,9 +342,9 @@ def rank_program(g, core, T, topo):
     iota(V("elb", 512, 1024, 2), [[1, 256]], C + 2 * K)
 
     quant("uc", "usc", 0, 128, V("ut"))
-    add("v", lambda: g.vector.tensor_copy(T.upc[:].bitcast(dt.uint32), T.uc[:].bitcast(dt.uint32).indirect(T.uo[:])),
-        [V("uc"), V("uo")], [V("upc")], 50 + 128 * GATHER * CY)
-    add("s", lambda: g.scalar.activation(T.ups[:], T.usc[:].indirect(T.uo[:]), ACT.Copy), [V("usc"), V("uo")], [V("ups")],
+    add("v", lambda: g.vector.tensor_copy(T.upc[:].bitcast(dt.uint32), T.uc[:].bitcast(dt.uint32).indirect(T.uo[:, 0:8])),
+        [V("uc"), V("uo", 0, 8)], [V("upc")], 50 + 128 * GATHER * CY)
+    add("s", lambda: g.scalar.activation(T.ups[:], T.usc[:].indirect(T.uo[:, 0:8]), ACT.Copy), [V("usc"), V("uo", 0, 8)], [V("ups")],
         65 + 128 * GATHER * CY)
     for h in range(2):
         quant("tc", "tsc", 128 * h, 128 * h + 128, V("xt", 512 * h, 512 * h + 512))
@@ -319,17 +353,17 @@ def rank_program(g, core, T, topo):
     copy(V("eau"), V("eai"))
     copy(V("ebu"), V("ebi"))
     for c in range(4):
-        move("sssv"[c], V("pa", 128 * c, 128 * c + 128), (V("ptab"), V("eau", 8 * c, 8 * c + 8)))
+        move(FIRST[c], V("pa", 128 * c, 128 * c + 128), (V("ptab"), V("eau", 8 * c, 8 * c + 8)))
     for c in range(4):
         tt(V("dd", 128 * c, 128 * c + 128), (V("ptab"), V("ebu", 8 * c, 8 * c + 8)), V("pa", 128 * c, 128 * c + 128), A.subtract)
     store_codes("y", 0, 256)
     store_scales("yyyy", 0, 256)
 
-    ts(V("xl", 32, 64), V("ebi"), 2.0 ** -9, A.mult, 1.0, A.add)
+    ts(V("xx", 32, 64), V("ebi"), 2.0 ** -9, A.mult, 1.0, A.add)
     for s in range(2):
-        tt(V("xl", 16 * s, 16 * s + 16), V("eai", s, 32, 2), V("xl", 32 + s, 64, 2), A.add)
-        dma("y", lambda s=s: T.x0[0:128:16, 256 * s:256 * s + 256], lambda s=s: T.xl[:, 16 * s:16 * s + 16],
-            [V("xl", 16 * s, 16 * s + 16)], [V("x0", 256 * s, 256 * s + 256)], "row%d" % s)
+        tt(V("xx", 16 * s, 16 * s + 16), V("eai", s, 32, 2), V("xx", 32 + s, 64, 2), A.add)
+        dma("y", lambda s=s: T.x0[0:128:16, 256 * s:256 * s + 256], lambda s=s: T.xx[:, 16 * s:16 * s + 16],
+            [V("xx", 16 * s, 16 * s + 16)], [V("x0", 256 * s, 256 * s + 256)], "row%d" % s)
     for j in range(16):
         dma("y", lambda j=j: T.xr[j:128:16, :], lambda: T.x0[0:128:16, :], [V("x0")], [V("xr", j, 512, 16)], "rows")
 
@@ -345,60 +379,64 @@ def rank_program(g, core, T, topo):
 
     unpack(0)
 
+    def verdict(o, name, n, cnt, side):
+        scan(last(o, n), last("dz", n), last(name, n), cnt, A.mult, A.add)
+        turn(V("tr", 32 * side, 32 * side + 32), last(o, 32))
+
+    def choose(k, row, n, init):
+        scan(V("th", 64 * k, 64 * k + n), V("tr", 0, n), row, init, A.max, A.min)
+        return col("th", 64 * k + n - 1)
+
     for t in range(1, R + 1):
         n = C + (t - 1) * K
         sd = V("sd", 32 * t - 32, 32 * t)
         li = "l%d" % t
 
-        def th(k):
-            return col("th", 32 * k - 1)
-
-        LO2 = col("th", 287)
-
-        act(V("ss", 0, 256), V("dd", 0, 256), ACT.Abs)
-        count(col("cnt", 8), V("ss", 0, 256), THR1)
-        copy(col("vf1", 0), col("cnt", 8))
-        count(col("cnt", 0), V("dd", 256, 512), THR1)
-        ts(V("vf1", 2, 258), V("dd", 256, 512), NTH, A.is_gt, -0.5, A.add)
+        for e in range(2):
+            part = (128 * e, 128 * e + 128) if t == 1 else (e, 256, 2)
+            act(V("ss", *part), V("dd", *part), ACT.Abs)
+        count(col("cnt", 8), V("ss", 0, 256), PA)
+        copy(col("v1", 1), col("cnt", 8))
+        ts(V("vb", 2, 258), V("ss", 0, 256), PB, A.is_lt, 2.0, A.mult)
+        count(col("cnt", 1), V("dd", 256, 512), PB, 1)
+        count(col("cnt", 0), V("dd", 256, 512), PA)
+        ts(V("vb", 258, 514), V("dd", 256, 512), NB, A.is_gt, 2.0, A.mult)
+        ts(V("v1", 2, 258), V("dd", 256, 512), NA, A.is_gt, 2.0, A.mult)
         act(V("ss", 256, 512), V("dd", 256, 512), ACT.Abs)
         dma("y", lambda t=t: T.sd[:, 32 * t - 32:32 * t], lambda: T.ss[0:128:16, :], [V("ss")], [sd], "sd%d" % t)
-
-        for k in range(1, 9):
-            thr = THR1 if k == 1 else th(k - 1)
-            cnt = col("cnt", k - 1)
-            src = "sp" if k == 8 else "ss"
-            row = V("t1") if k == 1 else V("row", 32 * k - 32, 32 * k)
-            if k == 1:
-                scan(V("vo", 0, 292), V("dz" if NV == 256 else "dz1"), V("vf1"), cnt, A.mult, A.add)
-                turn(V("tr"), V("vo", 260, 292))
+        verdict("ob", "vb", 513 + TAIL, col("cnt", 1), 1)
+        verdict("oa", "v1", 257 + TAIL, col("cnt", 0), 0)
+        pa = choose(0, V("t1", 0, 64), 64, 0.0)
+        pb = choose(1, V("t1", 64, 128), 64, 0.0)
+        low = choose(2, V("rows"), 64, 0.0)
+        count(col("cnt", 2), V("ss", 0, 512 - NV2), pa)
+        count(col("cnt", 3), V("ss", 0, 512 - NV2), pb, 1)
+        ts(V("va", 2, 2 + NV2), V("ss", 512 - NV2, 512), pa, A.is_lt, 2.0, A.mult)
+        ts(V("vb", 514 - NV2, 514), V("ss", 512 - NV2, 512), pb, A.is_lt, 2.0, A.mult)
+        ts(V("row", 0, 65), V("g65"), low, A.mult)
+        ts(V("row", 65, 130), V("e65"), low, A.mult)
+        verdict("oa", "va", 1 + NV2 + TAIL, col("cnt", 2), 0)
+        verdict("ob", "vb", NV2 + TAIL, col("cnt", 3), 1)
+        thr = choose(3, V("row", 0, 64), 64, col("row", 64))
+        LO2 = choose(4, V("row", 65, 129), 64, col("row", 129))
+        ts(col("sm", 5), LO2, -1.0, A.mult)
+        lin(V("sp", 0, 256), V("ss", 0, 256), 1.0, col("sm", 5))
+        lin(V("sp", 256, 512), V("ss", 256, 512), 1.0, col("sm", 5))
+        act(V("gl"), V("gg", 132, 165), ACT.Copy, LO2)
+        for k in range(3, 8):
+            src = "sp" if k > 5 else "ss"
+            row = V("row", 65 * k, 65 * k + 33)
+            count(col("cnt", k + 1), V(src, 0, 512 - NV), thr)
+            ts(V("va", 2 + NV2 - NV, 2 + NV2), V(src, 512 - NV, 512), thr, A.is_lt, 2.0, A.mult)
+            if k == 7:
+                ts(row, V("gl"), thr, A.add, LO2, A.add)
             else:
-                vf = "vf8" if k == 8 else "vf"
-                count(cnt, V(src, 0, 512 - NV), thr)
-                ts(V(vf, 2, NV + 2), V(src, 512 - NV, 512), thr, A.is_lt, -0.5, A.add)
-                if k == 2:
-                    ts(row, V("t2"), thr, A.mult)
-                    ts(V("row", 0, 32), V("l2t"), thr, A.mult)
-                elif k == 3:
-                    act(col("sm", 5), LO2, ACT.Copy, -1.0)
-                    ts(V("gl", 0, 32), V("gg", 0, 32), LO2, A.mult)
-                    ts(row, V("gl", 0, 32), thr, A.add)
-                    act(V("gl", 32, 193), V("gg", 32, 193), ACT.Copy, LO2)
-                    lin(V("sp", 0, 256), V("ss", 0, 256), 1.0, col("sm", 5))
-                    lin(V("sp", 256, 512), V("ss", 256, 512), 1.0, col("sm", 5))
-                elif k == 7:
+                if k == 5:
                     ts(col("sm", 4), thr, LO2, A.subtract)
-                    ts(row, V("gl", 128, 160), col("sm", 4), A.add)
-                elif k == 8:
-                    ts(row, V("gl", 160, 192), thr, A.add, LO2, A.add)
-                    ts(col("sm", 6), thr, col("gl", 192), A.subtract, LO2, A.add)
-                else:
-                    ts(row, V("gl", 32 * k - 96, 32 * k - 64), thr, A.add)
-                scan(V("vo", 0, NF), V("dz"), V(vf), cnt, A.mult, A.add)
-                turn(V("tr"), V("vo", NV + 4, NF))
-            scan(V("th", 32 * k - 32, 32 * k), V("tr"), row, col("sm", 6) if k == 8 else 0.0, A.max, A.min)
-            if k == 2:
-                scan(V("th", 256, 288), V("tr"), V("row", 0, 32), 0.0, A.max, A.min)
-        TT = th(8)
+                ts(row, V("gg", 33 * k - 99, 33 * k - 66), LO2, A.mult, col("sm", 4) if k == 5 else thr, A.add)
+            verdict("oa", "va", NV + TAIL, col("cnt", k + 1), 0)
+            thr = choose(k + 2, V("row", 65 * k, 65 * k + 32), 32, col("row", 65 * k + 32))
+        TT = thr
 
         if t == 1:
             for b in range(4):
@@ -432,26 +470,46 @@ def rank_program(g, core, T, topo):
         act(V("ysb", n - 256, n), bank(6))
         store_y("y", n - 256, n)
 
-        ts(V("fgt", 0, 32), sd, TT, A.is_gt)
-        ts(V("h0", 65, 160, 3), sd, TT, A.is_ge, -1.0, A.add)
-        scan(V("h1", 65, 256, 3), V("mgt"), V("fgt"), 0.0, A.mult, A.add)
-        scan(V("oge"), V("mge"), V("h0", 65, 256, 3), 32.0, A.mult, A.add)
-        turn(V("h0", 0, 32), V("h1", 161, 256, 3))
-        turn(V("h0", 32, 64), V("oge", 32, 64))
-        scan(V("qq"), V("h0", 0, 160), V("h1", 0, 160), -256.0, A.add, A.min)
-        scan(V("yy"), V("j0"), V("qq", 64, 160), 0.0, A.mult, A.add)
-        ts(V("so"), V("yy", 2, 96, 3), col("qq", 31), A.subtract, -1.0, A.add)
         if t == 1:
+            ts(V("fgt", 0, 32), sd, TT, A.is_gt)
+            ts(V("h0", 65, 160, 3), sd, TT, A.is_ge, -1.0, A.add)
+            scan(V("h1", 65, 256, 3), V("mgt"), V("fgt"), 0.0, A.mult, A.add)
+            scan(V("oge"), V("mge"), V("h0", 65, 256, 3), 32.0, A.mult, A.add)
+            turn(V("h0", 0, 32), V("h1", 161, 256, 3))
+            turn(V("h0", 32, 64), V("oge", 32, 64))
+            scan(V("qq"), V("h0", 0, 160), V("h1", 0, 160), -256.0, A.add, A.min)
+            scan(V("yy"), V("j0"), V("qq", 64, 160), 0.0, A.mult, A.add)
+            ts(V("so"), V("yy", 2, 96, 3), col("qq", 31), A.subtract, -1.0, A.add)
             copy((V("r1"), V("so")), V("xr"))
-            scan(V("ex1"), V("k1"), V("r1", 0, 256), 0.0, A.mult, A.add)
-            ts(V("la"), V("ex1", 15, 256, 16), col("cs", 20), A.mult, -1.0, A.add)
-            ts(V("wi"), V("ex1", 15, 256, 16), col("cs", 21), A.mult)
-            ts(V("wb"), V("wi"), 511, A.bitwise_and)
-            copy(V("lb"), V("wb"))
+            for h in range(2):
+                a, b = 128 * h, 8 * h
+                scan(V("ex1", a, a + 128), V("k1"), V("r1", a, a + 128), 0.0, A.mult, A.add)
+                ts(V("wi", b, b + 8), V("ex1", a + 15, a + 128, 16), col("cs", 21), A.mult)
+                ts(V("la", b, b + 8), V("ex1", a + 15, a + 128, 16), col("cs", 20), A.mult, -1.0, A.add)
+                ts(V("wb", b, b + 8), V("wi", b, b + 8), 511, A.bitwise_and)
+                copy(V("lb", b, b + 8), V("wb", b, b + 8))
         else:
-            copy((V("r2"), V("so")), V("phm"))
-            scan(V("ex2"), V("k2"), V("r2", 0, 256), 0.0, A.add, A.min)
-            ts(V(li), V("ex2", 15, 256, 16), 256.0, A.add)
+            s0, s1 = V("sd", 32 * t - 32, 32 * t, 2), V("sd", 32 * t - 31, 32 * t, 2)
+            act(V("pw", IN6 + 3, IN6 + 96, 6), s0)
+            act(V("pw", IN6 + 5, IN6 + 96, 6), s1)
+            tt(V("pw", IN6 + 1, IN6 + 96, 6), s0, s1, A.max)
+            tt(V("pw", IN6 + 2, IN6 + 96, 6), s0, s1, A.max)
+            ts(V("pw", FG6, FG6 + 96), V("pw", IN6, IN6 + 96), TT, A.is_gt, 1024.0, A.add)
+            ts(V("pn", P0 + 64, P0 + 160), V("pw", IN6, IN6 + 96), TT, A.is_ge, -1.0, A.add)
+            scan(V("pn", P1 + 64, P1 + 192), V("pw", MG, MG + 128), V("pw", FG6, FG6 + 128), 0.0, A.mult, A.add)
+            scan(V("pn", OE, OE + 128), V("pn", ME, ME + 128), V("pn", P0 + 64, P0 + 192), 0.0, A.mult, A.add)
+            turn(V("pn", P0, P0 + 32), V("pn", P1 + 160, P1 + 192))
+            turn(V("pn", P0 + 32, P0 + 64), V("pn", OE + 96, OE + 128))
+            scan(V("pn", Q6, Q6 + 160), V("pn", P0, P0 + 160), V("pn", P1, P1 + 160), -256.0, A.subtract, A.min)
+            scan(V("pw", Y6, Y6 + 96), V("pw", J6, J6 + 96), V("pn", Q6 + 64, Q6 + 160), 0.0, A.mult, A.add)
+            ts(V("so", 0, 16), V("pw", Y6 + 4, Y6 + 96, 6), col("pn", Q6 + 31), A.subtract, 2.0, A.mult)
+            rw = "r%d" % t
+            copy((V(rw), V("so", 0, 16)), V("phm"))
+            for h in range(2):
+                a = 258 * h
+                scan(V("fx", 256 * h, a + 256), V("k3", 0, 256 + 2 * h), V(rw, 254 * h, 256 * h + 256), -1000.0, A.add, A.max)
+                scan(V("ex2", 128 * h, 128 * h + 128), V("k2"), V("fx", a + 1, a + 256, 2), 0.0, A.add, A.min)
+                ts(V(li, 8 * h, 8 * h + 8), V("ex2", 128 * h + 15, 128 * h + 128, 16), 256.0, A.add)
 
         for h in range(2):
             for b in range(4):
@@ -481,7 +539,7 @@ def rank_program(g, core, T, topo):
         for h in range(2):
             for b in range(4):
                 src = T.cores[(rank + t) % N]
-                extra = (("arr%d" % t, 2 * len(topo.engines(src, core))),) if h == 0 and b == 0 else ()
+                extra = (("arr%d" % t, 2 * len(topo.engines(src, core))),)
                 mm(4 * h + b, "wl%d" % t, "wls%d" % t, 128 * b, "mc", "msc", 128 * h, 128 * h + 128, extra)
             for b in range(4):
                 out = V("ft", 512 * h + b, 512 * h + 512, 4)
@@ -513,9 +571,13 @@ def rank_program(g, core, T, topo):
     g.scalar.wait_ge(T.sem.outs, outs["outs"])
 
 
+FIRST = "sssv"
 PICK = ["vvss", "vvss"]
 ENDS = ["svsv", "svsv", "ssss"]
 SCALE = [["ssss", "ssvv"], ["ssvv", "ssvv"], ["ssvv", "ssvv"]]
+ORDER = (
+    "1v0308001u01020t04091r0a0f0e0b0u1s0c0h1d0d230i2r0g0k0v191o2s0l1p0y2t1t1w0m0j0w2x1q0n0x1x300q1y0o0r310p111610320s2033400506430734384142460z3h4a1z4944134j47174k184l1c4m454n48144o21224b4e124c3i4f4d4g5j4i5k4h4p5l5n4q5q5o5r3j5p5m5u1a3k155w5s1e5v5x3l1g1i5y4r605z3m63614s5t64623n671h661j691f1b3o686a65256c3p6b242a6d6i6h3q1k6j6k4t4u2b4v2f4w3r4x4y6l1m4z265051526m532c542j55563s576o6n586p276e286q1n2d296r2h3t2e6s2g2l2n6u6t6v2k1l2i6f6x3u2m6w6g6y593v6z5a7270715b3w735c3x74393a5h753b5e78763y775g3c5f797e3z3d2o7a5d7b2p5i7i7j7k7g7l7m7n3f7h7o3g2u7p3e7q2q367r2z7d377c2w2v2y7f357s7x7t7u7y7v7z82807w848186838885878b898d8c8f8a8h8e8o8g8p8i8q8s8r8t8j8u8l8v928k918w909693958x94978m8y988z9m8n999h9i9n9j9f9k9l9a9d9b9o9q9c9t9r9e9u9g9s9p9x9v9zbt9y9wa0bja1a2a3a6a4a7a5a8aabzc0acbwa9abadbkaeblafalakagamajahanbmaiaobuapbvasaqarbxbnatbyc1aubfavbgaxawbhbqayb0azcfcgb1cib2bib4b3b5c7b6c8bsb7brb8chbab9bbc5bccabobdcbbpbec3cjckccclcmc9cncocdcpc4cqcec6crc2csctcwcucxcvcyczd2d0d1d7d3d6d5dbddd4dfdedhdgd8djdidkd9dpdqdrdldtdsdadudmdvgadwdndxdoebdcdye6e7ece8e5e9eadze3e0edefe1eiege2eje4eheeemekeogdenelepgbeqesereveteweuezguexf1gmeyf0gvf2gcf3f4gefaf9f5fbf7fcgff6fdgnfegofgfffhgpfigzfjgyfkgrfmflfng4fpfofqgqfrg5ftfsfug7fvg6f8fwfxg8fzfyg0gxgwg1gsg9g2gjg3ggh0h1h2gth3h4h5h6gkh7glh8gih9ghhahdhbhehchfhghjhhhihlhnhkhohmhrhwhuhphvi0hxhyi7hzi9i1i8ibiaidiciehti2hqifi3i6hsigijikimili4inioihi5ii"
+)
 
 
 def depends(ops):
@@ -588,7 +650,8 @@ PLAN = []
 def emit(T, queue, ops):
     deps = depends(ops)
     if not PLAN:
-        PLAN.append(arrange(ops, deps))
+        given = [int(ORDER[i:i + 2], 36) for i in range(0, len(ORDER), 2)]
+        PLAN.append(given if len(given) == len(ops) else arrange(ops, deps))
     order = PLAN[0]
     at = {i: p for p, i in enumerate(order)}
     total = {}
@@ -610,15 +673,17 @@ def emit(T, queue, ops):
                 mine.append(j)
                 needed.add(j)
                 known[q] = known.get(q, 0) | done[j] | group.get(ops[j][4], 0)
-        waits[i] = (mine, known.get(q, 0))
+        waits[i] = (mine[::-1], known.get(q, 0))
         done[i] = known.get(q, 0) | 1 << i
     token, last, used = {}, {}, {}
     for i in order:
         q, call, sem, extra = ops[i][0], ops[i][1], ops[i][4], ops[i][5]
+        for name, val in extra:
+            if name not in used:
+                used[name] = True
+                queue[q].wait_ge(T.sem[name], val)
         for j in waits[i][0]:
             queue[q].wait_ge(T.sem[token[j][0]], token[j][1])
-        for name, val in extra:
-            queue[q].wait_ge(T.sem[name], val)
         if sem is None and i in needed:
             k = used.get(q, 0)
             free = [c % POOL[q] for c in range(k, k + POOL[q])

from concourse.mybir import dt, AluOpType, AxisListType, ActivationFunctionType

N, C, K, R = 8, 256, 256, 3
X4, U8 = "float8_e4m3fn_x4", "uint8"
F32, BF, I32, U16 = "float32", "bfloat16", "int32", "uint16"
NV = 256
NV2 = 288
TAIL = 34
W2 = 1398096
W = {3: 82242, 4: 4838, 5: 285, 6: 17, 7: 1, 8: 0}


def _sb(n, t):
    return ("sbuf", [128, n], t)


SCRATCH = {
    "xt": _sb(1024, BF), "ut": _sb(512, BF), "vt": _sb(512, BF), "eai": _sb(32, I32), "ebi": _sb(32, I32),
    "eau": _sb(32, U16), "ebu": _sb(32, U16),
    "tc": _sb(1024, X4), "tsc": _sb(1024, U8), "uc": _sb(128, X4), "usc": _sb(128, U8),
    "upc": _sb(128, X4), "ups": _sb(128, U8), "vc": _sb(128, X4), "vsc": _sb(128, U8),
    "ec": _sb(512, X4), "esc": _sb(512, U8), "mc": _sb(256, X4), "msc": _sb(256, U8),
    "wo": _sb(512, X4), "wos": _sb(512, U8),
    "wl1": _sb(512, X4), "wls1": _sb(512, U8), "wl2": _sb(512, X4), "wls2": _sb(512, U8),
    "wl3": _sb(512, X4), "wls3": _sb(512, U8),
    "ones": _sb(516, BF), "et": _sb(516, BF), "mt": _sb(1024, BF), "ft": _sb(1024, BF),
    "z1": _sb(1024, BF), "ea2": _sb(2048, BF), "eb2": _sb(2048, BF), "a3": _sb(1024, BF), "b3": _sb(1024, BF),
    "mid": _sb(2048, BF),
    "ptab": _sb(256, F32), "pa": _sb(512, F32), "dd": _sb(512, F32), "ss": _sb(512, F32), "sp": _sb(512, F32),
    "junk": _sb(1024, BF), "sd": _sb(32 * R, F32),
    "pa2": _sb(512, F32), "pb2": _sb(512, F32), "pa3": _sb(256, F32), "pb3": _sb(256, F32),
    "ia2": _sb(512, F32), "ib2": _sb(512, F32), "ia3": _sb(512, F32), "ib3": _sb(512, F32), "elb": _sb(1024, F32),
    "ysb": _sb(1024, F32), "xl": _sb(64, F32), "x0": _sb(512, F32), "xr": _sb(512, F32), "phm": _sb(256, BF),
    "ic": _sb(256, F32), "r1": _sb(1024, F32), "r2": _sb(2560, BF), "ex1": _sb(256, F32), "ex2": _sb(256, BF),
    "c16": _sb(128, BF), "k1": _sb(128, F32), "k2": _sb(128, BF),
    "pw": _sb(544, F32), "pn": _sb(800, BF), "r3": _sb(2560, BF), "k3": _sb(258, BF), "fx": _sb(514, BF),
    "pi": _sb(8, I32), "pj": _sb(8, I32), "pf": _sb(8, F32), "ui": _sb(16, I32), "uo": _sb(16, U16),
    "c32": _sb(32, F32), "cm": _sb(32, F32), "oth": _sb(32, F32), "tmp": _sb(256, F32), "cs": _sb(32, F32),
    "xx": _sb(64, F32), "rows": _sb(64, F32), "tr": _sb(64, BF), "th": _sb(64 * 10, F32), "cnt": _sb(16, F32),
    "sm": _sb(8, F32), "t1": _sb(128, F32), "ef": _sb(96, F32), "e65": _sb(65, F32), "f65": _sb(65, F32),
    "g65": _sb(65, F32), "fab": _sb(64, F32), "aa": _sb(33, F32),
    "gg": _sb(33 * 5, F32), "gl": _sb(33, F32), "row": _sb(65 * 8, F32),
    "v1": _sb(258 + TAIL, BF), "va": _sb(2 + NV2 + TAIL, BF), "vb": _sb(514 + TAIL, BF), "dz": _sb(514 + TAIL, BF),
    "oa": _sb(2 + NV2 + TAIL, BF), "ob": _sb(514 + TAIL, BF),
    "fgt": _sb(64, F32), "mgt": _sb(64, F32), "mge": _sb(64, BF), "oge": _sb(64, BF),
    "h0": _sb(256, BF), "h1": _sb(256, BF), "qq": _sb(160, BF), "j0": _sb(96, F32), "yy": _sb(96, F32),
    "so": _sb(32, U16), "wi": _sb(16, I32), "wb": _sb(16, I32), "la": _sb(16, U16), "lb": _sb(16, U16),
    "l2": _sb(16, U16), "l3": _sb(16, U16),
    "ps": ("psum", [128, 4096], F32),
}
POOL = {"v": 56, "s": 40, "t": 20, "g": 10}
LOADS = ["ldu", "lda", "ldb", "ldx0", "ldx1", "ldw", "ldws", "ldv", "row0", "row1", "rows", "sd1", "sd2", "sd3"]
SEMAPHORES = ([q + str(i) for q in POOL for i in range(POOL[q])] + LOADS
              + ["arr1", "arr2", "arr3", "sent", "outy", "outs"])
HUGE = 2.0 ** 84
UP, DOWN = 2.0 ** 60, 2.0 ** -60
STEP = 2.0 ** -23
A = AluOpType
ACT = ActivationFunctionType
CY, WAKE, GATHER, SCATTER, SFIX, MM = 1.1, 200.0, 1.8, 3.8, 100, 1.2


def rank_program(g, core, T, topo):
    rank = T.rank_of(core)
    if rank is None:
        return
    queue = {"v": g.vector, "s": g.scalar, "t": g.tensor, "g": g, "y": g.sync}
    ops = []

    def ap(a):
        if not isinstance(a, tuple):
            return a
        if len(a) == 2:
            return ap(a[0]).indirect(ap(a[1]))
        return T[a[0]][:, a[1]:a[2]:a[3]] if a[3] != 1 else T[a[0]][:, a[1]:a[2]]

    def V(name, a=0, b=None, step=1):
        return (name, a, SCRATCH[name][1][1] if b is None else b, step)

    def col(name, a):
        return V(name, a, a + 1)

    def last(name, n):
        return V(name, SCRATCH[name][1][1] - n)

    def flat(items):
        out = []
        for a in items:
            if isinstance(a, tuple):
                out += list(a) if len(a) == 2 else [a]
        return out

    def size(a):
        return 16 * size(a[1]) if len(a) == 2 else len(range(a[1], a[2], a[3]))

    def vcost(*sides):
        n = size(sides[0])
        if len(sides[0]) == 2:
            return 50 + n * GATHER * CY
        return max(64, n * (0.5 if all(SCRATCH[a[0]][2] in (BF, U16) for a in sides) else 1)) * CY

    def add(q, call, reads, writes, cost, sem=None, extra=(), late=None):
        ops.append((q, call, flat(reads), flat(writes), sem, extra, cost, cost if late is None else late))

    def copy(out, in_):
        if len(out) == 2:
            add("v", lambda: g.vector.tensor_copy(ap(out), ap(in_)), [in_, out[1]], [out[0]], 50 + size(in_) * SCATTER * CY)
        else:
            add("v", lambda: g.vector.tensor_copy(ap(out), ap(in_)), [in_], [out], vcost(in_, out))

    def tt(out, a, b, op):
        k = 1 if "ps" in (a[0], b[0]) else 2
        add("v", lambda: g.vector.tensor_tensor(ap(out), ap(a), ap(b), op), [a, b], [out],
            50 + size(a) * GATHER * CY if len(a) == 2 else max(64, k * size(a)) * CY)

    def ts(out, a, s1, op0, s2=None, op1=None):
        if op1 is None:
            add("v", lambda: g.vector.tensor_scalar(ap(out), ap(a), ap(s1), None, op0), [a, s1], [out], vcost(a, out))
        else:
            add("v", lambda: g.vector.tensor_scalar(ap(out), ap(a), ap(s1), ap(s2), op0, op1), [a, s1, s2], [out], vcost(a, out))

    def fill(out, c):
        add("v", lambda: g.vector.memset(ap(out), c), [], [out], vcost(out))

    def scan(out, d0, d1, init, op0, op1):
        add("v", lambda: g.vector.tensor_tensor_scan(ap(out), ap(d0), ap(d1), ap(init), op0, op1), [d0, d1, init], [out],
            vcost(d0, d1, out))

    def turn(out, in_):
        add("v", lambda: g.vector.transpose(ap(out), ap(in_)), [in_], [out], vcost(in_, out))

    def act(out, in_, func=ACT.Copy, scale=1.0):
        add("s", lambda: g.scalar.activation(ap(out), ap(in_), func, scale=ap(scale)), [in_, scale], [out],
            65 + size(in_) * CY * GATHER if len(in_) == 2 else SFIX + size(in_) * CY)

    def lin(out, in_, scale, bias):
        add("s", lambda: g.scalar.activation(ap(out), ap(in_), ACT.Identity, bias=ap(bias), scale=ap(scale)), [in_, bias, scale], [out],
            SFIX + size(in_) * CY)

    def move(q, out, in_):
        if q == "s":
            act(out, in_)
        else:
            copy(out, in_)

    def count(cnt, in_, thr, side=0):
        junk = V("junk", 512 * side + in_[1], 512 * side + in_[2])
        add("s", lambda: g.scalar.activation(ap(junk), ap(in_), ACT.Sign, bias=ap(thr), scale=-1.0, accum_out=ap(cnt)),
            [in_, thr], [junk, cnt], SFIX + 20 + size(in_) * CY)

    def quant(codes, scales, a, b, in_):
        add("v", lambda: g.vector.quantize_mx(T[codes][:, a:b], T[scales][:, a:b], ap(in_)), [in_],
            [V(codes, a, b), V(scales, a, b)], (12 + 0.22 * size(in_)) * CY / 0.83)

    def mm(bank, lc, ls, a, rc, rs, c, d, extra=()):
        out = V("ps", 512 * bank, 512 * bank + d - c)
        add("t", lambda: g.tensor.matmul_mx(ap(out), T[lc][:, a:a + 128], T[ls][:, a:a + 128], T[rc][:, c:d], T[rs][:, c:d],
                                            True, True),
            [V(lc, a, a + 128), V(ls, a, a + 128), V(rc, c, d), V(rs, c, d)], [out], (d - c + 16) * MM, None, extra)

    def bank(b, a=0, n=256):
        return V("ps", 512 * b + a, 512 * b + a + n)

    def iota(out, pattern, base=0, mult=0):
        if SCRATCH[out[0]][2] == I32:
            add("g", lambda: g.iota(ap(out), pattern, base, mult), [], [out], 130 + 2 * CY * size(out))
        else:
            add("g", lambda: g.iota(ap(out), pattern, base, mult, allow_small_or_imprecise_dtypes=True), [], [out],
                130 + 2 * CY * size(out))

    def dma(q, out, in_, reads, writes, sem, late=2400):
        late = late + (1500 if sem[:2] in ("ro", "sd") else 0)
        add(q, lambda: queue[q].dma_start(out(), in_()), reads, writes, 60, sem, (), late)

    def store(q, out, in_, reads):
        dma(q, out, in_, reads, [], "out" + q)

    def store_codes(q, a, b):
        store(q, lambda: T.oc[:, 4 * a:4 * b], lambda: T.tc[:, a:b].bitcast(dt.uint8), [V("tc", a, b)])

    def store_scales(qs, a, b):
        for k in range(4):
            store(qs[k], lambda k=k: T.osc[4 * k:4 * k + 4, a:b], lambda k=k: T.tsc[32 * k:32 * k + 4, a:b], [V("tsc", a, b)])

    def store_y(q, a, b):
        store(q, lambda: T.y[:, a:b], lambda: T.ysb[:, a:b], [V("ysb", a, b)])

    J, RR, H = col("pf", 0), col("pf", 1), col("cs", 0)
    PA, PB, NA, NB = col("tmp", 47), col("cs", 2), col("cs", 3), col("cs", 4)

    dma("y", lambda: T.ut[:], lambda: T.u[:], [], [V("ut")], "ldu")
    dma("s", lambda: T.xt[:, 0:512], lambda: T.x[:, 0:512], [], [V("xt", 0, 512)], "ldx0")
    dma("y", lambda: T.xt[:, 512:1024], lambda: T.x[:, 512:1024], [], [V("xt", 512, 1024)], "ldx1")
    dma("s", lambda: T.ebi[:], lambda: T.eb[:], [], [V("ebi")], "ldb")
    dma("y", lambda: T.eai[:], lambda: T.ea[:], [], [V("eai")], "lda")
    dma("y", lambda: T.wo[:].bitcast(dt.uint8), lambda: T.wc[:], [V("xt"), V("ut")], [V("wo")], "ldw", 3000)
    dma("y", lambda: T.wos[:], lambda: T.ws[:], [V("xt")], [V("wos")], "ldws")
    dma("y", lambda: T.vt[:], lambda: T.v[:], [V("xt")], [V("vt")], "ldv")

    iota(col("pi", 0), [[0, 1]], 0, 1)
    iota(V("ui", 0, 8), [[16, 8]])
    iota(V("c32"), [[1, 32]])
    iota(V("cm"), [[0, 2], [1, 16]])
    iota(V("ui", 8, 12), [[16, 2], [0, 2]], 1)
    iota(V("tmp", 128, 164), [[0, 6], [1, 6]])
    c16 = V("cm", 0, 16)
    ts(col("pj", 0), col("pi", 0), 15, A.bitwise_and)
    ts(col("pj", 1), col("pi", 0), 31, A.bitwise_and)
    copy(V("uo", 0, 8), V("ui", 0, 8))
    copy(V("pf", 0, 2), V("pj", 0, 2))
    ts(H, RR, 16.0, A.is_ge)
    ts(V("oth"), V("c32"), 16.0, A.is_ge, H, A.not_equal)
    ts(V("tmp", 0, 16), c16, J, A.is_lt, 32.0, A.mult)
    ts(V("tmp", 16, 32), V("tmp", 0, 16), 1.0, A.max)
    scan(V("tmp", 32, 48), V("tmp", 16, 32), V("tmp", 16, 32), 2.0 ** -88, A.mult, A.min)
    act(PB, PA, ACT.Copy, 2.0 ** 80)
    act(NA, PA, ACT.Copy, -1.0)
    act(NB, PA, ACT.Copy, -2.0 ** 80)
    ts(V("xx", 0, 32), V("oth"), 2.0 ** 90, A.mult, PA, A.max)
    ts(V("xx", 32, 64), V("oth"), 2.0 ** 90, A.mult, PB, A.max)
    turn(V("rows"), V("xx"))
    fill(V("tmp", 64, 100), 1.0)
    fill(V("tmp", 70, 100, 6), 2.0)
    scan(V("ef", 0, 36), V("tmp", 64, 100), V("tmp", 64, 100), 1.0, A.mult, A.max)
    ts(V("tmp", 164, 200), V("tmp", 128, 164), W2 * STEP, A.mult, 1.0, A.add)
    tt(V("ef", 48, 84), V("ef", 0, 36), V("tmp", 164, 200), A.mult)
    ts(V("uo", 8, 12), V("ui", 8, 12), J, A.add)
    act(V("xl", 0, 64), (V("ef", 0, 36), V("uo", 8, 12)))
    act(V("f65", 0, 64), (V("ef", 48, 84), V("uo", 8, 12)))
    fill(col("e65", 64), 1.0)
    fill(col("f65", 64), 1.0)
    turn(V("fab"), V("f65", 0, 64))
    act(V("t1", 0, 64), V("rows"), ACT.Copy, col("fab", 0))
    act(V("t1", 64, 128), V("rows"), ACT.Copy, col("fab", 32))
    ts(V("tmp", 200, 232), V("oth"), 2.0 ** 25, A.mult)
    tt(V("e65", 0, 32), V("xl", 0, 32), V("tmp", 200, 232), A.max)
    tt(V("e65", 32, 64), V("xl", 32, 64), V("tmp", 200, 232), A.max)
    ts(col("cs", 5), J, W[3] * STEP, A.mult, W[3] * STEP, A.add)
    act(V("row", 0, 65), V("e65"), ACT.Copy, col("cs", 5))
    tt(V("g65"), V("row", 0, 65), V("f65"), A.add)
    tt(V("aa", 0, 32), V("tmp", 200, 232), V("cm"), A.add)
    fill(col("aa", 32), -1.0)
    for k in range(3, 8):
        ts(col("cs", 5 + k), J, (W[k + 1] - W[k]) * STEP, A.mult, (W[k + 1] + {5: -0.5, 7: 0.5}.get(k, 0.0)) * STEP, A.add)
        lin(V("gg", 33 * k - 99, 33 * k - 66), V("aa"), W[k] * STEP, col("cs", 5 + k))
    act(col("cs", 14), H, ACT.Copy, -4096.0 * HUGE)
    ts(col("cs", 15), H, 8192.0 * HUGE, A.mult, -4096.0 * HUGE, A.add)
    fill(V("dz", 0, 516), 1.0)
    fill(col("dz", 516), -HUGE)
    fill(V("dz", 517, 548), 1.0)
    fill(col("vb", 514), -float(NV2))
    fill(col("vb", 515), -0.5)
    fill(V("vb", 517, 548), 0.0)
    act(col("vb", 516), col("cs", 14))
    act(col("vb", 532), col("cs", 15))
    fill(col("vb", 1), NV2 - 768.0)
    act(last("va", TAIL - 1), last("vb", TAIL - 1))
    act(last("v1", TAIL - 1), last("vb", TAIL - 1))
    fill(col("va", 2 + NV2), -float(NV))
    fill(col("va", 1), float(NV - NV2))
    fill(col("v1", 258), -512.0)
    fill(V("fgt", 32, 64), 0.0)
    fill(V("mgt"), 1.0)
    ts(col("mgt", 32), H, -1.0, A.mult, 1.0, A.add)
    ts(col("mgt", 32), col("mgt", 32), DOWN, A.max)
    ts(col("mgt", 48), H, UP, A.mult, 1.0, A.max)
    fill(V("mge", 0, 32), 1.0)
    ts(col("cs", 17), RR, 1.0, A.add)
    ts(V("mge", 32, 64), V("c32"), col("cs", 17), A.is_equal, UP, A.mult)
    ts(V("mge", 32, 64), V("mge", 32, 64), 1.0, A.max)
    fill(col("mge", 32), DOWN)
    copy(col("mge", 48), H)
    fill(V("h0", 64, 256), 0.0)
    fill(V("h0", 64, 160, 3), 1.0)
    ts(V("h1", 0, 32), V("c32"), RR, A.is_ge, 8192.0, A.mult)
    ts(V("h1", 0, 32), V("h1", 0, 32), -256.0, A.add)
    fill(V("h1", 32, 256), 8192.0)
    fill(col("h1", 63), 0.0)
    fill(V("j0", 0, 96, 3), 0.0)
    fill(V("j0", 1, 96, 3), -1.0)
    ts(col("cs", 18), J, -32.0, A.mult, -257.0, A.add)
    lin(V("j0", 2, 96, 3), V("c32"), -1.0, col("cs", 18))
    IN6, FG6, MG, J6, Y6 = 0, 96, 224, 352, 448
    P0, P1, ME, OE, Q6 = 0, 192, 384, 512, 640
    SG = col("cs", 22)
    ts(col("pj", 2), col("pi", 0), 1, A.bitwise_and)
    ts(SG, col("pj", 2), 2.0, A.mult, -1.0, A.add)
    iota(V("pw", IN6, IN6 + 96), [[0, 96]], -1)
    iota(V("pw", FG6 + 96, FG6 + 128), [[0, 32]])
    iota(V("pw", MG, MG + 96), [[0, 96]], -1)
    ts(V("pw", MG + 96, MG + 128), V("c32"), col("cs", 17), A.not_equal)
    act(col("pw", MG + 96), col("mgt", 32), ACT.Copy, SG)
    act(col("pw", MG + 112), H, ACT.Copy, UP)
    iota(V("pn", ME, ME + 96), [[0, 96]], -1)
    act(V("pn", ME + 97, ME + 128), V("mge", 33, 64))
    act(col("pn", ME + 96), SG, ACT.Copy, DOWN)
    iota(V("pn", P0 + 160, P0 + 192), [[0, 32]])
    iota(V("pn", P1, P1 + 63), [[0, 63]], 8192)
    iota(col("pn", P1 + 63), [[0, 1]])
    iota(V("pw", J6, J6 + 96), [[0, 16], [0, 3], [1, 2]])
    iota(V("pw", J6 + 3, J6 + 96, 6), [[0, 16]], -3)
    fill(V("pw", J6 + 4, J6 + 96, 6), 0.5)
    ts(col("cs", 23), J, 32.0, A.mult, 172.0, A.add)
    lin(V("pw", J6 + 2, J6 + 96, 6), c16, 2.0, col("cs", 23))
    iota(V("c16"), [[0, 8], [1, 16]])
    ts(col("cs", 19), J, 1.0, A.add)
    ts(V("fx", 0, 128), V("c16"), J, A.not_equal)
    ts(V("ex1", 0, 128), V("c16"), col("cs", 19), A.is_equal, 2.0 ** 48, A.mult)
    for c in range(2):
        a, b = 64 * c, 64 * c + 64
        tt(V("k1", a, b), V("fx", a, b), V("ex1", a, b), A.max)
    ts(V("k2"), V("c16"), J, A.is_equal, 1024.0, A.mult)
    ts(col("cs", 20), J, 15.0, A.is_equal, 2.0 ** -48, A.max)
    act(col("cs", 21), col("cs", 20), ACT.Copy, 512.0)

    iota(V("ones"), [[0, 516]])
    add("g", lambda: g.affine_select(T.et[:], T.ones[:], [[-1, 516]], A.not_equal, 0.5, 3, 4), [V("ones")], [V("et")],
        170 + 2 * CY * 516)

    sent = 0
    for t in range(1, R + 1):
        dst = T.cores[(rank - t) % N]
        rid, pid = topo.addr(dst)[:2]
        m = topo.mask(core, dst)
        for o, i, cast in (("wl%d" % t, "wo", True), ("wls%d" % t, "wos", False)):
            def send(o=o, i=i, cast=cast, t=t, pid=pid, rid=rid, m=m):
                a, b = (T[o][:].bitcast(dt.uint8), T[i][:].bitcast(dt.uint8)) if cast else (T[o][:], T[i][:])
                return g.remote_dma(a, b, T.sem["arr%d" % t], T.sem.sent, pid, rid, m)
            add("g", send, [V(i)], [V(o)], 1600, "remote", (), 9000)
        sent += 2 * len(topo.engines(core, dst))

    iota(V("ic"), [[1, 256]])
    iota(V("phm"), [[2, 16], [32, 16]], -255)
    iota(V("k3"), [[0, 129], [-3, 2]], 2)
    iota(V("r2", 0, 512), [[0, 512]], -1000)
    iota(V("r3", 0, 512), [[0, 512]], -1000)
    iota(V("ia2", 1, 512, 2), [[1, 256]], C)
    iota(V("ib2", 0, 512, 2), [[1, 256]], C)
    iota(V("ia3", 1, 512, 2), [[1, 256]], C + K)
    iota(V("ib3", 0, 512, 2), [[1, 256]], C + K)
    iota(V("elb", 1, 512, 2), [[1, 256]], C + 2 * K)
    iota(V("elb", 512, 1024, 2), [[1, 256]], C + 2 * K)

    quant("uc", "usc", 0, 128, V("ut"))
    add("v", lambda: g.vector.tensor_copy(T.upc[:].bitcast(dt.uint32), T.uc[:].bitcast(dt.uint32).indirect(T.uo[:, 0:8])),
        [V("uc"), V("uo", 0, 8)], [V("upc")], 50 + 128 * GATHER * CY)
    add("s", lambda: g.scalar.activation(T.ups[:], T.usc[:].indirect(T.uo[:, 0:8]), ACT.Copy), [V("usc"), V("uo", 0, 8)], [V("ups")],
        65 + 128 * GATHER * CY)
    for h in range(2):
        quant("tc", "tsc", 128 * h, 128 * h + 128, V("xt", 512 * h, 512 * h + 512))
        mm(4 * h, "upc", "ups", 0, "tc", "tsc", 128 * h, 128 * h + 128)
        move("sv"[h], V("ptab", 128 * h, 128 * h + 128), bank(4 * h, 0, 128))
    copy(V("eau"), V("eai"))
    copy(V("ebu"), V("ebi"))
    for c in range(4):
        move(FIRST[c], V("pa", 128 * c, 128 * c + 128), (V("ptab"), V("eau", 8 * c, 8 * c + 8)))
    for c in range(4):
        tt(V("dd", 128 * c, 128 * c + 128), (V("ptab"), V("ebu", 8 * c, 8 * c + 8)), V("pa", 128 * c, 128 * c + 128), A.subtract)
    store_codes("y", 0, 256)
    store_scales("yyyy", 0, 256)

    ts(V("xx", 32, 64), V("ebi"), 2.0 ** -9, A.mult, 1.0, A.add)
    for s in range(2):
        tt(V("xx", 16 * s, 16 * s + 16), V("eai", s, 32, 2), V("xx", 32 + s, 64, 2), A.add)
        dma("y", lambda s=s: T.x0[0:128:16, 256 * s:256 * s + 256], lambda s=s: T.xx[:, 16 * s:16 * s + 16],
            [V("xx", 16 * s, 16 * s + 16)], [V("x0", 256 * s, 256 * s + 256)], "row%d" % s)
    for j in range(16):
        dma("y", lambda j=j: T.xr[j:128:16, :], lambda: T.x0[0:128:16, :], [V("x0")], [V("xr", j, 512, 16)], "rows")

    DB = [1, 2, 3, 5]
    for b in range(4):
        quant("ec", "esc", 128 * b, 128 * b + 128, V("et", 3 - b, 515 - b))
    quant("vc", "vsc", 0, 128, V("vt"))

    def unpack(n):
        for b in range(4):
            mm(DB[b], "ec", "esc", 128 * b, "tc", "tsc", n, n + 256)
        mm(6, "vc", "vsc", 0, "tc", "tsc", n, n + 256)

    unpack(0)

    def verdict(o, name, n, cnt, side):
        scan(last(o, n), last("dz", n), last(name, n), cnt, A.mult, A.add)
        turn(V("tr", 32 * side, 32 * side + 32), last(o, 32))

    def choose(k, row, n, init):
        scan(V("th", 64 * k, 64 * k + n), V("tr", 0, n), row, init, A.max, A.min)
        return col("th", 64 * k + n - 1)

    for t in range(1, R + 1):
        n = C + (t - 1) * K
        sd = V("sd", 32 * t - 32, 32 * t)
        li = "l%d" % t

        for e in range(2):
            part = (128 * e, 128 * e + 128) if t == 1 else (e, 256, 2)
            act(V("ss", *part), V("dd", *part), ACT.Abs)
        count(col("cnt", 8), V("ss", 0, 256), PA)
        copy(col("v1", 1), col("cnt", 8))
        ts(V("vb", 2, 258), V("ss", 0, 256), PB, A.is_lt, 2.0, A.mult)
        count(col("cnt", 1), V("dd", 256, 512), PB, 1)
        count(col("cnt", 0), V("dd", 256, 512), PA)
        ts(V("vb", 258, 514), V("dd", 256, 512), NB, A.is_gt, 2.0, A.mult)
        ts(V("v1", 2, 258), V("dd", 256, 512), NA, A.is_gt, 2.0, A.mult)
        act(V("ss", 256, 512), V("dd", 256, 512), ACT.Abs)
        dma("y", lambda t=t: T.sd[:, 32 * t - 32:32 * t], lambda: T.ss[0:128:16, :], [V("ss")], [sd], "sd%d" % t)
        verdict("ob", "vb", 513 + TAIL, col("cnt", 1), 1)
        verdict("oa", "v1", 257 + TAIL, col("cnt", 0), 0)
        pa = choose(0, V("t1", 0, 64), 64, 0.0)
        pb = choose(1, V("t1", 64, 128), 64, 0.0)
        low = choose(2, V("rows"), 64, 0.0)
        count(col("cnt", 2), V("ss", 0, 512 - NV2), pa)
        count(col("cnt", 3), V("ss", 0, 512 - NV2), pb, 1)
        ts(V("va", 2, 2 + NV2), V("ss", 512 - NV2, 512), pa, A.is_lt, 2.0, A.mult)
        ts(V("vb", 514 - NV2, 514), V("ss", 512 - NV2, 512), pb, A.is_lt, 2.0, A.mult)
        ts(V("row", 0, 65), V("g65"), low, A.mult)
        ts(V("row", 65, 130), V("e65"), low, A.mult)
        verdict("oa", "va", 1 + NV2 + TAIL, col("cnt", 2), 0)
        verdict("ob", "vb", NV2 + TAIL, col("cnt", 3), 1)
        thr = choose(3, V("row", 0, 64), 64, col("row", 64))
        LO2 = choose(4, V("row", 65, 129), 64, col("row", 129))
        ts(col("sm", 5), LO2, -1.0, A.mult)
        lin(V("sp", 0, 256), V("ss", 0, 256), 1.0, col("sm", 5))
        lin(V("sp", 256, 512), V("ss", 256, 512), 1.0, col("sm", 5))
        act(V("gl"), V("gg", 132, 165), ACT.Copy, LO2)
        for k in range(3, 8):
            src = "sp" if k > 5 else "ss"
            row = V("row", 65 * k, 65 * k + 33)
            count(col("cnt", k + 1), V(src, 0, 512 - NV), thr)
            ts(V("va", 2 + NV2 - NV, 2 + NV2), V(src, 512 - NV, 512), thr, A.is_lt, 2.0, A.mult)
            if k == 7:
                ts(row, V("gl"), thr, A.add, LO2, A.add)
            else:
                if k == 5:
                    ts(col("sm", 4), thr, LO2, A.subtract)
                ts(row, V("gg", 33 * k - 99, 33 * k - 66), LO2, A.mult, col("sm", 4) if k == 5 else thr, A.add)
            verdict("oa", "va", NV + TAIL, col("cnt", k + 1), 0)
            thr = choose(k + 2, V("row", 65 * k, 65 * k + 32), 32, col("row", 65 * k + 32))
        TT = thr

        if t == 1:
            for b in range(4):
                act(V("z1", 256 * b, 256 * b + 256), bank(DB[b]))
        else:
            for e in range(2):
                for b in range(4):
                    if t == 2:
                        old = V("eb2" if e else "ea2", 512 * b + e, 512 * b + 512, 2)
                        if e:
                            act(old, (V("z1", 256 * b, 256 * b + 256), V("lb")))
                    else:
                        old = V("b3" if e else "a3", 256 * b, 256 * b + 256)
                        act(old, (V("eb2" if e else "ea2", 512 * b, 512 * b + 512), V("l2")))
                    for h in range(2):
                        st = old[3]
                        tt(V("mid", 512 * b + 256 * h + e, 512 * b + 256 * h + 256, 2),
                           V(old[0], old[1] + 128 * st * h, old[1] + 128 * st * h + 127 * st + 1, st), bank(DB[b], 128 * h, 128), A.add)
            if t == 2:
                for h in range(2):
                    act(V("pa2", 256 * h + 1, 256 * h + 256, 2), bank(4 * h, 0, 128))
                    act(V("pb2", 256 * h, 256 * h + 256, 2), bank(4 * h, 0, 128))
                for b in range(4):
                    act(V("ea2", 512 * b + 1, 512 * b + 512, 2), bank(DB[b]))
                    act(V("eb2", 512 * b, 512 * b + 512, 2), bank(DB[b]))
                act(V("ia2", 0, 512, 2), (V("ic"), V("la")))
                act(V("ib2", 1, 512, 2), (V("ic"), V("lb")))
            else:
                act(V("ia3", 0, 512, 2), (V("ia2"), V("l2")))
                act(V("ib3", 1, 512, 2), (V("ib2"), V("l2")))
        act(V("ysb", n - 256, n), bank(6))
        store_y("y", n - 256, n)

        if t == 1:
            ts(V("fgt", 0, 32), sd, TT, A.is_gt)
            ts(V("h0", 65, 160, 3), sd, TT, A.is_ge, -1.0, A.add)
            scan(V("h1", 65, 256, 3), V("mgt"), V("fgt"), 0.0, A.mult, A.add)
            scan(V("oge"), V("mge"), V("h0", 65, 256, 3), 32.0, A.mult, A.add)
            turn(V("h0", 0, 32), V("h1", 161, 256, 3))
            turn(V("h0", 32, 64), V("oge", 32, 64))
            scan(V("qq"), V("h0", 0, 160), V("h1", 0, 160), -256.0, A.add, A.min)
            scan(V("yy"), V("j0"), V("qq", 64, 160), 0.0, A.mult, A.add)
            ts(V("so"), V("yy", 2, 96, 3), col("qq", 31), A.subtract, -1.0, A.add)
            copy((V("r1"), V("so")), V("xr"))
            for h in range(2):
                a, b = 128 * h, 8 * h
                scan(V("ex1", a, a + 128), V("k1"), V("r1", a, a + 128), 0.0, A.mult, A.add)
                ts(V("wi", b, b + 8), V("ex1", a + 15, a + 128, 16), col("cs", 21), A.mult)
                ts(V("la", b, b + 8), V("ex1", a + 15, a + 128, 16), col("cs", 20), A.mult, -1.0, A.add)
                ts(V("wb", b, b + 8), V("wi", b, b + 8), 511, A.bitwise_and)
                copy(V("lb", b, b + 8), V("wb", b, b + 8))
        else:
            s0, s1 = V("sd", 32 * t - 32, 32 * t, 2), V("sd", 32 * t - 31, 32 * t, 2)
            act(V("pw", IN6 + 3, IN6 + 96, 6), s0)
            act(V("pw", IN6 + 5, IN6 + 96, 6), s1)
            tt(V("pw", IN6 + 1, IN6 + 96, 6), s0, s1, A.max)
            tt(V("pw", IN6 + 2, IN6 + 96, 6), s0, s1, A.max)
            ts(V("pw", FG6, FG6 + 96), V("pw", IN6, IN6 + 96), TT, A.is_gt, 1024.0, A.add)
            ts(V("pn", P0 + 64, P0 + 160), V("pw", IN6, IN6 + 96), TT, A.is_ge, -1.0, A.add)
            scan(V("pn", P1 + 64, P1 + 192), V("pw", MG, MG + 128), V("pw", FG6, FG6 + 128), 0.0, A.mult, A.add)
            scan(V("pn", OE, OE + 128), V("pn", ME, ME + 128), V("pn", P0 + 64, P0 + 192), 0.0, A.mult, A.add)
            turn(V("pn", P0, P0 + 32), V("pn", P1 + 160, P1 + 192))
            turn(V("pn", P0 + 32, P0 + 64), V("pn", OE + 96, OE + 128))
            scan(V("pn", Q6, Q6 + 160), V("pn", P0, P0 + 160), V("pn", P1, P1 + 160), -256.0, A.subtract, A.min)
            scan(V("pw", Y6, Y6 + 96), V("pw", J6, J6 + 96), V("pn", Q6 + 64, Q6 + 160), 0.0, A.mult, A.add)
            ts(V("so", 0, 16), V("pw", Y6 + 4, Y6 + 96, 6), col("pn", Q6 + 31), A.subtract, 2.0, A.mult)
            rw = "r%d" % t
            copy((V(rw), V("so", 0, 16)), V("phm"))
            for h in range(2):
                a = 258 * h
                scan(V("fx", 256 * h, a + 256), V("k3", 0, 256 + 2 * h), V(rw, 254 * h, 256 * h + 256), -1000.0, A.add, A.max)
                scan(V("ex2", 128 * h, 128 * h + 128), V("k2"), V("fx", a + 1, a + 256, 2), 0.0, A.add, A.min)
                ts(V(li, 8 * h, 8 * h + 8), V("ex2", 128 * h + 15, 128 * h + 128, 16), 256.0, A.add)

        for h in range(2):
            for b in range(4):
                o = V("mt", 512 * h + b, 512 * h + 512, 4)
                if t == 1:
                    w = V("z1", 256 * b, 256 * b + 256)
                    a = V("ea2", 512 * b + 256 * h, 512 * b + 256 * h + 256, 2)
                    act(a, (w, V("la", 8 * h, 8 * h + 8)))
                    tt(o, (w, V("lb", 8 * h, 8 * h + 8)), a, A.add)
                else:
                    move(PICK[h][b], o, (V("mid", 512 * b, 512 * b + 512), V(li, 8 * h, 8 * h + 8)))
            quant("mc", "msc", 128 * h, 128 * h + 128, V("mt", 512 * h, 512 * h + 512))
        ends = {}
        for h in range(2):
            for e in range(2):
                if t == 1:
                    w, a = V("ptab"), V("lb" if e else "la", 8 * h, 8 * h + 8)
                    o = V("pb2" if e else "pa2", 256 * h + e, 256 * h + 256, 2)
                elif t == 2:
                    w, a = V("pb2" if e else "pa2"), V(li, 8 * h, 8 * h + 8)
                    o = V("pb3" if e else "pa3", 128 * h, 128 * h + 128)
                else:
                    w, a = V("ib3" if e else "ia3"), V(li, 8 * h, 8 * h + 8)
                    o = V("elb", 513 * e + 256 * h, 512 * e + 256 * h + 256, 2)
                move(ENDS[t - 1][2 * h + e], o, (w, a))
                ends[h, e] = o
        for h in range(2):
            for b in range(4):
                src = T.cores[(rank + t) % N]
                extra = (("arr%d" % t, 2 * len(topo.engines(src, core))),)
                mm(4 * h + b, "wl%d" % t, "wls%d" % t, 128 * b, "mc", "msc", 128 * h, 128 * h + 128, extra)
            for b in range(4):
                out = V("ft", 512 * h + b, 512 * h + 512, 4)
                if SCALE[t - 1][h][b] == "s":
                    act(out, bank(4 * h + b, 0, 128), ACT.Copy, 0.03125)
                else:
                    ts(out, bank(4 * h + b, 0, 128), 0.03125, A.mult)
            a = n + 128 * h
            quant("tc", "tsc", a, a + 128, V("ft", 512 * h, 512 * h + 512))
            mm(4 * h, "upc" if t < R else "vc", "ups" if t < R else "vsc", 0, "tc", "tsc", a, a + 128)
            if t < R:
                for e in range(2):
                    tt(V("dd", 256 * h + e, 256 * h + 256, 2), ends[h, e], bank(4 * h, 0, 128), A.subtract)
            else:
                copy(V("ysb", a, a + 128), bank(4 * h, 0, 128))
                store_y("y", a, a + 128)
                store_codes("y", a, a + 128)
        if t < R:
            unpack(n)
            store_codes("y", n, n + 256)
            store_scales("yyyy", n, n + 256)
        else:
            store_scales("yyss", n, n + 256)
            store("s", lambda: T.el[:, :], lambda: T.elb[0:128:16, :], [V("elb")])

    outs = emit(T, queue, ops)
    g.wait_ge(T.sem.sent, sent)
    g.sync.wait_ge(T.sem.outy, outs["outy"])
    g.scalar.wait_ge(T.sem.outs, outs["outs"])


FIRST = "sssv"
PICK = ["vvss", "vvss"]
ENDS = ["svsv", "svsv", "ssss"]
SCALE = [["ssss", "ssvv"], ["ssvv", "ssvv"], ["ssvv", "ssvv"]]
ORDER = (
    "1v0308001u01020t04091r0a0f0e0b0u1s0c0h1d0d230i2r0g0k0v191o2s0l1p0y2t1t1w0m0j0w2x1q0n0x1x300q1y0o0r310p111610320s2033400506430734384142460z3h4a1z4944134j47174k184l1c4m454n48144o21224b4e124c3i4f4d4g5j4i5k4h4p5l5n4q5q5o5r3j5p5m5u1a3k155w5s1e5v5x3l1g1i5y4r605z3m63614s5t64623n671h661j691f1b3o686a65256c3p6b242a6d6i6h3q1k6j6k4t4u2b4v2f4w3r4x4y6l1m4z265051526m532c542j55563s576o6n586p276e286q1n2d296r2h3t2e6s2g2l2n6u6t6v2k1l2i6f6x3u2m6w6g6y593v6z5a7270715b3w735c3x74393a5h753b5e78763y775g3c5f797e3z3d2o7a5d7b2p5i7i7j7k7g7l7m7n3f7h7o3g2u7p3e7q2q367r2z7d377c2w2v2y7f357s7x7t7u7y7v7z82807w848186838885878b898d8c8f8a8h8e8o8g8p8i8q8s8r8t8j8u8l8v928k918w909693958x94978m8y988z9m8n999h9i9n9j9f9k9l9a9d9b9o9q9c9t9r9e9u9g9s9p9x9v9zbt9y9wa0bja1a2a3a6a4a7a5a8aabzc0acbwa9abadbkaeblafalakagamajahanbmaiaobuapbvasaqarbxbnatbyc1aubfavbgaxawbhbqayb0azcfcgb1cib2bib4b3b5c7b6c8bsb7brb8chbab9bbc5bccabobdcbbpbec3cjckccclcmc9cncocdcpc4cqcec6crc2csctcwcucxcvcyczd2d0d1d7d3d6d5dbddd4dfdedhdgd8djdidkd9dpdqdrdldtdsdadudmdvgadwdndxdoebdcdye6e7ece8e5e9eadze3e0edefe1eiege2eje4eheeemekeogdenelepgbeqesereveteweuezguexf1gmeyf0gvf2gcf3f4gefaf9f5fbf7fcgff6fdgnfegofgfffhgpfigzfjgyfkgrfmflfng4fpfofqgqfrg5ftfsfug7fvg6f8fwfxg8fzfyg0gxgwg1gsg9g2gjg3ggh0h1h2gth3h4h5h6gkh7glh8gih9ghhahdhbhehchfhghjhhhihlhnhkhohmhrhwhuhphvi0hxhyi7hzi9i1i8ibiaidiciehti2hqifi3i6hsigijikimili4inioihi5ii"
)


def depends(ops):
    def bits(a):
        if a[0] == "ps":
            return 1 << (a[1] // 512)
        m = 0
        for c in range(a[1], a[2], a[3]):
            m |= 1 << c
        return m

    seen, deps = {}, []
    for i, op in enumerate(ops):
        d = set()
        touch = [(a[0], bits(a), False) for a in op[2]] + [(a[0], bits(a), True) for a in op[3]]
        for name, m, w in touch:
            for j, m2, w2 in seen.get(name, []):
                if m & m2 and (w or w2 or (name == "ps" and ops[j][0] != op[0])):
                    d.add(j)
        deps.append(d)
        for name, m, w in touch:
            seen.setdefault(name, []).append((i, m, w))
    return deps


def arrange(ops, deps):
    n = len(ops)
    after = [[] for _ in range(n)]
    for i in range(n):
        for j in deps[i]:
            after[j].append(i)
    tail = [0.0] * n
    for i in range(n - 1, -1, -1):
        tail[i] = ops[i][7] + max([WAKE + tail[k] for k in after[i]] + [0.0])
    best = None
    for turn in range(6):
        start, busy = [0.0] * n, {}
        for i in sorted(range(n), key=lambda i: (-tail[i], i)):
            t = max([start[j] + ops[j][7] + WAKE for j in deps[i]] + [0.0])
            line = busy.setdefault(ops[i][0], [])
            k = 0
            for k in range(len(line) + 1):
                if k == len(line) or t + ops[i][6] <= line[k][0] + 1e-6:
                    break
                t = max(t, line[k][1])
            line.insert(k, (t, t + ops[i][6]))
            start[i] = t
        end = max(start[i] + ops[i][7] for i in range(n))
        order = sorted(range(n), key=lambda i: (start[i], i))
        if best is None or end < best[0] - 1e-6:
            best = (end, order)
        late, busy = [0.0] * n, {}
        for i in sorted(range(n), key=lambda i: (-(start[i] + ops[i][7]), -i)):
            t = max([late[k] + WAKE for k in after[i]] + [0.0]) + ops[i][7] - ops[i][6]
            line = busy.setdefault(ops[i][0], [])
            k = 0
            for k in range(len(line) + 1):
                if k == len(line) or t + ops[i][6] <= line[k][0] + 1e-6:
                    break
                t = max(t, line[k][1])
            line.insert(k, (t, t + ops[i][6]))
            late[i] = t + ops[i][6]
        tail = late
    return best[1]


PLAN = []


def emit(T, queue, ops):
    deps = depends(ops)
    if not PLAN:
        given = [int(ORDER[i:i + 2], 36) for i in range(0, len(ORDER), 2)]
        PLAN.append(given if len(given) == len(ops) else arrange(ops, deps))
    order = PLAN[0]
    at = {i: p for p, i in enumerate(order)}
    total = {}
    for op in ops:
        if op[4] not in (None, "remote"):
            total[op[4]] = total.get(op[4], 0) + 16
    group = {}
    for i, op in enumerate(ops):
        if op[4] is not None:
            group[op[4]] = group.get(op[4], 0) | 1 << i
    known, done, waits, needed = {}, {}, {}, set()
    for i in order:
        q = ops[i][0]
        mine = []
        for j in sorted(deps[i], key=lambda j: -at[j]):
            if ops[j][4] == "remote":
                continue
            if not known.get(q, 0) >> j & 1:
                mine.append(j)
                needed.add(j)
                known[q] = known.get(q, 0) | done[j] | group.get(ops[j][4], 0)
        waits[i] = (mine[::-1], known.get(q, 0))
        done[i] = known.get(q, 0) | 1 << i
    token, last, used = {}, {}, {}
    for i in order:
        q, call, sem, extra = ops[i][0], ops[i][1], ops[i][4], ops[i][5]
        for name, val in extra:
            if name not in used:
                used[name] = True
                queue[q].wait_ge(T.sem[name], val)
        for j in waits[i][0]:
            queue[q].wait_ge(T.sem[token[j][0]], token[j][1])
        if sem is None and i in needed:
            k = used.get(q, 0)
            free = [c % POOL[q] for c in range(k, k + POOL[q])
                    if (q, c % POOL[q]) not in last or waits[i][1] >> last[q, c % POOL[q]] & 1]
            c = free[0] if free else k % POOL[q]
            j = last.get((q, c))
            if not free:
                queue[q].wait_ge(T.sem[token[j][0]], token[j][1])
            token[i] = (q + str(c), 1 if j is None else token[j][1] + 1)
            last[q, c] = i
            used[q] = c + 1
        ins = call()
        if sem == "remote":
            continue
        if sem is not None:
            ins.then_inc(T.sem[sem], 16)
            token[i] = (sem, total[sem])
        elif i in needed:
            ins.then_inc(T.sem[token[i][0]], 1)
    return total
